import numpy as np
import ml_dtypes


def mxq(x, axis, fmt="e4m3"):
    dtype, down = {"e4m3": (ml_dtypes.float8_e4m3fn, 7), "e5m2": (ml_dtypes.float8_e5m2, 14)}[fmt]
    v = np.moveaxis(np.asarray(x, np.float32).astype(ml_dtypes.bfloat16).astype(np.float64), axis, -1)
    blocks = v.reshape(v.shape[:-1] + (-1, 32))
    amax = np.abs(blocks).max(-1, keepdims=True)
    byte = np.maximum(np.where(amax > 0, np.frexp(amax)[1] - 1 + 127, 0) - down, 1)
    scale = np.exp2(byte - 127.0)
    codes = (blocks / scale).astype(np.float32).astype(dtype).astype(np.float64)
    return np.moveaxis((codes * scale).reshape(v.shape), -1, axis)


WIDE = False


def mx_kscale(k):
    if not WIDE:
        return np.ones(k)
    levels = np.array([10, -10, 5, -5, 0])
    if k % 512:
        return np.exp2(np.random.permutation(np.resize(levels, k // 32))).repeat(32)
    a = np.empty((k // 512, 16))
    for p in range(k // 512):
        a[p, :8] = np.random.permutation(np.resize(levels, 8))
        for g in range(8):
            far = levels[np.abs(levels - a[p, g]) >= 10]
            a[p, g + 8] = far[np.random.randint(len(far))]
    return np.exp2(a.ravel()).repeat(32)


def f64(x):
    return np.asarray(x).astype(np.float64)


def striped(idx):
    return np.tile(idx.reshape(-1, 16).T, (8, 1)).astype(np.uint16)


def unstriped(offs):
    return offs[:16].T.reshape(-1).astype(np.int64)


E2M1 = np.array([0.0, 0.5, 1.0, 1.5, 2.0, 3.0, 4.0, 6.0, -0.0, -0.5, -1.0, -1.5, -2.0, -3.0, -4.0, -6.0])


def pack_weight(w, fmt):
    k, n = w.shape
    w = f64(np.asarray(w, np.float32).astype(ml_dtypes.bfloat16)).reshape(k // 32, 32, n)
    amax = np.abs(w).max(1)
    if fmt == "e4m3":
        byte = np.frexp(amax)[1] - 1 + 127 - 7
    else:
        mant, ex = np.frexp(amax / 6.0)
        byte = np.where(mant > 0.5, ex, ex - 1) + 127
    byte = np.clip(np.where(amax > 0, byte, 1), 1, 254)
    scaled = (w * np.exp2(127.0 - byte)[:, None, :]).reshape(k, n).astype(np.float32)
    by_word = np.ascontiguousarray(scaled.reshape(k // 512, 128, 4, n).transpose(0, 1, 3, 2))
    if fmt == "e4m3":
        words = by_word.astype(ml_dtypes.float8_e4m3fn).view(np.uint8)
    else:
        c = by_word.astype(ml_dtypes.float4_e2m1fn).view(np.uint8) & 0xF
        words = (c[..., 0::2] | (c[..., 1::2] << 4)).reshape(k // 512, 128, 2 * n)
    return np.ascontiguousarray(words), np.ascontiguousarray(byte.astype(np.uint8).reshape(k // 512, 16, n))


def unpack_weight(words, scales, fmt):
    g, _, n = scales.shape
    words = np.ascontiguousarray(words).reshape(g, 128, n, -1)
    if fmt == "e4m3":
        vals = words.view(ml_dtypes.float8_e4m3fn).astype(np.float64)
    else:
        nib = np.empty((g, 128, n, 4), np.uint8)
        nib[..., 0::2] = words & 0xF
        nib[..., 1::2] = words >> 4
        vals = E2M1[nib]
    vals = vals * np.repeat(np.exp2(scales.astype(np.float64) - 127.0), 8, axis=1)[..., None]
    return vals.transpose(0, 1, 3, 2).reshape(g * 512, n)


def gelu(v):
    return 0.5 * v * (1.0 + np.tanh(np.sqrt(2.0 / np.pi) * (v + 0.044715 * v**3)))


K, T, S, T2, S2, N = 1024, 2048, 1024, 4096, 1024, 512


def setup_inputs():
    n = np.random.standard_normal
    s = mx_kscale(K)[:, None]
    u = mx_kscale(S)[:, None]
    tab_words, tab_scales = pack_weight(n((K, T)) * s, "e4m3")
    tab2_words, tab2_scales = pack_weight(n((K, T2)) / np.sqrt(K) / s, "e4m3")
    wi_words, wi_scales = pack_weight(2.0 * n((S, N)) / np.sqrt(S) / u, "e2m1")
    return {
        "tab_words": tab_words, "tab_scales": tab_scales,
        "offs": striped(np.random.permutation(T)[:S]),
        "tab2_words": tab2_words, "tab2_scales": tab2_scales,
        "offs2": striped(np.random.permutation(T2)[:S2]),
        "res": (0.2 + 0.4 * n(S)).astype(np.float32),
        "wt": (np.exp(0.3 * n(S)) * u[:, 0]).astype(np.float32),
        "wi_words": wi_words, "wi_scales": wi_scales,
        "wo": (2.0 * n((S, N)) / np.sqrt(S) / u).astype(np.float32),
    }


def reference(tab_words, tab_scales, offs, tab2_words, tab2_scales, offs2, res, wt, wi_words, wi_scales, wo):
    v = unpack_weight(tab_words, tab_scales, "e4m3")[:, unstriped(offs)]
    v2 = unpack_weight(tab2_words, tab2_scales, "e4m3")[:, unstriped(offs2)]
    a = v.T @ v2
    z = np.maximum(a - f64(res)[:, None], 0.0) * f64(wt)[:, None]
    zq = mxq(z, 0, "e4m3")
    wi = unpack_weight(wi_words, wi_scales, "e2m1")
    interest = wi.T @ zq
    offer = mxq(f64(wo), 0, "e4m3").T @ zq
    return offer / (1.0 + np.exp(-interest))

@@ -1,0 +1,214 @@
+from contextlib import ExitStack
+
+import concourse.mybir as mybir
+
+K, T, S, T2, S2, N = 1024, 2048, 1024, 4096, 1024, 512
+FLOPS = 2 * K * S * S2 + 2 * 2 * S * N * S2
+
+F32 = mybir.dt.float32
+BF16 = mybir.dt.bfloat16
+I32 = mybir.dt.int32
+U32 = mybir.dt.uint32
+U16 = mybir.dt.uint16
+U8 = mybir.dt.uint8
+FP8X4 = mybir.dt.float8_e4m3fn_x4
+FP4X4 = mybir.dt.float4_e2m1fn_x4
+ACT = mybir.ActivationFunctionType
+MULT = mybir.AluOpType.mult
+
+P = 128
+PACK = 4
+PASS = P * PACK
+QUADS = 4
+BANK = 512
+RUN = 4
+LIST_ROWS = 16
+
+
+def tile_list_two_sided_match_kernel(
+    tc, tab_words, tab_scales, offs, tab2_words, tab2_scales, offs2, res, wt, wi_words, wi_scales, wo, out
+):
+    nc = tc.nc
+    k_passes = K // PASS
+    i_passes = S // PASS
+    j_chunks = S2 // BANK
+    n_tiles = N // P
+    cols = PASS // LIST_ROWS
+
+    with ExitStack() as ctx:
+        keep = ctx.enter_context(tc.tile_pool(name="keep", bufs=1))
+        stage = ctx.enter_context(tc.tile_pool(name="stage", bufs=3))
+        reuse = ctx.enter_context(tc.tile_pool(name="reuse", bufs=1))
+        ring = ctx.enter_context(tc.tile_pool(name="ring", bufs=3))
+        psum = ctx.enter_context(tc.psum_pool(name="psum", bufs=8))
+
+        idx = keep.tile([P, S // LIST_ROWS], U16, name="idx")
+        idx2 = keep.tile([P, S2 // LIST_ROWS], U16, name="idx2")
+        v_tab_s = keep.tile([P, T // 4], I32, name="v_tab_s", tag="then_wi", align_bytes=64)
+        v2_tab_s = reuse.tile([P, T2 // 4], I32, name="v2_tab_s", align_bytes=64, offset=1024)
+        wi_s = keep.tile([P, i_passes, N // 4], I32, name="wi_s", align_bytes=64)
+        neg_res = keep.tile([P, i_passes, PACK], F32, name="neg_res")
+        wt_t = keep.tile([P, i_passes, PACK], F32, name="wt_t")
+        warm = keep.tile([P, 8], F32, name="warm")
+
+        def staged(shape, dtype, name):
+            return stage.tile(shape, dtype, name=name, tag="staged", align_bytes=64)
+
+        def words(table, a):
+            return table[a].rearrange("p t i -> p (t i)").bitcast(I32)
+
+        nc.vector.memset(v2_tab_s[:], 0)
+        nc.vector.memset(v_tab_s[:], 0)
+        nc.vector.memset(wi_s[:], 0)
+        nc.vector.memset(warm[:], 0.0)
+
+        v_tab = [staged([P, T], I32, f"v_tab{a}") for a in range(k_passes)]
+        res_t = staged([P, i_passes, PACK], F32, "res_t")
+        nc.sync.dma_start(out=v_tab[0][:], in_=words(tab_words, 0))
+        nc.sync.dma_start(out=idx[:], in_=offs)
+        nc.sync.dma_start(out=res_t[:], in_=res.rearrange("(b p t) -> p b t", p=P, t=PACK))
+        nc.sync.dma_start(out=v_tab[1][:], in_=words(tab_words, 1))
+        nc.sync.dma_start(out=idx2[:], in_=offs2)
+        nc.sync.dma_start(out=wt_t[:], in_=wt.rearrange("(b p t) -> p b t", p=P, t=PACK))
+
+        v_row, v2_row = 0, 8
+        for q in range(QUADS):
+            nc.scalar.dma_start(
+                out=v_tab_s[32 * q + v_row : 32 * q + v_row + 8, :],
+                in_=tab_scales.bitcast(I32)[:, 4 * q : 4 * q + 4, :],
+            )
+        for q in range(QUADS):
+            nc.gpsimd.dma_start(
+                out=v2_tab_s[32 * q + v2_row : 32 * q + v2_row + 8, :],
+                in_=tab2_scales.bitcast(I32)[:, 4 * q : 4 * q + 4, :],
+            )
+        for q in range(QUADS):
+            nc.scalar.dma_start(
+                out=wi_s[32 * q : 32 * q + 4, :, :],
+                in_=wi_scales.bitcast(I32)[:, 4 * q : 4 * q + 4, :].rearrange("b r w -> r b w"),
+            )
+        nc.scalar.activation(warm[:, 0:1], warm[:, 1:2], ACT.Sigmoid)
+        nc.vector.tensor_scalar_mul(neg_res[:], res_t[:], -1.0)
+
+        v2_tab = []
+        for a in range(k_passes):
+            v2_tab.append(staged([P, T2], I32, f"v2_tab{a}"))
+            nc.sync.dma_start(out=v2_tab[a][:], in_=words(tab2_words, a))
+        wo_raw = []
+        for b in range(i_passes):
+            wo_raw.append(staged([P, PACK, N], F32, f"wo_raw{b}"))
+            nc.sync.dma_start(
+                out=wo_raw[b][:], in_=wo[b * PASS : (b + 1) * PASS, :].rearrange("(p t) n -> p t n", t=PACK)
+            )
+        wi_c = keep.tile([P, i_passes, N // 2], I32, name="wi_c", tag="then_wi", align_bytes=64)
+        nc.sync.dma_start(out=wi_c[:], in_=wi_words.bitcast(I32).rearrange("b p w -> p b w"))
+
+        v_c = [[keep.tile([P, PACK, P], U32, name=f"v_c{a}_{b}", align_bytes=64) for b in range(i_passes)] for a in range(k_passes)]
+        v_s_listed = keep.tile([P, S], U8, name="v_s_listed", align_bytes=64)
+        v_s = keep.tile([P, i_passes, PACK, P], U8, name="v_s", align_bytes=64)
+        v2_c = {(0, 0): keep.tile([P, BANK], U32, name="v2_c0_0", align_bytes=64)}
+        for place, (a, h) in enumerate([(1, 0), (0, 1), (1, 1)]):
+            v2_c[a, h] = reuse.tile([P, BANK], U32, name=f"v2_c{a}_{h}", align_bytes=64, offset=2048 * place)
+        v2_s = keep.tile([P, S2], U8, name="v2_s", align_bytes=64)
+
+        def gather_v_words(a):
+            for b in range(i_passes):
+                nc.vector.tensor_copy(
+                    v_c[a][b][:].rearrange("p t m -> p m t"),
+                    v_tab[a][:].bitcast(U32).indirect(idx[:, b * cols : (b + 1) * cols]),
+                )
+
+        def gather_v2_words(a, h):
+            nc.vector.tensor_copy(
+                v2_c[a, h][:], v2_tab[a][:].bitcast(U32).indirect(idx2[:, h * cols : (h + 1) * cols])
+            )
+
+        gather_v_words(0)
+        nc.vector.tensor_copy(v_s_listed[:], v_tab_s[:].bitcast(U8).indirect(idx[:]))
+        gather_v_words(1)
+        nc.vector.tensor_copy(
+            v_s[:], v_s_listed[:].rearrange("p (b m t) -> p b t m", b=i_passes, t=PACK)
+        )
+
+        z_c = [[keep.tile([P, BANK], U32, name=f"z_c{h}_{b}", align_bytes=64) for b in range(i_passes)] for h in range(j_chunks)]
+        z_s = [[keep.tile([P, BANK], U8, name=f"z_s{h}_{b}", align_bytes=64) for b in range(i_passes)] for h in range(j_chunks)]
+        half = N // 2
+        wo_c = [[keep.tile([P, half], U32, name=f"wo_c{u}_{b}", align_bytes=64) for b in range(i_passes)] for u in range(2)]
+        wo_s = [[keep.tile([P, half], U8, name=f"wo_s{u}_{b}", align_bytes=64) for b in range(i_passes)] for u in range(2)]
+
+        def surplus(h, b):
+            above = ring.tile([P, PACK, BANK], F32, name="above", align_bytes=64)
+            for t in range(PACK):
+                fit = psum.tile([P, BANK], F32, name="bank")
+                for a in range(k_passes):
+                    nc.tensor.matmul_mx(
+                        out=fit[:],
+                        lhsT=v_c[a][b][:, t, :].bitcast(FP8X4),
+                        lhsT_scale=v_s[v_row + 4 * a : P, b, t, :],
+                        rhs=v2_c[a, h][:].bitcast(FP8X4),
+                        rhs_scale=v2_s[v2_row + 4 * a : P, BANK * h : BANK * (h + 1)],
+                        start=(a == 0),
+                        stop=(a == k_passes - 1),
+                    )
+                nc.scalar.activation(above[:, t, :], fit[:], ACT.Relu, bias=neg_res[:, b, t : t + 1])
+            z_bf = ring.tile([P, BANK * PACK], BF16, name="z_bf", align_bytes=64)
+            nc.vector.tensor_tensor(
+                z_bf[:].rearrange("p (c r t) -> p c t r", r=RUN, t=PACK),
+                above[:].rearrange("p t (c r) -> p c t r", r=RUN),
+                wt_t[:, b, :].unsqueeze(1).unsqueeze(3).to_broadcast([P, BANK // RUN, PACK, RUN]),
+                MULT,
+            )
+            nc.vector.quantize_mx(out=z_c[h][b][:].bitcast(FP8X4), scales=z_s[h][b][:], in_=z_bf[:])
+
+        def quantise_wo(u):
+            for b in range(i_passes):
+                wo_bf = keep.tile([P, half * PACK], BF16, name=f"wo_bf{u}_{b}", align_bytes=64)
+                nc.scalar.copy(
+                    wo_bf[:].rearrange("p (c r t) -> p c t r", r=RUN, t=PACK),
+                    wo_raw[b][:, :, u * half : (u + 1) * half].rearrange("p t (c r) -> p c t r", r=RUN),
+                )
+                nc.vector.quantize_mx(out=wo_c[u][b][:].bitcast(FP8X4), scales=wo_s[u][b][:], in_=wo_bf[:])
+
+        def scores(h, n):
+            interest = psum.tile([P, BANK], F32, name="bank")
+            for b in range(i_passes):
+                nc.tensor.matmul_mx(
+                    out=interest[:],
+                    lhsT=wi_c[:, b, :].bitcast(U8)[:, 2 * P * n : 2 * P * (n + 1)].bitcast(FP4X4),
+                    lhsT_scale=wi_s[:, b, :].bitcast(U8)[:, P * n : P * (n + 1)],
+                    rhs=z_c[h][b][:].bitcast(FP8X4),
+                    rhs_scale=z_s[h][b][:],
+                    start=(b == 0),
+                    stop=(b == i_passes - 1),
+                )
+            offer = psum.tile([P, BANK], F32, name="bank")
+            for b in range(i_passes):
+                nc.tensor.matmul_mx(
+                    out=offer[:],
+                    lhsT=wo_c[n // 2][b][:, P * (n % 2) : P * (n % 2 + 1)].bitcast(FP8X4),
+                    lhsT_scale=wo_s[n // 2][b][:, P * (n % 2) : P * (n % 2 + 1)],
+                    rhs=z_c[h][b][:].bitcast(FP8X4),
+                    rhs_scale=z_s[h][b][:],
+                    start=(b == 0),
+                    stop=(b == i_passes - 1),
+                )
+            chance = ring.tile([P, BANK], F32, name="chance")
+            nc.scalar.activation(chance[:], interest[:], ACT.Sigmoid)
+            result = keep.tile([P, BANK], F32, name=f"result{h}_{n}")
+            nc.vector.tensor_tensor(result[:], offer[:], chance[:], MULT)
+            nc.sync.dma_start(out=out[P * n : P * (n + 1), BANK * h : BANK * (h + 1)], in_=result[:])
+
+        gather_v2_words(0, 0)
+        nc.vector.tensor_copy(v2_s[:], v2_tab_s[:].bitcast(U8).indirect(idx2[:]))
+        gather_v2_words(1, 0)
+        surplus(0, 0)
+        gather_v2_words(0, 1)
+        gather_v2_words(1, 1)
+        surplus(0, 1)
+        surplus(1, 0)
+        quantise_wo(0)
+        surplus(1, 1)
+        quantise_wo(1)
+        for h in range(j_chunks):
+            for n in range(n_tiles):
+                scores(h, n)

@@ -33,47 +33,55 @@ def tile_list_two_sided_match_kernel(
     i_passes = S // PASS
     j_chunks = S2 // BANK
     n_tiles = N // P
-    cols = PASS // LIST_ROWS
+    cols = BANK // LIST_ROWS
+    half = N // 2
 
     with ExitStack() as ctx:
         keep = ctx.enter_context(tc.tile_pool(name="keep", bufs=1))
-        stage = ctx.enter_context(tc.tile_pool(name="stage", bufs=3))
         reuse = ctx.enter_context(tc.tile_pool(name="reuse", bufs=1))
         ring = ctx.enter_context(tc.tile_pool(name="ring", bufs=3))
         psum = ctx.enter_context(tc.psum_pool(name="psum", bufs=8))
 
         idx = keep.tile([P, S // LIST_ROWS], U16, name="idx")
         idx2 = keep.tile([P, S2 // LIST_ROWS], U16, name="idx2")
-        v_tab_s = keep.tile([P, T // 4], I32, name="v_tab_s", tag="then_wi", align_bytes=64)
+        v_tab_s = keep.tile([P, T // 4], I32, name="v_tab_s", tag="v_scales", align_bytes=64)
         v2_tab_s = reuse.tile([P, T2 // 4], I32, name="v2_tab_s", align_bytes=64, offset=1024)
         wi_s = keep.tile([P, i_passes, N // 4], I32, name="wi_s", align_bytes=64)
+        res_t = keep.tile([P, i_passes, PACK], F32, name="res_t")
         neg_res = keep.tile([P, i_passes, PACK], F32, name="neg_res")
         wt_t = keep.tile([P, i_passes, PACK], F32, name="wt_t")
         warm = keep.tile([P, 8], F32, name="warm")
 
-        def staged(shape, dtype, name):
-            return stage.tile(shape, dtype, name=name, tag="staged", align_bytes=64)
-
         def words(table, a):
             return table[a].rearrange("p t i -> p (t i)").bitcast(I32)
 
-        nc.vector.memset(v2_tab_s[:], 0)
         nc.vector.memset(v_tab_s[:], 0)
+        nc.vector.memset(v2_tab_s[:], 0)
         nc.vector.memset(wi_s[:], 0)
         nc.vector.memset(warm[:], 0.0)
 
-        v_tab = [staged([P, T], I32, f"v_tab{a}") for a in range(k_passes)]
-        res_t = staged([P, i_passes, PACK], F32, "res_t")
+        v_tab = [keep.tile([P, T], I32, name=f"v_tab{a}", tag=tag, align_bytes=64) for a, tag in enumerate(["slot_b", "slot_c"])]
+        v2_tab = [keep.tile([P, T2], I32, name=f"v2_tab{a}", tag=tag, align_bytes=64) for a, tag in enumerate(["slot_a", "slot_b"])]
+        wo_raw = [keep.tile([P, PACK, N], F32, name=f"wo_raw{b}", tag=tag, align_bytes=64) for b, tag in enumerate(["slot_a", "slot_b"])]
+        wi_c = keep.tile([P, i_passes, N // 2], I32, name="wi_c", tag="slot_c", align_bytes=64)
+
         nc.sync.dma_start(out=v_tab[0][:], in_=words(tab_words, 0))
         nc.sync.dma_start(out=idx[:], in_=offs)
-        nc.sync.dma_start(out=res_t[:], in_=res.rearrange("(b p t) -> p b t", p=P, t=PACK))
         nc.sync.dma_start(out=v_tab[1][:], in_=words(tab_words, 1))
         nc.sync.dma_start(out=idx2[:], in_=offs2)
+        nc.sync.dma_start(out=v2_tab[0][:], in_=words(tab2_words, 0))
+        nc.sync.dma_start(out=res_t[:], in_=res.rearrange("(b p t) -> p b t", p=P, t=PACK))
         nc.sync.dma_start(out=wt_t[:], in_=wt.rearrange("(b p t) -> p b t", p=P, t=PACK))
+        nc.sync.dma_start(out=v2_tab[1][:], in_=words(tab2_words, 1))
+        nc.sync.dma_start(out=wi_c[:], in_=wi_words.bitcast(I32).rearrange("b p w -> p b w"))
+        for b in range(i_passes):
+            nc.sync.dma_start(
+                out=wo_raw[b][:], in_=wo[b * PASS : (b + 1) * PASS, :].rearrange("(p t) n -> p t n", t=PACK)
+            )
 
         v_row, v2_row = 0, 8
         for q in range(QUADS):
-            nc.scalar.dma_start(
+            nc.gpsimd.dma_start(
                 out=v_tab_s[32 * q + v_row : 32 * q + v_row + 8, :],
                 in_=tab_scales.bitcast(I32)[:, 4 * q : 4 * q + 4, :],
             )
@@ -82,102 +90,97 @@ def tile_list_two_sided_match_kernel(
                 out=v2_tab_s[32 * q + v2_row : 32 * q + v2_row + 8, :],
                 in_=tab2_scales.bitcast(I32)[:, 4 * q : 4 * q + 4, :],
             )
+        nc.scalar.activation(warm[:, 0:1], warm[:, 1:2], ACT.Sigmoid)
         for q in range(QUADS):
             nc.scalar.dma_start(
                 out=wi_s[32 * q : 32 * q + 4, :, :],
                 in_=wi_scales.bitcast(I32)[:, 4 * q : 4 * q + 4, :].rearrange("b r w -> r b w"),
             )
-        nc.scalar.activation(warm[:, 0:1], warm[:, 1:2], ACT.Sigmoid)
-        nc.vector.tensor_scalar_mul(neg_res[:], res_t[:], -1.0)
+        nc.scalar.mul(neg_res[:], res_t[:], -1.0)
 
-        v2_tab = []
-        for a in range(k_passes):
-            v2_tab.append(staged([P, T2], I32, f"v2_tab{a}"))
-            nc.sync.dma_start(out=v2_tab[a][:], in_=words(tab2_words, a))
-        wo_raw = []
-        for b in range(i_passes):
-            wo_raw.append(staged([P, PACK, N], F32, f"wo_raw{b}"))
-            nc.sync.dma_start(
-                out=wo_raw[b][:], in_=wo[b * PASS : (b + 1) * PASS, :].rearrange("(p t) n -> p t n", t=PACK)
-            )
-        wi_c = keep.tile([P, i_passes, N // 2], I32, name="wi_c", tag="then_wi", align_bytes=64)
-        nc.sync.dma_start(out=wi_c[:], in_=wi_words.bitcast(I32).rearrange("b p w -> p b w"))
-
-        v_c = [[keep.tile([P, PACK, P], U32, name=f"v_c{a}_{b}", align_bytes=64) for b in range(i_passes)] for a in range(k_passes)]
+        v_c = [keep.tile([P, i_passes, PACK, P], U32, name=f"v_c{a}", align_bytes=64) for a in range(k_passes)]
         v_s_listed = keep.tile([P, S], U8, name="v_s_listed", align_bytes=64)
         v_s = keep.tile([P, i_passes, PACK, P], U8, name="v_s", align_bytes=64)
-        v2_c = {(0, 0): keep.tile([P, BANK], U32, name="v2_c0_0", align_bytes=64)}
+        v2_c = {(0, 0): keep.tile([P, BANK], U32, name="v2_c0_0", tag="v_scales", align_bytes=64)}
         for place, (a, h) in enumerate([(1, 0), (0, 1), (1, 1)]):
             v2_c[a, h] = reuse.tile([P, BANK], U32, name=f"v2_c{a}_{h}", align_bytes=64, offset=2048 * place)
         v2_s = keep.tile([P, S2], U8, name="v2_s", align_bytes=64)
-
-        def gather_v_words(a):
-            for b in range(i_passes):
-                nc.vector.tensor_copy(
-                    v_c[a][b][:].rearrange("p t m -> p m t"),
-                    v_tab[a][:].bitcast(U32).indirect(idx[:, b * cols : (b + 1) * cols]),
-                )
 
         def gather_v2_words(a, h):
             nc.vector.tensor_copy(
                 v2_c[a, h][:], v2_tab[a][:].bitcast(U32).indirect(idx2[:, h * cols : (h + 1) * cols])
             )
 
-        gather_v_words(0)
-        nc.vector.tensor_copy(v_s_listed[:], v_tab_s[:].bitcast(U8).indirect(idx[:]))
-        gather_v_words(1)
-        nc.vector.tensor_copy(
-            v_s[:], v_s_listed[:].rearrange("p (b m t) -> p b t m", b=i_passes, t=PACK)
-        )
-
-        z_c = [[keep.tile([P, BANK], U32, name=f"z_c{h}_{b}", align_bytes=64) for b in range(i_passes)] for h in range(j_chunks)]
-        z_s = [[keep.tile([P, BANK], U8, name=f"z_s{h}_{b}", align_bytes=64) for b in range(i_passes)] for h in range(j_chunks)]
-        half = N // 2
-        wo_c = [[keep.tile([P, half], U32, name=f"wo_c{u}_{b}", align_bytes=64) for b in range(i_passes)] for u in range(2)]
-        wo_s = [[keep.tile([P, half], U8, name=f"wo_s{u}_{b}", align_bytes=64) for b in range(i_passes)] for u in range(2)]
-
-        def surplus(h, b):
-            above = ring.tile([P, PACK, BANK], F32, name="above", align_bytes=64)
-            for t in range(PACK):
-                fit = psum.tile([P, BANK], F32, name="bank")
-                for a in range(k_passes):
-                    nc.tensor.matmul_mx(
-                        out=fit[:],
-                        lhsT=v_c[a][b][:, t, :].bitcast(FP8X4),
-                        lhsT_scale=v_s[v_row + 4 * a : P, b, t, :],
-                        rhs=v2_c[a, h][:].bitcast(FP8X4),
-                        rhs_scale=v2_s[v2_row + 4 * a : P, BANK * h : BANK * (h + 1)],
-                        start=(a == 0),
-                        stop=(a == k_passes - 1),
-                    )
-                nc.scalar.activation(above[:, t, :], fit[:], ACT.Relu, bias=neg_res[:, b, t : t + 1])
-            z_bf = ring.tile([P, BANK * PACK], BF16, name="z_bf", align_bytes=64)
-            nc.vector.tensor_tensor(
-                z_bf[:].rearrange("p (c r t) -> p c t r", r=RUN, t=PACK),
-                above[:].rearrange("p t (c r) -> p c t r", r=RUN),
-                wt_t[:, b, :].unsqueeze(1).unsqueeze(3).to_broadcast([P, BANK // RUN, PACK, RUN]),
-                MULT,
+        for a in range(k_passes):
+            nc.vector.tensor_copy(
+                v_c[a][:].rearrange("p b t m -> p b m t"), v_tab[a][:].bitcast(U32).indirect(idx[:])
             )
-            nc.vector.quantize_mx(out=z_c[h][b][:].bitcast(FP8X4), scales=z_s[h][b][:], in_=z_bf[:])
+        nc.vector.tensor_copy(v_s_listed[:], v_tab_s[:].bitcast(U8).indirect(idx[:]))
+        gather_v2_words(0, 0)
+        nc.vector.tensor_copy(v_s[:], v_s_listed[:].rearrange("p (b m t) -> p b t m", b=i_passes, t=PACK))
+        nc.vector.tensor_copy(v2_s[:], v2_tab_s[:].bitcast(U8).indirect(idx2[:]))
+        gather_v2_words(1, 0)
+
+        z_c = {}
+        z_s = {}
+        z_bf = {}
+        wo_c = [keep.tile([P, i_passes, half], U32, name=f"wo_c{u}", align_bytes=64) for u in range(2)]
+        wo_s = [keep.tile([P, i_passes, half], U8, name=f"wo_s{u}", align_bytes=64) for u in range(2)]
+
+        def surplus(h, b, pieces=1):
+            width = BANK // pieces
+            z_bf[h, b] = ring.tile([P, BANK * PACK], BF16, name="z_bf", align_bytes=64)
+            for piece in range(pieces):
+                j0 = width * piece
+                above = ring.tile([P, PACK, width], F32, name="above", bufs=4, align_bytes=64)
+                for t in range(PACK):
+                    fit = psum.tile([P, width], F32, name="bank")
+                    for a in range(k_passes):
+                        nc.tensor.matmul_mx(
+                            out=fit[:],
+                            lhsT=v_c[a][:, b, t, :].bitcast(FP8X4),
+                            lhsT_scale=v_s[v_row + 4 * a : P, b, t, :],
+                            rhs=v2_c[a, h][:, j0 : j0 + width].bitcast(FP8X4),
+                            rhs_scale=v2_s[v2_row + 4 * a : P, BANK * h + j0 : BANK * h + j0 + width],
+                            start=(a == 0),
+                            stop=(a == k_passes - 1),
+                        )
+                    nc.scalar.activation(above[:, t, :], fit[:], ACT.Relu, bias=neg_res[:, b, t : t + 1])
+                nc.vector.tensor_tensor(
+                    z_bf[h, b][:, PACK * j0 : PACK * (j0 + width)].rearrange("p (c r t) -> p c t r", r=RUN, t=PACK),
+                    above[:].rearrange("p t (c r) -> p c t r", r=RUN),
+                    wt_t[:, b, :].unsqueeze(1).unsqueeze(3).to_broadcast([P, width // RUN, PACK, RUN]),
+                    MULT,
+                )
+
+        def quantise_z(h, b):
+            z_c[h, b] = keep.tile([P, BANK], U32, name=f"z_c{h}_{b}", align_bytes=64)
+            z_s[h, b] = keep.tile([P, BANK], U8, name=f"z_s{h}_{b}", align_bytes=64)
+            nc.vector.quantize_mx(out=z_c[h, b][:].bitcast(FP8X4), scales=z_s[h, b][:], in_=z_bf[h, b][:])
 
         def quantise_wo(u):
+            wo_bf = keep.tile([P, i_passes, half * PACK], BF16, name=f"wo_bf{u}", align_bytes=64)
             for b in range(i_passes):
-                wo_bf = keep.tile([P, half * PACK], BF16, name=f"wo_bf{u}_{b}", align_bytes=64)
                 nc.scalar.copy(
-                    wo_bf[:].rearrange("p (c r t) -> p c t r", r=RUN, t=PACK),
+                    wo_bf[:, b, :].rearrange("p (c r t) -> p c t r", r=RUN, t=PACK),
                     wo_raw[b][:, :, u * half : (u + 1) * half].rearrange("p t (c r) -> p c t r", r=RUN),
                 )
-                nc.vector.quantize_mx(out=wo_c[u][b][:].bitcast(FP8X4), scales=wo_s[u][b][:], in_=wo_bf[:])
+            nc.vector.quantize_mx(
+                out=wo_c[u][:].rearrange("p b n -> p (b n)").bitcast(FP8X4),
+                scales=wo_s[u][:].rearrange("p b n -> p (b n)"),
+                in_=wo_bf[:].rearrange("p b w -> p (b w)"),
+            )
 
         def scores(h, n):
+            u, n_cols = n // 2, slice(P * (n % 2), P * (n % 2 + 1))
             interest = psum.tile([P, BANK], F32, name="bank")
             for b in range(i_passes):
                 nc.tensor.matmul_mx(
                     out=interest[:],
                     lhsT=wi_c[:, b, :].bitcast(U8)[:, 2 * P * n : 2 * P * (n + 1)].bitcast(FP4X4),
                     lhsT_scale=wi_s[:, b, :].bitcast(U8)[:, P * n : P * (n + 1)],
-                    rhs=z_c[h][b][:].bitcast(FP8X4),
-                    rhs_scale=z_s[h][b][:],
+                    rhs=z_c[h, b][:].bitcast(FP8X4),
+                    rhs_scale=z_s[h, b][:],
                     start=(b == 0),
                     stop=(b == i_passes - 1),
                 )
@@ -185,30 +188,36 @@ def tile_list_two_sided_match_kernel(
             for b in range(i_passes):
                 nc.tensor.matmul_mx(
                     out=offer[:],
-                    lhsT=wo_c[n // 2][b][:, P * (n % 2) : P * (n % 2 + 1)].bitcast(FP8X4),
-                    lhsT_scale=wo_s[n // 2][b][:, P * (n % 2) : P * (n % 2 + 1)],
-                    rhs=z_c[h][b][:].bitcast(FP8X4),
-                    rhs_scale=z_s[h][b][:],
+                    lhsT=wo_c[u][:, b, n_cols].bitcast(FP8X4),
+                    lhsT_scale=wo_s[u][:, b, n_cols],
+                    rhs=z_c[h, b][:].bitcast(FP8X4),
+                    rhs_scale=z_s[h, b][:],
                     start=(b == 0),
                     stop=(b == i_passes - 1),
                 )
-            chance = ring.tile([P, BANK], F32, name="chance")
+            chance = ring.tile([P, BANK], F32, name="chance", bufs=4)
             nc.scalar.activation(chance[:], interest[:], ACT.Sigmoid)
             result = keep.tile([P, BANK], F32, name=f"result{h}_{n}")
             nc.vector.tensor_tensor(result[:], offer[:], chance[:], MULT)
             nc.sync.dma_start(out=out[P * n : P * (n + 1), BANK * h : BANK * (h + 1)], in_=result[:])
 
-        gather_v2_words(0, 0)
-        nc.vector.tensor_copy(v2_s[:], v2_tab_s[:].bitcast(U8).indirect(idx2[:]))
-        gather_v2_words(1, 0)
-        surplus(0, 0)
+        surplus(0, 0, pieces=2)
         gather_v2_words(0, 1)
         gather_v2_words(1, 1)
         surplus(0, 1)
+        quantise_z(0, 0)
         surplus(1, 0)
+        quantise_z(0, 1)
         quantise_wo(0)
         surplus(1, 1)
+        quantise_z(1, 0)
+        scores(0, 0)
+        quantise_z(1, 1)
+        scores(0, 1)
         quantise_wo(1)
-        for h in range(j_chunks):
-            for n in range(n_tiles):
-                scores(h, n)
+        scores(1, 0)
+        scores(1, 1)
+        scores(0, 2)
+        scores(0, 3)
+        scores(1, 2)
+        scores(1, 3)

@@ -39,25 +39,22 @@ def tile_list_two_sided_match_kernel(
     with ExitStack() as ctx:
         keep = ctx.enter_context(tc.tile_pool(name="keep", bufs=1))
         reuse = ctx.enter_context(tc.tile_pool(name="reuse", bufs=1))
+        reuse_v = ctx.enter_context(tc.tile_pool(name="reuse_v", bufs=1))
         ring = ctx.enter_context(tc.tile_pool(name="ring", bufs=3))
         psum = ctx.enter_context(tc.psum_pool(name="psum", bufs=8))
 
         idx = keep.tile([P, S // LIST_ROWS], U16, name="idx")
         idx2 = keep.tile([P, S2 // LIST_ROWS], U16, name="idx2")
-        v_tab_s = keep.tile([P, T // 4], I32, name="v_tab_s", tag="v_scales", align_bytes=64)
+        v_tab_s = reuse_v.tile([P, T // 4], I32, name="v_tab_s", align_bytes=64, offset=1024)
         v2_tab_s = reuse.tile([P, T2 // 4], I32, name="v2_tab_s", align_bytes=64, offset=1024)
-        wi_s = keep.tile([P, i_passes, N // 4], I32, name="wi_s", align_bytes=64)
-        res_t = keep.tile([P, i_passes, PACK], F32, name="res_t")
         neg_res = keep.tile([P, i_passes, PACK], F32, name="neg_res")
-        wt_t = keep.tile([P, i_passes, PACK], F32, name="wt_t")
         warm = keep.tile([P, 8], F32, name="warm")
 
         def words(table, a):
             return table[a].rearrange("p t i -> p (t i)").bitcast(I32)
 
-        nc.vector.memset(v_tab_s[:], 0)
         nc.vector.memset(v2_tab_s[:], 0)
-        nc.vector.memset(wi_s[:], 0)
+        nc.vector.memset(v_tab_s[:], 0)
         nc.vector.memset(warm[:], 0.0)
 
         v_tab = [keep.tile([P, T], I32, name=f"v_tab{a}", tag=tag, align_bytes=64) for a, tag in enumerate(["slot_b", "slot_c"])]
@@ -65,43 +62,33 @@ def tile_list_two_sided_match_kernel(
         wo_raw = [keep.tile([P, PACK, N], F32, name=f"wo_raw{b}", tag=tag, align_bytes=64) for b, tag in enumerate(["slot_a", "slot_b"])]
         wi_c = keep.tile([P, i_passes, N // 2], I32, name="wi_c", tag="slot_c", align_bytes=64)
 
-        nc.sync.dma_start(out=v_tab[0][:], in_=words(tab_words, 0))
         nc.sync.dma_start(out=idx[:], in_=offs)
-        nc.sync.dma_start(out=v_tab[1][:], in_=words(tab_words, 1))
         nc.sync.dma_start(out=idx2[:], in_=offs2)
+        nc.sync.dma_start(out=v_tab[0][:], in_=words(tab_words, 0))
+        nc.sync.dma_start(out=v_tab[1][:], in_=words(tab_words, 1))
         nc.sync.dma_start(out=v2_tab[0][:], in_=words(tab2_words, 0))
-        nc.sync.dma_start(out=res_t[:], in_=res.rearrange("(b p t) -> p b t", p=P, t=PACK))
-        nc.sync.dma_start(out=wt_t[:], in_=wt.rearrange("(b p t) -> p b t", p=P, t=PACK))
         nc.sync.dma_start(out=v2_tab[1][:], in_=words(tab2_words, 1))
-        nc.sync.dma_start(out=wi_c[:], in_=wi_words.bitcast(I32).rearrange("b p w -> p b w"))
-        for b in range(i_passes):
-            nc.sync.dma_start(
-                out=wo_raw[b][:], in_=wo[b * PASS : (b + 1) * PASS, :].rearrange("(p t) n -> p t n", t=PACK)
-            )
 
         v_row, v2_row = 0, 8
         for q in range(QUADS):
-            nc.gpsimd.dma_start(
+            nc.scalar.dma_start(
                 out=v_tab_s[32 * q + v_row : 32 * q + v_row + 8, :],
                 in_=tab_scales.bitcast(I32)[:, 4 * q : 4 * q + 4, :],
             )
-        for q in range(QUADS):
+        for q in range(3):
             nc.gpsimd.dma_start(
                 out=v2_tab_s[32 * q + v2_row : 32 * q + v2_row + 8, :],
                 in_=tab2_scales.bitcast(I32)[:, 4 * q : 4 * q + 4, :],
             )
+        for a in range(k_passes):
+            row = 32 * 3 + v2_row + 4 * a
+            nc.scalar.dma_start(out=v2_tab_s[row : row + 4, :], in_=tab2_scales.bitcast(I32)[a, 12:16, :])
         nc.scalar.activation(warm[:, 0:1], warm[:, 1:2], ACT.Sigmoid)
-        for q in range(QUADS):
-            nc.scalar.dma_start(
-                out=wi_s[32 * q : 32 * q + 4, :, :],
-                in_=wi_scales.bitcast(I32)[:, 4 * q : 4 * q + 4, :].rearrange("b r w -> r b w"),
-            )
-        nc.scalar.mul(neg_res[:], res_t[:], -1.0)
 
         v_c = [keep.tile([P, i_passes, PACK, P], U32, name=f"v_c{a}", align_bytes=64) for a in range(k_passes)]
         v_s_listed = keep.tile([P, S], U8, name="v_s_listed", align_bytes=64)
         v_s = keep.tile([P, i_passes, PACK, P], U8, name="v_s", align_bytes=64)
-        v2_c = {(0, 0): keep.tile([P, BANK], U32, name="v2_c0_0", tag="v_scales", align_bytes=64)}
+        v2_c = {(0, 0): reuse_v.tile([P, BANK], U32, name="v2_c0_0", align_bytes=64, offset=0)}
         for place, (a, h) in enumerate([(1, 0), (0, 1), (1, 1)]):
             v2_c[a, h] = reuse.tile([P, BANK], U32, name=f"v2_c{a}_{h}", align_bytes=64, offset=2048 * place)
         v2_s = keep.tile([P, S2], U8, name="v2_s", align_bytes=64)
@@ -117,6 +104,23 @@ def tile_list_two_sided_match_kernel(
             )
         nc.vector.tensor_copy(v_s_listed[:], v_tab_s[:].bitcast(U8).indirect(idx[:]))
         gather_v2_words(0, 0)
+        res_t = reuse_v.tile([P, i_passes, PACK], F32, name="res_t", align_bytes=64, offset=2048)
+        wt_t = reuse_v.tile([P, i_passes, PACK], F32, name="wt_t", align_bytes=64, offset=2112)
+        wi_s = reuse_v.tile([P, i_passes, N // 4], I32, name="wi_s", align_bytes=64, offset=2176)
+        nc.sync.dma_start(out=res_t[:], in_=res.rearrange("(b p t) -> p b t", p=P, t=PACK))
+        nc.sync.dma_start(out=wt_t[:], in_=wt.rearrange("(b p t) -> p b t", p=P, t=PACK))
+        nc.scalar.mul(neg_res[:], res_t[:], -1.0)
+        nc.vector.memset(wi_s[:], 0)
+        for q in range(QUADS):
+            nc.scalar.dma_start(
+                out=wi_s[32 * q : 32 * q + 4, :, :],
+                in_=wi_scales.bitcast(I32)[:, 4 * q : 4 * q + 4, :].rearrange("b r w -> r b w"),
+            )
+        nc.sync.dma_start(out=wi_c[:], in_=wi_words.bitcast(I32).rearrange("b p w -> p b w"))
+        for b in range(i_passes):
+            nc.sync.dma_start(
+                out=wo_raw[b][:], in_=wo[b * PASS : (b + 1) * PASS, :].rearrange("(p t) n -> p t n", t=PACK)
+            )
         nc.vector.tensor_copy(v_s[:], v_s_listed[:].rearrange("p (b m t) -> p b t m", b=i_passes, t=PACK))
         nc.vector.tensor_copy(v2_s[:], v2_tab_s[:].bitcast(U8).indirect(idx2[:]))
         gather_v2_words(1, 0)
@@ -204,17 +208,17 @@ def tile_list_two_sided_match_kernel(
         surplus(0, 0, pieces=2)
         gather_v2_words(0, 1)
         gather_v2_words(1, 1)
-        surplus(0, 1)
         quantise_z(0, 0)
-        surplus(1, 0)
+        surplus(0, 1)
         quantise_z(0, 1)
-        quantise_wo(0)
-        surplus(1, 1)
+        surplus(1, 0)
         quantise_z(1, 0)
-        scores(0, 0)
+        surplus(1, 1)
         quantise_z(1, 1)
-        scores(0, 1)
+        quantise_wo(0)
+        scores(0, 0)
         quantise_wo(1)
+        scores(0, 1)
         scores(1, 0)
         scores(1, 1)
         scores(0, 2)

@@ -57,40 +57,42 @@ def tile_list_two_sided_match_kernel(
         nc.vector.memset(v_tab_s[:], 0)
         nc.vector.memset(warm[:], 0.0)
 
+        res_t = keep.tile([P, i_passes, PACK], F32, name="res_t", tag="slot_a", align_bytes=64)
         v_tab = [keep.tile([P, T], I32, name=f"v_tab{a}", tag=tag, align_bytes=64) for a, tag in enumerate(["slot_b", "slot_c"])]
         v2_tab = [keep.tile([P, T2], I32, name=f"v2_tab{a}", tag=tag, align_bytes=64) for a, tag in enumerate(["slot_a", "slot_b"])]
         wo_raw = [keep.tile([P, PACK, N], F32, name=f"wo_raw{b}", tag=tag, align_bytes=64) for b, tag in enumerate(["slot_a", "slot_b"])]
         wi_c = keep.tile([P, i_passes, N // 2], I32, name="wi_c", tag="slot_c", align_bytes=64)
 
         nc.sync.dma_start(out=idx[:], in_=offs)
+        nc.sync.dma_start(out=res_t[:], in_=res.rearrange("(b p t) -> p b t", p=P, t=PACK))
         nc.sync.dma_start(out=idx2[:], in_=offs2)
         nc.sync.dma_start(out=v_tab[0][:], in_=words(tab_words, 0))
         nc.sync.dma_start(out=v_tab[1][:], in_=words(tab_words, 1))
-        nc.sync.dma_start(out=v2_tab[0][:], in_=words(tab2_words, 0))
-        nc.sync.dma_start(out=v2_tab[1][:], in_=words(tab2_words, 1))
 
         v_row, v2_row = 0, 8
         for q in range(QUADS):
-            nc.scalar.dma_start(
-                out=v_tab_s[32 * q + v_row : 32 * q + v_row + 8, :],
-                in_=tab_scales.bitcast(I32)[:, 4 * q : 4 * q + 4, :],
-            )
-        for q in range(3):
-            nc.gpsimd.dma_start(
+            queue = nc.gpsimd if q < 2 else nc.sync
+            queue.dma_start(
                 out=v2_tab_s[32 * q + v2_row : 32 * q + v2_row + 8, :],
                 in_=tab2_scales.bitcast(I32)[:, 4 * q : 4 * q + 4, :],
             )
-        for a in range(k_passes):
-            row = 32 * 3 + v2_row + 4 * a
-            nc.scalar.dma_start(out=v2_tab_s[row : row + 4, :], in_=tab2_scales.bitcast(I32)[a, 12:16, :])
+        for q in range(QUADS):
+            nc.sync.dma_start(
+                out=v_tab_s[32 * q + v_row : 32 * q + v_row + 8, :],
+                in_=tab_scales.bitcast(I32)[:, 4 * q : 4 * q + 4, :],
+            )
         nc.scalar.activation(warm[:, 0:1], warm[:, 1:2], ACT.Sigmoid)
+        nc.vector.tensor_scalar_mul(neg_res[:], res_t[:], -1.0)
+        nc.sync.dma_start(out=v2_tab[0][:], in_=words(tab2_words, 0))
+        nc.sync.dma_start(out=v2_tab[1][:], in_=words(tab2_words, 1))
 
         v_c = [keep.tile([P, i_passes, PACK, P], U32, name=f"v_c{a}", align_bytes=64) for a in range(k_passes)]
         v_s_listed = keep.tile([P, S], U8, name="v_s_listed", align_bytes=64)
         v_s = keep.tile([P, i_passes, PACK, P], U8, name="v_s", align_bytes=64)
         v2_c = {(0, 0): reuse_v.tile([P, BANK], U32, name="v2_c0_0", align_bytes=64, offset=0)}
-        for place, (a, h) in enumerate([(1, 0), (0, 1), (1, 1)]):
-            v2_c[a, h] = reuse.tile([P, BANK], U32, name=f"v2_c{a}_{h}", align_bytes=64, offset=2048 * place)
+        v2_c[0, 1] = keep.tile([P, BANK], U32, name="v2_c0_1", align_bytes=64)
+        for h in range(j_chunks):
+            v2_c[1, h] = reuse.tile([P, BANK], U32, name=f"v2_c1_{h}", align_bytes=64, offset=2048 * h)
         v2_s = keep.tile([P, S2], U8, name="v2_s", align_bytes=64)
 
         def gather_v2_words(a, h):
@@ -103,16 +105,12 @@ def tile_list_two_sided_match_kernel(
                 v_c[a][:].rearrange("p b t m -> p b m t"), v_tab[a][:].bitcast(U32).indirect(idx[:])
             )
         nc.vector.tensor_copy(v_s_listed[:], v_tab_s[:].bitcast(U8).indirect(idx[:]))
-        gather_v2_words(0, 0)
-        res_t = reuse_v.tile([P, i_passes, PACK], F32, name="res_t", align_bytes=64, offset=2048)
         wt_t = reuse_v.tile([P, i_passes, PACK], F32, name="wt_t", align_bytes=64, offset=2112)
         wi_s = reuse_v.tile([P, i_passes, N // 4], I32, name="wi_s", align_bytes=64, offset=2176)
-        nc.sync.dma_start(out=res_t[:], in_=res.rearrange("(b p t) -> p b t", p=P, t=PACK))
         nc.sync.dma_start(out=wt_t[:], in_=wt.rearrange("(b p t) -> p b t", p=P, t=PACK))
-        nc.scalar.mul(neg_res[:], res_t[:], -1.0)
         nc.vector.memset(wi_s[:], 0)
         for q in range(QUADS):
-            nc.scalar.dma_start(
+            nc.sync.dma_start(
                 out=wi_s[32 * q : 32 * q + 4, :, :],
                 in_=wi_scales.bitcast(I32)[:, 4 * q : 4 * q + 4, :].rearrange("b r w -> r b w"),
             )
@@ -123,6 +121,7 @@ def tile_list_two_sided_match_kernel(
             )
         nc.vector.tensor_copy(v_s[:], v_s_listed[:].rearrange("p (b m t) -> p b t m", b=i_passes, t=PACK))
         nc.vector.tensor_copy(v2_s[:], v2_tab_s[:].bitcast(U8).indirect(idx2[:]))
+        gather_v2_words(0, 0)
         gather_v2_words(1, 0)
 
         z_c = {}
@@ -136,7 +135,7 @@ def tile_list_two_sided_match_kernel(
             z_bf[h, b] = ring.tile([P, BANK * PACK], BF16, name="z_bf", align_bytes=64)
             for piece in range(pieces):
                 j0 = width * piece
-                above = ring.tile([P, PACK, width], F32, name="above", bufs=4, align_bytes=64)
+                above = ring.tile([P, PACK, width], F32, name="above", bufs=5, align_bytes=64)
                 for t in range(PACK):
                     fit = psum.tile([P, width], F32, name="bank")
                     for a in range(k_passes):
@@ -163,7 +162,7 @@ def tile_list_two_sided_match_kernel(
             nc.vector.quantize_mx(out=z_c[h, b][:].bitcast(FP8X4), scales=z_s[h, b][:], in_=z_bf[h, b][:])
 
         def quantise_wo(u):
-            wo_bf = keep.tile([P, i_passes, half * PACK], BF16, name=f"wo_bf{u}", align_bytes=64)
+            wo_bf = ring.tile([P, i_passes, half * PACK], BF16, name="wo_bf", tag="above", bufs=5, align_bytes=64)
             for b in range(i_passes):
                 nc.scalar.copy(
                     wo_bf[:, b, :].rearrange("p (c r t) -> p c t r", r=RUN, t=PACK),
@@ -175,12 +174,13 @@ def tile_list_two_sided_match_kernel(
                 in_=wo_bf[:].rearrange("p b w -> p (b w)"),
             )
 
-        def scores(h, n):
-            u, n_cols = n // 2, slice(P * (n % 2), P * (n % 2 + 1))
-            interest = psum.tile([P, BANK], F32, name="bank")
+        chance = {}
+
+        def interest(h, n):
+            score = psum.tile([P, BANK], F32, name="bank")
             for b in range(i_passes):
                 nc.tensor.matmul_mx(
-                    out=interest[:],
+                    out=score[:],
                     lhsT=wi_c[:, b, :].bitcast(U8)[:, 2 * P * n : 2 * P * (n + 1)].bitcast(FP4X4),
                     lhsT_scale=wi_s[:, b, :].bitcast(U8)[:, P * n : P * (n + 1)],
                     rhs=z_c[h, b][:].bitcast(FP8X4),
@@ -188,10 +188,15 @@ def tile_list_two_sided_match_kernel(
                     start=(b == 0),
                     stop=(b == i_passes - 1),
                 )
-            offer = psum.tile([P, BANK], F32, name="bank")
+            chance[h, n] = keep.tile([P, BANK], F32, name=f"chance{h}_{n}")
+            nc.scalar.activation(chance[h, n][:], score[:], ACT.Sigmoid)
+
+        def offer(h, n):
+            u, n_cols = n // 2, slice(P * (n % 2), P * (n % 2 + 1))
+            score = psum.tile([P, BANK], F32, name="bank")
             for b in range(i_passes):
                 nc.tensor.matmul_mx(
-                    out=offer[:],
+                    out=score[:],
                     lhsT=wo_c[u][:, b, n_cols].bitcast(FP8X4),
                     lhsT_scale=wo_s[u][:, b, n_cols],
                     rhs=z_c[h, b][:].bitcast(FP8X4),
@@ -199,10 +204,8 @@ def tile_list_two_sided_match_kernel(
                     start=(b == 0),
                     stop=(b == i_passes - 1),
                 )
-            chance = ring.tile([P, BANK], F32, name="chance", bufs=4)
-            nc.scalar.activation(chance[:], interest[:], ACT.Sigmoid)
             result = keep.tile([P, BANK], F32, name=f"result{h}_{n}")
-            nc.vector.tensor_tensor(result[:], offer[:], chance[:], MULT)
+            nc.vector.tensor_tensor(result[:], score[:], chance[h, n][:], MULT)
             nc.sync.dma_start(out=out[P * n : P * (n + 1), BANK * h : BANK * (h + 1)], in_=result[:])
 
         surplus(0, 0, pieces=2)
@@ -213,15 +216,23 @@ def tile_list_two_sided_match_kernel(
         quantise_z(0, 1)
         surplus(1, 0)
         quantise_z(1, 0)
-        surplus(1, 1)
-        quantise_z(1, 1)
         quantise_wo(0)
-        scores(0, 0)
+        surplus(1, 1)
+        interest(0, 0)
+        interest(0, 1)
+        interest(0, 2)
+        interest(0, 3)
+        quantise_z(1, 1)
+        offer(0, 0)
+        offer(0, 1)
+        interest(1, 0)
+        interest(1, 1)
         quantise_wo(1)
-        scores(0, 1)
-        scores(1, 0)
-        scores(1, 1)
-        scores(0, 2)
-        scores(0, 3)
-        scores(1, 2)
-        scores(1, 3)
+        offer(1, 0)
+        offer(1, 1)
+        interest(1, 2)
+        interest(1, 3)
+        offer(0, 2)
+        offer(0, 3)
+        offer(1, 2)
+        offer(1, 3)

@@ -21,7 +21,7 @@ PACK = 4
 PASS = P * PACK
 QUADS = 4
 BANK = 512
-RUN = 4
+RUN = 2
 LIST_ROWS = 16
 
 
@@ -63,11 +63,11 @@ def tile_list_two_sided_match_kernel(
         wo_raw = [keep.tile([P, PACK, N], F32, name=f"wo_raw{b}", tag=tag, align_bytes=64) for b, tag in enumerate(["slot_a", "slot_b"])]
         wi_c = keep.tile([P, i_passes, N // 2], I32, name="wi_c", tag="slot_c", align_bytes=64)
 
+        nc.sync.dma_start(out=v_tab[0][:], in_=words(tab_words, 0))
         nc.sync.dma_start(out=idx[:], in_=offs)
         nc.sync.dma_start(out=res_t[:], in_=res.rearrange("(b p t) -> p b t", p=P, t=PACK))
-        nc.sync.dma_start(out=idx2[:], in_=offs2)
-        nc.sync.dma_start(out=v_tab[0][:], in_=words(tab_words, 0))
         nc.sync.dma_start(out=v_tab[1][:], in_=words(tab_words, 1))
+        nc.sync.dma_start(out=idx2[:], in_=offs2)
 
         v_row, v2_row = 0, 8
         for q in range(QUADS):
@@ -100,11 +100,15 @@ def tile_list_two_sided_match_kernel(
                 v2_c[a, h][:], v2_tab[a][:].bitcast(U32).indirect(idx2[:, h * cols : (h + 1) * cols])
             )
 
+        v_listed = [keep.tile([P, S], U32, name=f"v_listed{a}", align_bytes=64) for a in range(k_passes)]
+        for a in range(k_passes):
+            nc.vector.tensor_copy(v_listed[a][:], v_tab[a][:].bitcast(U32).indirect(idx[:]))
+        nc.vector.tensor_copy(v_s_listed[:], v_tab_s[:].bitcast(U8).indirect(idx[:]))
         for a in range(k_passes):
             nc.vector.tensor_copy(
-                v_c[a][:].rearrange("p b t m -> p b m t"), v_tab[a][:].bitcast(U32).indirect(idx[:])
+                v_c[a][:].bitcast(I32).rearrange("p b t (g r) -> p b g t r", r=4),
+                v_listed[a][:].bitcast(I32).rearrange("p (b g r t) -> p b g t r", b=i_passes, r=4, t=PACK),
             )
-        nc.vector.tensor_copy(v_s_listed[:], v_tab_s[:].bitcast(U8).indirect(idx[:]))
         wt_t = reuse_v.tile([P, i_passes, PACK], F32, name="wt_t", align_bytes=64, offset=2112)
         wi_s = reuse_v.tile([P, i_passes, N // 4], I32, name="wi_s", align_bytes=64, offset=2176)
         nc.sync.dma_start(out=wt_t[:], in_=wt.rearrange("(b p t) -> p b t", p=P, t=PACK))
@@ -165,8 +169,8 @@ def tile_list_two_sided_match_kernel(
             wo_bf = ring.tile([P, i_passes, half * PACK], BF16, name="wo_bf", tag="above", bufs=5, align_bytes=64)
             for b in range(i_passes):
                 nc.scalar.copy(
-                    wo_bf[:, b, :].rearrange("p (c r t) -> p c t r", r=RUN, t=PACK),
-                    wo_raw[b][:, :, u * half : (u + 1) * half].rearrange("p t (c r) -> p c t r", r=RUN),
+                    wo_bf[:, b, :].rearrange("p (c r t) -> p c t r", r=4, t=PACK),
+                    wo_raw[b][:, :, u * half : (u + 1) * half].rearrange("p t (c r) -> p c t r", r=4),
                 )
             nc.vector.quantize_mx(
                 out=wo_c[u][:].rearrange("p b n -> p (b n)").bitcast(FP8X4),

@@ -38,169 +38,208 @@ def tile_list_two_sided_match_kernel(
 
     with ExitStack() as ctx:
         keep = ctx.enter_context(tc.tile_pool(name="keep", bufs=1))
-        reuse = ctx.enter_context(tc.tile_pool(name="reuse", bufs=1))
-        reuse_v = ctx.enter_context(tc.tile_pool(name="reuse_v", bufs=1))
+        stage = ctx.enter_context(tc.tile_pool(name="stage", bufs=1))
         ring = ctx.enter_context(tc.tile_pool(name="ring", bufs=3))
         psum = ctx.enter_context(tc.psum_pool(name="psum", bufs=8))
 
-        idx = keep.tile([P, S // LIST_ROWS], U16, name="idx")
-        idx2 = keep.tile([P, S2 // LIST_ROWS], U16, name="idx2")
-        v_tab_s = reuse_v.tile([P, T // 4], I32, name="v_tab_s", align_bytes=64, offset=1024)
-        v2_tab_s = reuse.tile([P, T2 // 4], I32, name="v2_tab_s", align_bytes=64, offset=1024)
-        neg_res = keep.tile([P, i_passes, PACK], F32, name="neg_res")
-        warm = keep.tile([P, 8], F32, name="warm")
+        def staged(shape, dtype, name, offset):
+            return stage.tile(shape, dtype, name=name, align_bytes=64, offset=offset)
 
         def words(table, a):
             return table[a].rearrange("p t i -> p (t i)").bitcast(I32)
 
+        idx = keep.tile([P, S // LIST_ROWS], U16, name="idx")
+        idx2 = keep.tile([P, S2 // LIST_ROWS], U16, name="idx2")
+        neg_res = keep.tile([P, i_passes, PACK], F32, name="neg_res")
+
+        LAP = 64
+        at_v2_0 = 0
+        at_res = at_v2_0 + 4 * T2
+        at_wt = at_res + LAP
+        at_v1 = at_wt + LAP
+        at_warm = at_res - LAP
+        at_wo0 = at_v1 + 4 * T
+        at_v0 = at_wo0 + 4 * PACK * N - LAP
+        at_v2_1 = at_v0 + 4 * T - LAP
+        at_wo1 = at_v2_1 + 4 * T2
+        at_listed0 = at_wo1 + 4 * PACK * N - LAP
+        at_vs = at_listed0 + 4 * S
+        at_v2_first = at_vs + T
+        at_v2s = at_v2_first + 4 * BANK - LAP
+        at_listed1 = [at_v2s + T2 - LAP, at_v2s + LAP]
+        at_v2_rest = at_listed1[0] + 4 * PASS - LAP
+        at_above = at_v2_rest + 3 * 4 * BANK
+        above_bytes = 4 * PACK * BANK
+
+        v2_tab_s = staged([P, T2 // 4], I32, "v2_tab_s", at_v2s)
+        v_tab_s = staged([P, T // 4], I32, "v_tab_s", at_vs)
+        warm = staged([P, LAP], F32, "warm", at_warm)
         nc.vector.memset(v2_tab_s[:], 0)
-        nc.vector.memset(v_tab_s[:], 0)
         nc.vector.memset(warm[:], 0.0)
+        nc.vector.memset(v_tab_s[:], 0)
 
-        res_t = keep.tile([P, i_passes, PACK], F32, name="res_t", tag="slot_a", align_bytes=64)
-        v_tab = [keep.tile([P, T], I32, name=f"v_tab{a}", tag=tag, align_bytes=64) for a, tag in enumerate(["slot_b", "slot_c"])]
-        v2_tab = [keep.tile([P, T2], I32, name=f"v2_tab{a}", tag=tag, align_bytes=64) for a, tag in enumerate(["slot_a", "slot_b"])]
-        wo_raw = [keep.tile([P, PACK, N], F32, name=f"wo_raw{b}", tag=tag, align_bytes=64) for b, tag in enumerate(["slot_a", "slot_b"])]
-        wi_c = keep.tile([P, i_passes, N // 2], I32, name="wi_c", tag="slot_c", align_bytes=64)
-
-        nc.sync.dma_start(out=v_tab[0][:], in_=words(tab_words, 0))
-        nc.sync.dma_start(out=idx[:], in_=offs)
-        nc.sync.dma_start(out=res_t[:], in_=res.rearrange("(b p t) -> p b t", p=P, t=PACK))
-        nc.sync.dma_start(out=v_tab[1][:], in_=words(tab_words, 1))
-        nc.sync.dma_start(out=idx2[:], in_=offs2)
+        v_tab = [staged([P, T], I32, f"v_tab{a}", at) for a, at in enumerate([at_v0, at_v1])]
+        v2_tab = [staged([P, T2], I32, f"v2_tab{a}", at) for a, at in enumerate([at_v2_0, at_v2_1])]
+        wo_raw = [staged([P, PACK, N], F32, f"wo_raw{b}", at) for b, at in enumerate([at_wo0, at_wo1])]
+        res_t = staged([P, i_passes, PACK], F32, "res_t", at_res)
+        wt_t = staged([P, i_passes, PACK], F32, "wt_t", at_wt)
 
         v_row, v2_row = 0, 8
-        for q in range(QUADS):
-            queue = nc.gpsimd if q < 2 else nc.sync
-            queue.dma_start(
-                out=v2_tab_s[32 * q + v2_row : 32 * q + v2_row + 8, :],
-                in_=tab2_scales.bitcast(I32)[:, 4 * q : 4 * q + 4, :],
-            )
+        nc.sync.dma_start(out=v_tab[0][:], in_=words(tab_words, 0))
+        nc.sync.dma_start(out=idx[:], in_=offs)
+        nc.sync.dma_start(out=idx2[:], in_=offs2)
         for q in range(QUADS):
             nc.sync.dma_start(
                 out=v_tab_s[32 * q + v_row : 32 * q + v_row + 8, :],
                 in_=tab_scales.bitcast(I32)[:, 4 * q : 4 * q + 4, :],
             )
+        for q in range(QUADS):
+            nc.gpsimd.dma_start(
+                out=v2_tab_s[32 * q + v2_row : 32 * q + v2_row + 8, :],
+                in_=tab2_scales.bitcast(I32)[:, 4 * q : 4 * q + 4, :],
+            )
         nc.scalar.activation(warm[:, 0:1], warm[:, 1:2], ACT.Sigmoid)
-        nc.vector.tensor_scalar_mul(neg_res[:], res_t[:], -1.0)
         nc.sync.dma_start(out=v2_tab[0][:], in_=words(tab2_words, 0))
-        nc.sync.dma_start(out=v2_tab[1][:], in_=words(tab2_words, 1))
+        nc.sync.dma_start(out=v_tab[1][:], in_=words(tab_words, 1))
+        nc.sync.dma_start(out=res_t[:], in_=res.rearrange("(b p t) -> p b t", p=P, t=PACK))
+        nc.sync.dma_start(out=wt_t[:], in_=wt.rearrange("(b p t) -> p b t", p=P, t=PACK))
+        nc.scalar.mul(neg_res[:], res_t[:], -1.0)
 
+        v_listed0 = staged([P, S], U32, "v_listed0", at_listed0)
+        v_listed1 = [staged([P, PASS], U32, f"v_listed1_{b}", at_listed1[b]) for b in range(i_passes)]
         v_c = [keep.tile([P, i_passes, PACK, P], U32, name=f"v_c{a}", align_bytes=64) for a in range(k_passes)]
         v_s_listed = keep.tile([P, S], U8, name="v_s_listed", align_bytes=64)
         v_s = keep.tile([P, i_passes, PACK, P], U8, name="v_s", align_bytes=64)
-        v2_c = {(0, 0): reuse_v.tile([P, BANK], U32, name="v2_c0_0", align_bytes=64, offset=0)}
-        v2_c[0, 1] = keep.tile([P, BANK], U32, name="v2_c0_1", align_bytes=64)
-        for h in range(j_chunks):
-            v2_c[1, h] = reuse.tile([P, BANK], U32, name=f"v2_c1_{h}", align_bytes=64, offset=2048 * h)
+        v2_first = staged([P, BANK], U32, "v2_first", at_v2_first)
+        v2_rest = staged([P, 3, BANK], U32, "v2_rest", at_v2_rest)
+        v2_c = {(0, 0): v2_first[:], (1, 0): v2_rest[:, 0, :], (0, 1): v2_rest[:, 1, :], (1, 1): v2_rest[:, 2, :]}
         v2_s = keep.tile([P, S2], U8, name="v2_s", align_bytes=64)
 
-        def gather_v2_words(a, h):
+        def order_v_words(ordered, listed, passes):
             nc.vector.tensor_copy(
-                v2_c[a, h][:], v2_tab[a][:].bitcast(U32).indirect(idx2[:, h * cols : (h + 1) * cols])
+                ordered.bitcast(I32).rearrange("p b t (g r) -> p b g t r", r=4),
+                listed.bitcast(I32).rearrange("p (b g r t) -> p b g t r", b=passes, r=4, t=PACK),
             )
 
-        v_listed = [keep.tile([P, S], U32, name=f"v_listed{a}", align_bytes=64) for a in range(k_passes)]
-        for a in range(k_passes):
-            nc.vector.tensor_copy(v_listed[a][:], v_tab[a][:].bitcast(U32).indirect(idx[:]))
+        def gather_v2_words(a, h):
+            nc.vector.tensor_copy(v2_c[a, h], v2_tab[a][:].bitcast(U32).indirect(idx2[:, h * cols : (h + 1) * cols]))
+
+        nc.vector.tensor_copy(v_listed0[:], v_tab[0][:].bitcast(U32).indirect(idx[:]))
         nc.vector.tensor_copy(v_s_listed[:], v_tab_s[:].bitcast(U8).indirect(idx[:]))
-        for a in range(k_passes):
-            nc.vector.tensor_copy(
-                v_c[a][:].bitcast(I32).rearrange("p b t (g r) -> p b g t r", r=4),
-                v_listed[a][:].bitcast(I32).rearrange("p (b g r t) -> p b g t r", b=i_passes, r=4, t=PACK),
+        order_v_words(v_c[0][:], v_listed0[:], i_passes)
+        nc.vector.tensor_copy(v_s[:], v_s_listed[:].rearrange("p (b m t) -> p b t m", b=i_passes, t=PACK))
+
+        nc.sync.dma_start(out=v2_tab[1][:], in_=words(tab2_words, 1))
+        for b in range(i_passes):
+            nc.sync.dma_start(
+                out=wo_raw[b][:], in_=wo[b * PASS : (b + 1) * PASS, :].rearrange("(p t) n -> p t n", t=PACK)
             )
-        wt_t = reuse_v.tile([P, i_passes, PACK], F32, name="wt_t", align_bytes=64, offset=2112)
-        wi_s = reuse_v.tile([P, i_passes, N // 4], I32, name="wi_s", align_bytes=64, offset=2176)
-        nc.sync.dma_start(out=wt_t[:], in_=wt.rearrange("(b p t) -> p b t", p=P, t=PACK))
+        wi_c = staged([P, i_passes, N // 2], I32, "wi_c", at_listed0 + LAP)
+        wi_s = staged([P, i_passes, N // 4], I32, "wi_s", at_vs)
+        nc.sync.dma_start(out=wi_c[:], in_=wi_words.bitcast(I32).rearrange("b p w -> p b w"))
         nc.vector.memset(wi_s[:], 0)
         for q in range(QUADS):
             nc.sync.dma_start(
                 out=wi_s[32 * q : 32 * q + 4, :, :],
                 in_=wi_scales.bitcast(I32)[:, 4 * q : 4 * q + 4, :].rearrange("b r w -> r b w"),
             )
-        nc.sync.dma_start(out=wi_c[:], in_=wi_words.bitcast(I32).rearrange("b p w -> p b w"))
-        for b in range(i_passes):
-            nc.sync.dma_start(
-                out=wo_raw[b][:], in_=wo[b * PASS : (b + 1) * PASS, :].rearrange("(p t) n -> p t n", t=PACK)
-            )
-        nc.vector.tensor_copy(v_s[:], v_s_listed[:].rearrange("p (b m t) -> p b t m", b=i_passes, t=PACK))
+
         nc.vector.tensor_copy(v2_s[:], v2_tab_s[:].bitcast(U8).indirect(idx2[:]))
         gather_v2_words(0, 0)
+        for b in range(i_passes):
+            nc.vector.tensor_copy(
+                v_listed1[b][:], v_tab[1][:].bitcast(U32).indirect(idx[:, b * cols : (b + 1) * cols])
+            )
+        order_v_words(v_c[1][:, 0:1], v_listed1[0][:], 1)
         gather_v2_words(1, 0)
+        order_v_words(v_c[1][:, 1:2], v_listed1[1][:], 1)
+        gather_v2_words(0, 1)
+        gather_v2_words(1, 1)
 
         z_c = {}
         z_s = {}
         z_bf = {}
+        above = {}
+        fit = {}
+        wo_bf = {}
         wo_c = [keep.tile([P, i_passes, half], U32, name=f"wo_c{u}", align_bytes=64) for u in range(2)]
         wo_s = [keep.tile([P, i_passes, half], U8, name=f"wo_s{u}", align_bytes=64) for u in range(2)]
 
-        def surplus(h, b, pieces=1):
-            width = BANK // pieces
+        def fit_pass(h, b, t, a):
+            if a == 0:
+                fit[h, b, t] = psum.tile([P, BANK], F32, name="bank")
+            nc.tensor.matmul_mx(
+                out=fit[h, b, t][:],
+                lhsT=v_c[a][:, b, t, :].bitcast(FP8X4),
+                lhsT_scale=v_s[v_row + 4 * a : P, b, t, :],
+                rhs=v2_c[a, h].bitcast(FP8X4),
+                rhs_scale=v2_s[v2_row + 4 * a : P, BANK * h : BANK * (h + 1)],
+                start=(a == 0),
+                stop=(a == k_passes - 1),
+            )
+
+        def surplus(h, b, first_pass=0):
+            above[h, b] = staged([P, PACK, BANK], F32, f"above{h}_{b}", at_above + above_bytes * (2 * h + b))
+            for t in range(PACK):
+                for a in range(first_pass, k_passes):
+                    fit_pass(h, b, t, a)
+                nc.scalar.activation(above[h, b][:, t, :], fit[h, b, t][:], ACT.Relu, bias=neg_res[:, b, t : t + 1])
+
+        def weigh(h, b):
             z_bf[h, b] = ring.tile([P, BANK * PACK], BF16, name="z_bf", align_bytes=64)
-            for piece in range(pieces):
-                j0 = width * piece
-                above = ring.tile([P, PACK, width], F32, name="above", bufs=5, align_bytes=64)
-                for t in range(PACK):
-                    fit = psum.tile([P, width], F32, name="bank")
-                    for a in range(k_passes):
-                        nc.tensor.matmul_mx(
-                            out=fit[:],
-                            lhsT=v_c[a][:, b, t, :].bitcast(FP8X4),
-                            lhsT_scale=v_s[v_row + 4 * a : P, b, t, :],
-                            rhs=v2_c[a, h][:, j0 : j0 + width].bitcast(FP8X4),
-                            rhs_scale=v2_s[v2_row + 4 * a : P, BANK * h + j0 : BANK * h + j0 + width],
-                            start=(a == 0),
-                            stop=(a == k_passes - 1),
-                        )
-                    nc.scalar.activation(above[:, t, :], fit[:], ACT.Relu, bias=neg_res[:, b, t : t + 1])
-                nc.vector.tensor_tensor(
-                    z_bf[h, b][:, PACK * j0 : PACK * (j0 + width)].rearrange("p (c r t) -> p c t r", r=RUN, t=PACK),
-                    above[:].rearrange("p t (c r) -> p c t r", r=RUN),
-                    wt_t[:, b, :].unsqueeze(1).unsqueeze(3).to_broadcast([P, width // RUN, PACK, RUN]),
-                    MULT,
-                )
+            nc.vector.tensor_tensor(
+                z_bf[h, b][:].rearrange("p (c r t) -> p c t r", r=RUN, t=PACK),
+                above[h, b][:].rearrange("p t (c r) -> p c t r", r=RUN),
+                wt_t[:, b, :].unsqueeze(1).unsqueeze(3).to_broadcast([P, BANK // RUN, PACK, RUN]),
+                MULT,
+            )
 
         def quantise_z(h, b):
             z_c[h, b] = keep.tile([P, BANK], U32, name=f"z_c{h}_{b}", align_bytes=64)
             z_s[h, b] = keep.tile([P, BANK], U8, name=f"z_s{h}_{b}", align_bytes=64)
             nc.vector.quantize_mx(out=z_c[h, b][:].bitcast(FP8X4), scales=z_s[h, b][:], in_=z_bf[h, b][:])
 
-        def quantise_wo(u):
-            wo_bf = ring.tile([P, i_passes, half * PACK], BF16, name="wo_bf", tag="above", bufs=5, align_bytes=64)
+        def round_wo(u):
+            wo_bf[u] = staged([P, i_passes, half * PACK], BF16, f"wo_bf{u}", at_above + above_bytes * 2 * u)
             for b in range(i_passes):
                 nc.scalar.copy(
-                    wo_bf[:, b, :].rearrange("p (c r t) -> p c t r", r=4, t=PACK),
+                    wo_bf[u][:, b, :].rearrange("p (c r t) -> p c t r", r=4, t=PACK),
                     wo_raw[b][:, :, u * half : (u + 1) * half].rearrange("p t (c r) -> p c t r", r=4),
                 )
+
+        def quantise_wo(u):
             nc.vector.quantize_mx(
                 out=wo_c[u][:].rearrange("p b n -> p (b n)").bitcast(FP8X4),
                 scales=wo_s[u][:].rearrange("p b n -> p (b n)"),
-                in_=wo_bf[:].rearrange("p b w -> p (b w)"),
+                in_=wo_bf[u][:].rearrange("p b w -> p (b w)"),
             )
 
         chance = {}
+        score = {}
 
-        def interest(h, n):
-            score = psum.tile([P, BANK], F32, name="bank")
-            for b in range(i_passes):
-                nc.tensor.matmul_mx(
-                    out=score[:],
-                    lhsT=wi_c[:, b, :].bitcast(U8)[:, 2 * P * n : 2 * P * (n + 1)].bitcast(FP4X4),
-                    lhsT_scale=wi_s[:, b, :].bitcast(U8)[:, P * n : P * (n + 1)],
-                    rhs=z_c[h, b][:].bitcast(FP8X4),
-                    rhs_scale=z_s[h, b][:],
-                    start=(b == 0),
-                    stop=(b == i_passes - 1),
-                )
+        def interest_pass(h, n, b):
+            if b == 0:
+                score["interest", h, n] = psum.tile([P, BANK], F32, name="bank")
+            nc.tensor.matmul_mx(
+                out=score["interest", h, n][:],
+                lhsT=wi_c[:, b, :].bitcast(U8)[:, 2 * P * n : 2 * P * (n + 1)].bitcast(FP4X4),
+                lhsT_scale=wi_s[:, b, :].bitcast(U8)[:, P * n : P * (n + 1)],
+                rhs=z_c[h, b][:].bitcast(FP8X4),
+                rhs_scale=z_s[h, b][:],
+                start=(b == 0),
+                stop=(b == i_passes - 1),
+            )
+
+        def sigmoid(h, n):
             chance[h, n] = keep.tile([P, BANK], F32, name=f"chance{h}_{n}")
-            nc.scalar.activation(chance[h, n][:], score[:], ACT.Sigmoid)
+            nc.scalar.activation(chance[h, n][:], score["interest", h, n][:], ACT.Sigmoid)
 
-        def offer(h, n):
+        def offer_passes(h, n):
             u, n_cols = n // 2, slice(P * (n % 2), P * (n % 2 + 1))
-            score = psum.tile([P, BANK], F32, name="bank")
+            score["offer", h, n] = psum.tile([P, BANK], F32, name="bank")
             for b in range(i_passes):
                 nc.tensor.matmul_mx(
-                    out=score[:],
+                    out=score["offer", h, n][:],
                     lhsT=wo_c[u][:, b, n_cols].bitcast(FP8X4),
                     lhsT_scale=wo_s[u][:, b, n_cols],
                     rhs=z_c[h, b][:].bitcast(FP8X4),
@@ -208,35 +247,58 @@ def tile_list_two_sided_match_kernel(
                     start=(b == 0),
                     stop=(b == i_passes - 1),
                 )
+
+        def finish(h, n):
             result = keep.tile([P, BANK], F32, name=f"result{h}_{n}")
-            nc.vector.tensor_tensor(result[:], score[:], chance[h, n][:], MULT)
+            nc.vector.tensor_tensor(result[:], score["offer", h, n][:], chance[h, n][:], MULT)
             nc.sync.dma_start(out=out[P * n : P * (n + 1), BANK * h : BANK * (h + 1)], in_=result[:])
 
-        surplus(0, 0, pieces=2)
-        gather_v2_words(0, 1)
-        gather_v2_words(1, 1)
+        for b in range(i_passes):
+            for t in range(PACK):
+                fit_pass(0, b, t, 0)
+        surplus(0, 0, first_pass=1)
+        surplus(0, 1, first_pass=1)
+        weigh(0, 0)
         quantise_z(0, 0)
-        surplus(0, 1)
+        weigh(0, 1)
         quantise_z(0, 1)
         surplus(1, 0)
+        round_wo(0)
+        surplus(1, 1)
+        for b in range(i_passes):
+            for n in range(n_tiles):
+                interest_pass(0, n, b)
+        weigh(1, 0)
         quantise_z(1, 0)
         quantise_wo(0)
-        surplus(1, 1)
-        interest(0, 0)
-        interest(0, 1)
-        interest(0, 2)
-        interest(0, 3)
+        first, second = (0, 1), (2, 3)
+        for n in first:
+            sigmoid(0, n)
+            offer_passes(0, n)
+        weigh(1, 1)
         quantise_z(1, 1)
-        offer(0, 0)
-        offer(0, 1)
-        interest(1, 0)
-        interest(1, 1)
+        round_wo(1)
+        for n in second:
+            sigmoid(0, n)
+        for b in range(i_passes):
+            for n in first:
+                interest_pass(1, n, b)
+        for n in first:
+            finish(0, n)
         quantise_wo(1)
-        offer(1, 0)
-        offer(1, 1)
-        interest(1, 2)
-        interest(1, 3)
-        offer(0, 2)
-        offer(0, 3)
-        offer(1, 2)
-        offer(1, 3)
+        for n in first:
+            offer_passes(1, n)
+            sigmoid(1, n)
+        for n in second:
+            offer_passes(0, n)
+        for n in first:
+            finish(1, n)
+        for n in second:
+            for b in range(i_passes):
+                interest_pass(1, n, b)
+            sigmoid(1, n)
+        for n in second:
+            finish(0, n)
+        for n in second:
+            offer_passes(1, n)
+            finish(1, n)

@@ -21,7 +21,7 @@ PACK = 4
 PASS = P * PACK
 QUADS = 4
 BANK = 512
-RUN = 2
+RUN = 4
 LIST_ROWS = 16
 
 
@@ -64,11 +64,9 @@ def tile_list_two_sided_match_kernel(
         at_wo1 = at_v2_1 + 4 * T2
         at_listed0 = at_wo1 + 4 * PACK * N - LAP
         at_vs = at_listed0 + 4 * S
-        at_v2_first = at_vs + T
-        at_v2s = at_v2_first + 4 * BANK - LAP
-        at_listed1 = [at_v2s + T2 - LAP, at_v2s + LAP]
-        at_v2_rest = at_listed1[0] + 4 * PASS - LAP
-        at_above = at_v2_rest + 3 * 4 * BANK
+        at_v2s = at_vs + T
+        at_listed1 = [at_v2s + T2 - LAP, at_v2s]
+        at_above = at_listed1[0] + 4 * PASS
         above_bytes = 4 * PACK * BANK
 
         v2_tab_s = staged([P, T2 // 4], I32, "v2_tab_s", at_v2s)
@@ -94,15 +92,16 @@ def tile_list_two_sided_match_kernel(
                 in_=tab_scales.bitcast(I32)[:, 4 * q : 4 * q + 4, :],
             )
         for q in range(QUADS):
-            nc.gpsimd.dma_start(
+            queue = nc.gpsimd if q < 2 else nc.sync
+            queue.dma_start(
                 out=v2_tab_s[32 * q + v2_row : 32 * q + v2_row + 8, :],
                 in_=tab2_scales.bitcast(I32)[:, 4 * q : 4 * q + 4, :],
             )
         nc.scalar.activation(warm[:, 0:1], warm[:, 1:2], ACT.Sigmoid)
-        nc.sync.dma_start(out=v2_tab[0][:], in_=words(tab2_words, 0))
-        nc.sync.dma_start(out=v_tab[1][:], in_=words(tab_words, 1))
         nc.sync.dma_start(out=res_t[:], in_=res.rearrange("(b p t) -> p b t", p=P, t=PACK))
         nc.sync.dma_start(out=wt_t[:], in_=wt.rearrange("(b p t) -> p b t", p=P, t=PACK))
+        nc.sync.dma_start(out=v2_tab[0][:], in_=words(tab2_words, 0))
+        nc.sync.dma_start(out=v_tab[1][:], in_=words(tab_words, 1))
         nc.scalar.mul(neg_res[:], res_t[:], -1.0)
 
         v_listed0 = staged([P, S], U32, "v_listed0", at_listed0)
@@ -110,9 +109,8 @@ def tile_list_two_sided_match_kernel(
         v_c = [keep.tile([P, i_passes, PACK, P], U32, name=f"v_c{a}", align_bytes=64) for a in range(k_passes)]
         v_s_listed = keep.tile([P, S], U8, name="v_s_listed", align_bytes=64)
         v_s = keep.tile([P, i_passes, PACK, P], U8, name="v_s", align_bytes=64)
-        v2_first = staged([P, BANK], U32, "v2_first", at_v2_first)
-        v2_rest = staged([P, 3, BANK], U32, "v2_rest", at_v2_rest)
-        v2_c = {(0, 0): v2_first[:], (1, 0): v2_rest[:, 0, :], (0, 1): v2_rest[:, 1, :], (1, 1): v2_rest[:, 2, :]}
+        v2_c = {ah: keep.tile([P, BANK], U32, name=f"v2_c{ah[0]}_{ah[1]}", align_bytes=64) for ah in [(0, 0), (1, 0), (1, 1)]}
+        v2_c[0, 1] = staged([P, BANK], U32, "v2_c0_1", at_v2_1 + LAP + 2 * PACK * N)
         v2_s = keep.tile([P, S2], U8, name="v2_s", align_bytes=64)
 
         def order_v_words(ordered, listed, passes):
@@ -122,7 +120,10 @@ def tile_list_two_sided_match_kernel(
             )
 
         def gather_v2_words(a, h):
-            nc.vector.tensor_copy(v2_c[a, h], v2_tab[a][:].bitcast(U32).indirect(idx2[:, h * cols : (h + 1) * cols]))
+            nc.vector.tensor_copy(
+                v2_c[a, h][:],
+                v2_tab[a][:].bitcast(U32).indirect(idx2[:, h * cols : (h + 1) * cols]),
+            )
 
         nc.vector.tensor_copy(v_listed0[:], v_tab[0][:].bitcast(U32).indirect(idx[:]))
         nc.vector.tensor_copy(v_s_listed[:], v_tab_s[:].bitcast(U8).indirect(idx[:]))
@@ -150,18 +151,21 @@ def tile_list_two_sided_match_kernel(
             nc.vector.tensor_copy(
                 v_listed1[b][:], v_tab[1][:].bitcast(U32).indirect(idx[:, b * cols : (b + 1) * cols])
             )
-        order_v_words(v_c[1][:, 0:1], v_listed1[0][:], 1)
+        for b in range(i_passes):
+            order_v_words(v_c[1][:, b : b + 1], v_listed1[b][:], 1)
         gather_v2_words(1, 0)
-        order_v_words(v_c[1][:, 1:2], v_listed1[1][:], 1)
-        gather_v2_words(0, 1)
         gather_v2_words(1, 1)
+        gather_v2_words(0, 1)
 
         z_c = {}
         z_s = {}
         z_bf = {}
         above = {}
         fit = {}
-        wo_bf = {}
+        wo_bf = [
+            staged([P, i_passes, half * PACK], BF16, f"wo_bf{u}", at)
+            for u, at in enumerate([at_v2_1 + LAP, at_above + above_bytes * 2])
+        ]
         wo_c = [keep.tile([P, i_passes, half], U32, name=f"wo_c{u}", align_bytes=64) for u in range(2)]
         wo_s = [keep.tile([P, i_passes, half], U8, name=f"wo_s{u}", align_bytes=64) for u in range(2)]
 
@@ -172,7 +176,7 @@ def tile_list_two_sided_match_kernel(
                 out=fit[h, b, t][:],
                 lhsT=v_c[a][:, b, t, :].bitcast(FP8X4),
                 lhsT_scale=v_s[v_row + 4 * a : P, b, t, :],
-                rhs=v2_c[a, h].bitcast(FP8X4),
+                rhs=v2_c[a, h][:].bitcast(FP8X4),
                 rhs_scale=v2_s[v2_row + 4 * a : P, BANK * h : BANK * (h + 1)],
                 start=(a == 0),
                 stop=(a == k_passes - 1),
@@ -199,13 +203,11 @@ def tile_list_two_sided_match_kernel(
             z_s[h, b] = keep.tile([P, BANK], U8, name=f"z_s{h}_{b}", align_bytes=64)
             nc.vector.quantize_mx(out=z_c[h, b][:].bitcast(FP8X4), scales=z_s[h, b][:], in_=z_bf[h, b][:])
 
-        def round_wo(u):
-            wo_bf[u] = staged([P, i_passes, half * PACK], BF16, f"wo_bf{u}", at_above + above_bytes * 2 * u)
-            for b in range(i_passes):
-                nc.scalar.copy(
-                    wo_bf[u][:, b, :].rearrange("p (c r t) -> p c t r", r=4, t=PACK),
-                    wo_raw[b][:, :, u * half : (u + 1) * half].rearrange("p t (c r) -> p c t r", r=4),
-                )
+        def round_wo(u, b, copy):
+            copy(
+                wo_bf[u][:, b, :].rearrange("p (c r t) -> p c t r", r=4, t=PACK),
+                wo_raw[b][:, :, u * half : (u + 1) * half].rearrange("p t (c r) -> p c t r", r=4),
+            )
 
         def quantise_wo(u):
             nc.vector.quantize_mx(
@@ -263,7 +265,8 @@ def tile_list_two_sided_match_kernel(
         weigh(0, 1)
         quantise_z(0, 1)
         surplus(1, 0)
-        round_wo(0)
+        for b in range(i_passes):
+            round_wo(0, b, nc.scalar.copy)
         surplus(1, 1)
         for b in range(i_passes):
             for n in range(n_tiles):
@@ -277,7 +280,8 @@ def tile_list_two_sided_match_kernel(
             offer_passes(0, n)
         weigh(1, 1)
         quantise_z(1, 1)
-        round_wo(1)
+        for b in range(i_passes):
+            round_wo(1, b, nc.scalar.copy)
         for n in second:
             sigmoid(0, n)
         for b in range(i_passes):

@@ -34,7 +34,6 @@ def tile_list_two_sided_match_kernel(
     j_chunks = S2 // BANK
     n_tiles = N // P
     cols = BANK // LIST_ROWS
-    half = N // 2
 
     with ExitStack() as ctx:
         keep = ctx.enter_context(tc.tile_pool(name="keep", bufs=1))
@@ -64,12 +63,8 @@ def tile_list_two_sided_match_kernel(
         at_wo1 = at_v2_1 + 4 * T2
         at_listed0 = at_wo1 + 4 * PACK * N - LAP
         at_vs = at_listed0 + 4 * S
-        at_v2s = at_vs + T
-        at_listed1 = [at_v2s + T2 - LAP, at_v2s]
-        at_above = at_listed1[0] + 4 * PASS
-        above_bytes = 4 * PACK * BANK
 
-        v2_tab_s = staged([P, T2 // 4], I32, "v2_tab_s", at_v2s)
+        v2_tab_s = keep.tile([P, T2 // 4], I32, name="v2_tab_s", align_bytes=64)
         v_tab_s = staged([P, T // 4], I32, "v_tab_s", at_vs)
         warm = staged([P, LAP], F32, "warm", at_warm)
         nc.vector.memset(v2_tab_s[:], 0)
@@ -103,15 +98,28 @@ def tile_list_two_sided_match_kernel(
         nc.sync.dma_start(out=v2_tab[0][:], in_=words(tab2_words, 0))
         nc.sync.dma_start(out=v_tab[1][:], in_=words(tab_words, 1))
         nc.scalar.mul(neg_res[:], res_t[:], -1.0)
+        wt_size = keep.tile([P, i_passes, PACK], F32, name="wt_size")
+        wt_sign = keep.tile([P, i_passes, PACK], BF16, name="wt_sign")
+        neg_level = keep.tile([P, i_passes, PACK], F32, name="neg_level")
+        nc.scalar.activation(wt_size[:], wt_t[:], ACT.Abs)
+        nc.scalar.activation(wt_sign[:], wt_t[:], ACT.Sign)
+        for b in range(i_passes):
+            for t in range(PACK):
+                nc.scalar.activation(
+                    neg_level[:, b, t : t + 1], neg_res[:, b, t : t + 1], ACT.Copy, scale=wt_size[:, b, t : t + 1]
+                )
 
         v_listed0 = staged([P, S], U32, "v_listed0", at_listed0)
-        v_listed1 = [staged([P, PASS], U32, f"v_listed1_{b}", at_listed1[b]) for b in range(i_passes)]
+        v_listed1 = [keep.tile([P, PASS], U32, name=f"v_listed1_{b}", align_bytes=64) for b in range(i_passes)]
         v_c = [keep.tile([P, i_passes, PACK, P], U32, name=f"v_c{a}", align_bytes=64) for a in range(k_passes)]
         v_s_listed = keep.tile([P, S], U8, name="v_s_listed", align_bytes=64)
         v_s = keep.tile([P, i_passes, PACK, P], U8, name="v_s", align_bytes=64)
         v2_c = {ah: keep.tile([P, BANK], U32, name=f"v2_c{ah[0]}_{ah[1]}", align_bytes=64) for ah in [(0, 0), (1, 0), (1, 1)]}
-        v2_c[0, 1] = staged([P, BANK], U32, "v2_c0_1", at_v2_1 + LAP + 2 * PACK * N)
-        v2_s = keep.tile([P, S2], U8, name="v2_s", align_bytes=64)
+        v2_c[0, 1] = staged([P, BANK], U32, "v2_c0_1", at_v2_1 + LAP)
+        v2_s = [
+            keep.tile([P, BANK], U8, name="v2_s0", align_bytes=64),
+            staged([P, BANK], U8, "v2_s1", at_v2_1 + LAP + 4 * BANK),
+        ]
 
         def order_v_words(ordered, listed, passes):
             nc.vector.tensor_copy(
@@ -124,6 +132,9 @@ def tile_list_two_sided_match_kernel(
                 v2_c[a, h][:],
                 v2_tab[a][:].bitcast(U32).indirect(idx2[:, h * cols : (h + 1) * cols]),
             )
+
+        def gather_v2_scales(h):
+            nc.vector.tensor_copy(v2_s[h][:], v2_tab_s[:].bitcast(U8).indirect(idx2[:, h * cols : (h + 1) * cols]))
 
         nc.vector.tensor_copy(v_listed0[:], v_tab[0][:].bitcast(U32).indirect(idx[:]))
         nc.vector.tensor_copy(v_s_listed[:], v_tab_s[:].bitcast(U8).indirect(idx[:]))
@@ -145,7 +156,7 @@ def tile_list_two_sided_match_kernel(
                 in_=wi_scales.bitcast(I32)[:, 4 * q : 4 * q + 4, :].rearrange("b r w -> r b w"),
             )
 
-        nc.vector.tensor_copy(v2_s[:], v2_tab_s[:].bitcast(U8).indirect(idx2[:]))
+        gather_v2_scales(0)
         gather_v2_words(0, 0)
         for b in range(i_passes):
             nc.vector.tensor_copy(
@@ -156,18 +167,16 @@ def tile_list_two_sided_match_kernel(
         gather_v2_words(1, 0)
         gather_v2_words(1, 1)
         gather_v2_words(0, 1)
+        gather_v2_scales(1)
 
         z_c = {}
         z_s = {}
         z_bf = {}
         above = {}
         fit = {}
-        wo_bf = [
-            staged([P, i_passes, half * PACK], BF16, f"wo_bf{u}", at)
-            for u, at in enumerate([at_v2_1 + LAP, at_above + above_bytes * 2])
-        ]
-        wo_c = [keep.tile([P, i_passes, half], U32, name=f"wo_c{u}", align_bytes=64) for u in range(2)]
-        wo_s = [keep.tile([P, i_passes, half], U8, name=f"wo_s{u}", align_bytes=64) for u in range(2)]
+        wo_bf = [keep.tile([P, N * PACK], BF16, name=f"wo_bf{b}", align_bytes=64) for b in range(i_passes)]
+        wo_c = [keep.tile([P, N], U32, name=f"wo_c{b}", align_bytes=64) for b in range(i_passes)]
+        wo_s = [keep.tile([P, N], U8, name=f"wo_s{b}", align_bytes=64) for b in range(i_passes)]
 
         def fit_pass(h, b, t, a):
             if a == 0:
@@ -177,16 +186,15 @@ def tile_list_two_sided_match_kernel(
                 lhsT=v_c[a][:, b, t, :].bitcast(FP8X4),
                 lhsT_scale=v_s[v_row + 4 * a : P, b, t, :],
                 rhs=v2_c[a, h][:].bitcast(FP8X4),
-                rhs_scale=v2_s[v2_row + 4 * a : P, BANK * h : BANK * (h + 1)],
+                rhs_scale=v2_s[h][v2_row + 4 * a : P, :],
                 start=(a == 0),
                 stop=(a == k_passes - 1),
             )
 
-        def surplus(h, b, first_pass=0):
-            above[h, b] = staged([P, PACK, BANK], F32, f"above{h}_{b}", at_above + above_bytes * (2 * h + b))
+        def surplus(h, b):
+            above[h, b] = keep.tile([P, PACK, BANK], F32, name=f"above{h}_{b}", align_bytes=64)
             for t in range(PACK):
-                for a in range(first_pass, k_passes):
-                    fit_pass(h, b, t, a)
+                fit_pass(h, b, t, 1)
                 nc.scalar.activation(above[h, b][:, t, :], fit[h, b, t][:], ACT.Relu, bias=neg_res[:, b, t : t + 1])
 
         def weigh(h, b):
@@ -198,23 +206,41 @@ def tile_list_two_sided_match_kernel(
                 MULT,
             )
 
+        def paired_surplus(h, b, first_pass=0):
+            above[h, b] = keep.tile([P, 2, BANK, 2], BF16, name=f"above{h}_{b}", align_bytes=64)
+            for t in range(PACK):
+                for a in range(first_pass, k_passes):
+                    fit_pass(h, b, t, a)
+                nc.scalar.activation(
+                    above[h, b][:, t // 2, :, t % 2],
+                    fit[h, b, t][:],
+                    ACT.Relu,
+                    bias=neg_level[:, b, t : t + 1],
+                    scale=wt_size[:, b, t : t + 1],
+                )
+
+        def give_sign(h, b):
+            z_bf[h, b] = ring.tile([P, BANK * PACK], BF16, name="z_bf", align_bytes=64)
+            nc.vector.tensor_tensor(
+                z_bf[h, b][:].rearrange("p (c u e) -> p c u e", u=2, e=2),
+                above[h, b][:].rearrange("p u c e -> p c u e"),
+                wt_sign[:, b, :].rearrange("p (u e) -> p u e", e=2).unsqueeze(1).to_broadcast([P, BANK, 2, 2]),
+                MULT,
+            )
+
         def quantise_z(h, b):
             z_c[h, b] = keep.tile([P, BANK], U32, name=f"z_c{h}_{b}", align_bytes=64)
             z_s[h, b] = keep.tile([P, BANK], U8, name=f"z_s{h}_{b}", align_bytes=64)
             nc.vector.quantize_mx(out=z_c[h, b][:].bitcast(FP8X4), scales=z_s[h, b][:], in_=z_bf[h, b][:])
 
-        def round_wo(u, b, copy):
-            copy(
-                wo_bf[u][:, b, :].rearrange("p (c r t) -> p c t r", r=4, t=PACK),
-                wo_raw[b][:, :, u * half : (u + 1) * half].rearrange("p t (c r) -> p c t r", r=4),
+        def round_wo(b):
+            nc.vector.tensor_copy(
+                wo_bf[b][:].rearrange("p (c r t) -> p c t r", r=4, t=PACK),
+                wo_raw[b][:].rearrange("p t (c r) -> p c t r", r=4),
             )
 
-        def quantise_wo(u):
-            nc.vector.quantize_mx(
-                out=wo_c[u][:].rearrange("p b n -> p (b n)").bitcast(FP8X4),
-                scales=wo_s[u][:].rearrange("p b n -> p (b n)"),
-                in_=wo_bf[u][:].rearrange("p b w -> p (b w)"),
-            )
+        def quantise_wo(b):
+            nc.vector.quantize_mx(out=wo_c[b][:].bitcast(FP8X4), scales=wo_s[b][:], in_=wo_bf[b][:])
 
         chance = {}
         score = {}
@@ -237,13 +263,12 @@ def tile_list_two_sided_match_kernel(
             nc.scalar.activation(chance[h, n][:], score["interest", h, n][:], ACT.Sigmoid)
 
         def offer_passes(h, n):
-            u, n_cols = n // 2, slice(P * (n % 2), P * (n % 2 + 1))
             score["offer", h, n] = psum.tile([P, BANK], F32, name="bank")
             for b in range(i_passes):
                 nc.tensor.matmul_mx(
                     out=score["offer", h, n][:],
-                    lhsT=wo_c[u][:, b, n_cols].bitcast(FP8X4),
-                    lhsT_scale=wo_s[u][:, b, n_cols],
+                    lhsT=wo_c[b][:, P * n : P * (n + 1)].bitcast(FP8X4),
+                    lhsT_scale=wo_s[b][:, P * n : P * (n + 1)],
                     rhs=z_c[h, b][:].bitcast(FP8X4),
                     rhs_scale=z_s[h, b][:],
                     start=(b == 0),
@@ -258,51 +283,34 @@ def tile_list_two_sided_match_kernel(
         for b in range(i_passes):
             for t in range(PACK):
                 fit_pass(0, b, t, 0)
-        surplus(0, 0, first_pass=1)
-        surplus(0, 1, first_pass=1)
+        surplus(0, 0)
+        paired_surplus(0, 1, first_pass=1)
         weigh(0, 0)
+        round_wo(0)
         quantise_z(0, 0)
-        weigh(0, 1)
+        give_sign(0, 1)
+        quantise_wo(0)
         quantise_z(0, 1)
-        surplus(1, 0)
-        for b in range(i_passes):
-            round_wo(0, b, nc.scalar.copy)
-        surplus(1, 1)
+        paired_surplus(1, 0)
+        paired_surplus(1, 1)
         for b in range(i_passes):
             for n in range(n_tiles):
                 interest_pass(0, n, b)
-        weigh(1, 0)
-        quantise_z(1, 0)
-        quantise_wo(0)
-        first, second = (0, 1), (2, 3)
-        for n in first:
-            sigmoid(0, n)
-            offer_passes(0, n)
-        weigh(1, 1)
-        quantise_z(1, 1)
-        for b in range(i_passes):
-            round_wo(1, b, nc.scalar.copy)
-        for n in second:
-            sigmoid(0, n)
-        for b in range(i_passes):
-            for n in first:
-                interest_pass(1, n, b)
-        for n in first:
-            finish(0, n)
+        round_wo(1)
+        give_sign(1, 0)
         quantise_wo(1)
-        for n in first:
-            offer_passes(1, n)
-            sigmoid(1, n)
-        for n in second:
+        quantise_z(1, 0)
+        give_sign(1, 1)
+        quantise_z(1, 1)
+        for n in range(n_tiles):
+            sigmoid(0, n)
             offer_passes(0, n)
-        for n in first:
-            finish(1, n)
-        for n in second:
-            for b in range(i_passes):
+        for b in range(i_passes):
+            for n in range(n_tiles):
                 interest_pass(1, n, b)
-            sigmoid(1, n)
-        for n in second:
+        for n in range(n_tiles):
             finish(0, n)
-        for n in second:
+            sigmoid(1, n)
             offer_passes(1, n)
+        for n in range(n_tiles):
             finish(1, n)

@@ -110,31 +110,18 @@ def tile_list_two_sided_match_kernel(
                 )
 
         v_listed0 = staged([P, S], U32, "v_listed0", at_listed0)
-        v_listed1 = [keep.tile([P, PASS], U32, name=f"v_listed1_{b}", align_bytes=64) for b in range(i_passes)]
+        v_listed1 = keep.tile([P, S], U32, name="v_listed1", align_bytes=64)
         v_c = [keep.tile([P, i_passes, PACK, P], U32, name=f"v_c{a}", align_bytes=64) for a in range(k_passes)]
         v_s_listed = keep.tile([P, S], U8, name="v_s_listed", align_bytes=64)
         v_s = keep.tile([P, i_passes, PACK, P], U8, name="v_s", align_bytes=64)
-        v2_c = {ah: keep.tile([P, BANK], U32, name=f"v2_c{ah[0]}_{ah[1]}", align_bytes=64) for ah in [(0, 0), (1, 0), (1, 1)]}
-        v2_c[0, 1] = staged([P, BANK], U32, "v2_c0_1", at_v2_1 + LAP)
-        v2_s = [
-            keep.tile([P, BANK], U8, name="v2_s0", align_bytes=64),
-            staged([P, BANK], U8, "v2_s1", at_v2_1 + LAP + 4 * BANK),
-        ]
+        v2_c = [keep.tile([P, S2], U32, name=f"v2_c{a}", align_bytes=64) for a in range(k_passes)]
+        v2_s = keep.tile([P, S2], U8, name="v2_s", align_bytes=64)
 
         def order_v_words(ordered, listed, passes):
             nc.vector.tensor_copy(
                 ordered.bitcast(I32).rearrange("p b t (g r) -> p b g t r", r=4),
                 listed.bitcast(I32).rearrange("p (b g r t) -> p b g t r", b=passes, r=4, t=PACK),
             )
-
-        def gather_v2_words(a, h):
-            nc.vector.tensor_copy(
-                v2_c[a, h][:],
-                v2_tab[a][:].bitcast(U32).indirect(idx2[:, h * cols : (h + 1) * cols]),
-            )
-
-        def gather_v2_scales(h):
-            nc.vector.tensor_copy(v2_s[h][:], v2_tab_s[:].bitcast(U8).indirect(idx2[:, h * cols : (h + 1) * cols]))
 
         nc.vector.tensor_copy(v_listed0[:], v_tab[0][:].bitcast(U32).indirect(idx[:]))
         nc.vector.tensor_copy(v_s_listed[:], v_tab_s[:].bitcast(U8).indirect(idx[:]))
@@ -156,18 +143,15 @@ def tile_list_two_sided_match_kernel(
                 in_=wi_scales.bitcast(I32)[:, 4 * q : 4 * q + 4, :].rearrange("b r w -> r b w"),
             )
 
-        gather_v2_scales(0)
-        gather_v2_words(0, 0)
-        for b in range(i_passes):
+        nc.vector.tensor_copy(v2_s[:], v2_tab_s[:].bitcast(U8).indirect(idx2[:]))
+        nc.vector.tensor_copy(v2_c[0][:], v2_tab[0][:].bitcast(U32).indirect(idx2[:]))
+        nc.vector.tensor_copy(v_listed1[:], v_tab[1][:].bitcast(U32).indirect(idx[:]))
+        order_v_words(v_c[1][:], v_listed1[:], i_passes)
+        for h in range(j_chunks):
             nc.vector.tensor_copy(
-                v_listed1[b][:], v_tab[1][:].bitcast(U32).indirect(idx[:, b * cols : (b + 1) * cols])
+                v2_c[1][:, BANK * h : BANK * (h + 1)],
+                v2_tab[1][:].bitcast(U32).indirect(idx2[:, h * cols : (h + 1) * cols]),
             )
-        for b in range(i_passes):
-            order_v_words(v_c[1][:, b : b + 1], v_listed1[b][:], 1)
-        gather_v2_words(1, 0)
-        gather_v2_words(1, 1)
-        gather_v2_words(0, 1)
-        gather_v2_scales(1)
 
         z_c = {}
         z_s = {}
@@ -185,8 +169,8 @@ def tile_list_two_sided_match_kernel(
                 out=fit[h, b, t][:],
                 lhsT=v_c[a][:, b, t, :].bitcast(FP8X4),
                 lhsT_scale=v_s[v_row + 4 * a : P, b, t, :],
-                rhs=v2_c[a, h][:].bitcast(FP8X4),
-                rhs_scale=v2_s[h][v2_row + 4 * a : P, :],
+                rhs=v2_c[a][:, BANK * h : BANK * (h + 1)].bitcast(FP8X4),
+                rhs_scale=v2_s[v2_row + 4 * a : P, BANK * h : BANK * (h + 1)],
                 start=(a == 0),
                 stop=(a == k_passes - 1),
             )
@@ -206,10 +190,10 @@ def tile_list_two_sided_match_kernel(
                 MULT,
             )
 
-        def paired_surplus(h, b, first_pass=0):
+        def paired_surplus(h, b):
             above[h, b] = keep.tile([P, 2, BANK, 2], BF16, name=f"above{h}_{b}", align_bytes=64)
             for t in range(PACK):
-                for a in range(first_pass, k_passes):
+                for a in range(k_passes):
                     fit_pass(h, b, t, a)
                 nc.scalar.activation(
                     above[h, b][:, t // 2, :, t % 2],
@@ -284,12 +268,12 @@ def tile_list_two_sided_match_kernel(
             for t in range(PACK):
                 fit_pass(0, b, t, 0)
         surplus(0, 0)
-        paired_surplus(0, 1, first_pass=1)
-        weigh(0, 0)
+        surplus(0, 1)
         round_wo(0)
-        quantise_z(0, 0)
-        give_sign(0, 1)
         quantise_wo(0)
+        weigh(0, 0)
+        quantise_z(0, 0)
+        weigh(0, 1)
         quantise_z(0, 1)
         paired_surplus(1, 0)
         paired_surplus(1, 1)

@@ -63,8 +63,9 @@ def tile_list_two_sided_match_kernel(
         at_wo1 = at_v2_1 + 4 * T2
         at_listed0 = at_wo1 + 4 * PACK * N - LAP
         at_vs = at_listed0 + 4 * S
+        at_v2s = at_vs + T
 
-        v2_tab_s = keep.tile([P, T2 // 4], I32, name="v2_tab_s", align_bytes=64)
+        v2_tab_s = staged([P, T2 // 4], I32, "v2_tab_s", at_v2s)
         v_tab_s = staged([P, T // 4], I32, "v_tab_s", at_vs)
         warm = staged([P, LAP], F32, "warm", at_warm)
         nc.vector.memset(v2_tab_s[:], 0)
@@ -87,7 +88,7 @@ def tile_list_two_sided_match_kernel(
                 in_=tab_scales.bitcast(I32)[:, 4 * q : 4 * q + 4, :],
             )
         for q in range(QUADS):
-            queue = nc.gpsimd if q < 2 else nc.sync
+            queue = nc.gpsimd if q < 3 else nc.sync
             queue.dma_start(
                 out=v2_tab_s[32 * q + v2_row : 32 * q + v2_row + 8, :],
                 in_=tab2_scales.bitcast(I32)[:, 4 * q : 4 * q + 4, :],
@@ -110,11 +111,12 @@ def tile_list_two_sided_match_kernel(
                 )
 
         v_listed0 = staged([P, S], U32, "v_listed0", at_listed0)
-        v_listed1 = keep.tile([P, S], U32, name="v_listed1", align_bytes=64)
+        v_listed1 = [staged([P, PASS], U32, f"v_listed1_{b}", at_v2s + 4 * PASS * b) for b in range(i_passes)]
         v_c = [keep.tile([P, i_passes, PACK, P], U32, name=f"v_c{a}", align_bytes=64) for a in range(k_passes)]
         v_s_listed = keep.tile([P, S], U8, name="v_s_listed", align_bytes=64)
         v_s = keep.tile([P, i_passes, PACK, P], U8, name="v_s", align_bytes=64)
-        v2_c = [keep.tile([P, S2], U32, name=f"v2_c{a}", align_bytes=64) for a in range(k_passes)]
+        v2_c = {ah: keep.tile([P, BANK], U32, name=f"v2_c{ah[0]}_{ah[1]}", align_bytes=64) for ah in [(0, 0), (1, 0), (1, 1)]}
+        v2_c[0, 1] = staged([P, BANK], U32, "v2_c0_1", at_v2_1 + LAP)
         v2_s = keep.tile([P, S2], U8, name="v2_s", align_bytes=64)
 
         def order_v_words(ordered, listed, passes):
@@ -122,6 +124,9 @@ def tile_list_two_sided_match_kernel(
                 ordered.bitcast(I32).rearrange("p b t (g r) -> p b g t r", r=4),
                 listed.bitcast(I32).rearrange("p (b g r t) -> p b g t r", b=passes, r=4, t=PACK),
             )
+
+        def gather_v2_words(a, h):
+            nc.vector.tensor_copy(v2_c[a, h][:], v2_tab[a][:].bitcast(U32).indirect(idx2[:, h * cols : (h + 1) * cols]))
 
         nc.vector.tensor_copy(v_listed0[:], v_tab[0][:].bitcast(U32).indirect(idx[:]))
         nc.vector.tensor_copy(v_s_listed[:], v_tab_s[:].bitcast(U8).indirect(idx[:]))
@@ -144,14 +149,16 @@ def tile_list_two_sided_match_kernel(
             )
 
         nc.vector.tensor_copy(v2_s[:], v2_tab_s[:].bitcast(U8).indirect(idx2[:]))
-        nc.vector.tensor_copy(v2_c[0][:], v2_tab[0][:].bitcast(U32).indirect(idx2[:]))
-        nc.vector.tensor_copy(v_listed1[:], v_tab[1][:].bitcast(U32).indirect(idx[:]))
-        order_v_words(v_c[1][:], v_listed1[:], i_passes)
-        for h in range(j_chunks):
+        gather_v2_words(0, 0)
+        for b in range(i_passes):
             nc.vector.tensor_copy(
-                v2_c[1][:, BANK * h : BANK * (h + 1)],
-                v2_tab[1][:].bitcast(U32).indirect(idx2[:, h * cols : (h + 1) * cols]),
+                v_listed1[b][:], v_tab[1][:].bitcast(U32).indirect(idx[:, b * cols : (b + 1) * cols])
             )
+        for b in range(i_passes):
+            order_v_words(v_c[1][:, b : b + 1], v_listed1[b][:], 1)
+        gather_v2_words(1, 0)
+        gather_v2_words(1, 1)
+        gather_v2_words(0, 1)
 
         z_c = {}
         z_s = {}
@@ -169,7 +176,7 @@ def tile_list_two_sided_match_kernel(
                 out=fit[h, b, t][:],
                 lhsT=v_c[a][:, b, t, :].bitcast(FP8X4),
                 lhsT_scale=v_s[v_row + 4 * a : P, b, t, :],
-                rhs=v2_c[a][:, BANK * h : BANK * (h + 1)].bitcast(FP8X4),
+                rhs=v2_c[a, h][:].bitcast(FP8X4),
                 rhs_scale=v2_s[v2_row + 4 * a : P, BANK * h : BANK * (h + 1)],
                 start=(a == 0),
                 stop=(a == k_passes - 1),
@@ -269,10 +276,10 @@ def tile_list_two_sided_match_kernel(
                 fit_pass(0, b, t, 0)
         surplus(0, 0)
         surplus(0, 1)
-        round_wo(0)
-        quantise_wo(0)
         weigh(0, 0)
+        round_wo(0)
         quantise_z(0, 0)
+        quantise_wo(0)
         weigh(0, 1)
         quantise_z(0, 1)
         paired_surplus(1, 0)

@@ -23,6 +23,9 @@ QUADS = 4
 BANK = 512
 RUN = 4
 LIST_ROWS = 16
+INTEREST_BANK = [[0, 1, 2, 3], [0, 2, 4, 5]]
+OFFER_BANK = [[4, 5, 6, 7], [1, 3, 6, 7]]
+GPSIMD_LOADS = 4
 
 
 def tile_list_two_sided_match_kernel(
@@ -39,7 +42,7 @@ def tile_list_two_sided_match_kernel(
         keep = ctx.enter_context(tc.tile_pool(name="keep", bufs=1))
         stage = ctx.enter_context(tc.tile_pool(name="stage", bufs=1))
         ring = ctx.enter_context(tc.tile_pool(name="ring", bufs=3))
-        psum = ctx.enter_context(tc.psum_pool(name="psum", bufs=8))
+        psum = ctx.enter_context(tc.psum_pool(name="psum", bufs=1))
 
         def staged(shape, dtype, name, offset):
             return stage.tile(shape, dtype, name=name, align_bytes=64, offset=offset)
@@ -52,25 +55,28 @@ def tile_list_two_sided_match_kernel(
         neg_res = keep.tile([P, i_passes, PACK], F32, name="neg_res")
 
         LAP = 64
-        at_v2_0 = 0
-        at_res = at_v2_0 + 4 * T2
+        at_v2_1 = 0
+        at_v0 = at_v2_1 + 4 * T2 - LAP
+        at_vs_listed = at_v0 + LAP
+        at_res = at_vs_listed + S
         at_wt = at_res + LAP
-        at_v1 = at_wt + LAP
-        at_warm = at_res - LAP
+        at_v1 = at_v0 + 4 * T - LAP
         at_wo0 = at_v1 + 4 * T
-        at_v0 = at_wo0 + 4 * PACK * N - LAP
-        at_v2_1 = at_v0 + 4 * T - LAP
-        at_wo1 = at_v2_1 + 4 * T2
-        at_listed0 = at_wo1 + 4 * PACK * N - LAP
-        at_vs = at_listed0 + 4 * S
-        at_v2s = at_vs + T
+        at_listed0 = at_wo0 + 4 * PACK * N - LAP
+        at_wi = at_listed0 + LAP
+        at_wo1 = at_listed0 + 4 * S - LAP
+        at_warm = at_wo1 + 4 * PACK * N
+        at_v2_0 = at_warm
+        at_v2s = at_v2_0 + 4 * T2
+        at_vs = at_v2s + T2
+        at_v2s_listed = at_vs + T // 2
 
         v2_tab_s = staged([P, T2 // 4], I32, "v2_tab_s", at_v2s)
         v_tab_s = staged([P, T // 4], I32, "v_tab_s", at_vs)
-        warm = staged([P, LAP], F32, "warm", at_warm)
+        warm = staged([P, 16], F32, "warm", at_warm)
         nc.vector.memset(v2_tab_s[:], 0)
-        nc.vector.memset(warm[:], 0.0)
         nc.vector.memset(v_tab_s[:], 0)
+        nc.vector.memset(warm[:], 0.0)
 
         v_tab = [staged([P, T], I32, f"v_tab{a}", at) for a, at in enumerate([at_v0, at_v1])]
         v2_tab = [staged([P, T2], I32, f"v2_tab{a}", at) for a, at in enumerate([at_v2_0, at_v2_1])]
@@ -88,16 +94,53 @@ def tile_list_two_sided_match_kernel(
                 in_=tab_scales.bitcast(I32)[:, 4 * q : 4 * q + 4, :],
             )
         for q in range(QUADS):
-            queue = nc.gpsimd if q < 3 else nc.sync
+            queue = nc.gpsimd if q < GPSIMD_LOADS else nc.sync
             queue.dma_start(
                 out=v2_tab_s[32 * q + v2_row : 32 * q + v2_row + 8, :],
                 in_=tab2_scales.bitcast(I32)[:, 4 * q : 4 * q + 4, :],
             )
         nc.scalar.activation(warm[:, 0:1], warm[:, 1:2], ACT.Sigmoid)
+        nc.sync.dma_start(out=v2_tab[0][:], in_=words(tab2_words, 0))
+
+        v_listed0 = [staged([P, PASS], U32, f"v_listed0_{b}", at_listed0 + 4 * PASS * b) for b in range(i_passes)]
+        v_listed1 = [staged([P, PASS], U32, f"v_listed1_{b}", at) for b, at in enumerate([at_v2s, at_v2s + 4 * PASS])]
+        v_listed = [v_listed0, v_listed1]
+        v_c = [
+            [keep.tile([P, PACK, P], U32, name=f"v_c{a}_{b}", align_bytes=64) for b in range(i_passes)]
+            for a in range(k_passes)
+        ]
+        v_s_listed = [staged([P, PASS], U8, f"v_s_listed{b}", at_vs_listed + PASS * b) for b in range(i_passes)]
+        v_s = [keep.tile([P, PACK, P], U8, name=f"v_s{b}", align_bytes=64) for b in range(i_passes)]
+        v2_c = {ah: keep.tile([P, BANK], U32, name=f"v2_c{ah[0]}_{ah[1]}", align_bytes=64) for ah in [(0, 0), (1, 0), (1, 1)]}
+        v2_c[0, 1] = staged([P, BANK], U32, "v2_c0_1", at_v2_1 + LAP)
+        v2_s = staged([P, S2], U8, "v2_s", at_v2s_listed)
+
+        def gather_v_words(a, b):
+            nc.vector.tensor_copy(
+                v_listed[a][b][:], v_tab[a][:].bitcast(U32).indirect(idx[:, b * cols : (b + 1) * cols])
+            )
+
+        def order_v_words(a, b):
+            nc.vector.tensor_copy(
+                v_c[a][b][:].bitcast(I32).rearrange("p t (g r) -> p g t r", r=4),
+                v_listed[a][b][:].bitcast(I32).rearrange("p (g r t) -> p g t r", r=4, t=PACK),
+            )
+
+        def gather_v_scales(b):
+            nc.vector.tensor_copy(v_s_listed[b][:], v_tab_s[:].bitcast(U8).indirect(idx[:, b * cols : (b + 1) * cols]))
+
+        def order_v_scales(b):
+            nc.vector.tensor_copy(v_s[b][:], v_s_listed[b][:].rearrange("p (m t) -> p t m", t=PACK))
+
+        def gather_v2_words(a, h):
+            nc.vector.tensor_copy(v2_c[a, h][:], v2_tab[a][:].bitcast(U32).indirect(idx2[:, h * cols : (h + 1) * cols]))
+
+        gather_v_words(0, 0)
+        gather_v_words(0, 1)
+        nc.sync.dma_start(out=v_tab[1][:], in_=words(tab_words, 1))
+        nc.sync.dma_start(out=v2_tab[1][:], in_=words(tab2_words, 1))
         nc.sync.dma_start(out=res_t[:], in_=res.rearrange("(b p t) -> p b t", p=P, t=PACK))
         nc.sync.dma_start(out=wt_t[:], in_=wt.rearrange("(b p t) -> p b t", p=P, t=PACK))
-        nc.sync.dma_start(out=v2_tab[0][:], in_=words(tab2_words, 0))
-        nc.sync.dma_start(out=v_tab[1][:], in_=words(tab_words, 1))
         nc.scalar.mul(neg_res[:], res_t[:], -1.0)
         wt_size = keep.tile([P, i_passes, PACK], F32, name="wt_size")
         wt_sign = keep.tile([P, i_passes, PACK], BF16, name="wt_sign")
@@ -109,38 +152,20 @@ def tile_list_two_sided_match_kernel(
                 nc.scalar.activation(
                     neg_level[:, b, t : t + 1], neg_res[:, b, t : t + 1], ACT.Copy, scale=wt_size[:, b, t : t + 1]
                 )
+        order_v_words(0, 0)
+        gather_v_scales(0)
+        order_v_words(0, 1)
+        gather_v_scales(1)
+        order_v_scales(0)
 
-        v_listed0 = staged([P, S], U32, "v_listed0", at_listed0)
-        v_listed1 = [staged([P, PASS], U32, f"v_listed1_{b}", at_v2s + 4 * PASS * b) for b in range(i_passes)]
-        v_c = [keep.tile([P, i_passes, PACK, P], U32, name=f"v_c{a}", align_bytes=64) for a in range(k_passes)]
-        v_s_listed = keep.tile([P, S], U8, name="v_s_listed", align_bytes=64)
-        v_s = keep.tile([P, i_passes, PACK, P], U8, name="v_s", align_bytes=64)
-        v2_c = {ah: keep.tile([P, BANK], U32, name=f"v2_c{ah[0]}_{ah[1]}", align_bytes=64) for ah in [(0, 0), (1, 0), (1, 1)]}
-        v2_c[0, 1] = staged([P, BANK], U32, "v2_c0_1", at_v2_1 + LAP)
-        v2_s = keep.tile([P, S2], U8, name="v2_s", align_bytes=64)
-
-        def order_v_words(ordered, listed, passes):
-            nc.vector.tensor_copy(
-                ordered.bitcast(I32).rearrange("p b t (g r) -> p b g t r", r=4),
-                listed.bitcast(I32).rearrange("p (b g r t) -> p b g t r", b=passes, r=4, t=PACK),
-            )
-
-        def gather_v2_words(a, h):
-            nc.vector.tensor_copy(v2_c[a, h][:], v2_tab[a][:].bitcast(U32).indirect(idx2[:, h * cols : (h + 1) * cols]))
-
-        nc.vector.tensor_copy(v_listed0[:], v_tab[0][:].bitcast(U32).indirect(idx[:]))
-        nc.vector.tensor_copy(v_s_listed[:], v_tab_s[:].bitcast(U8).indirect(idx[:]))
-        order_v_words(v_c[0][:], v_listed0[:], i_passes)
-        nc.vector.tensor_copy(v_s[:], v_s_listed[:].rearrange("p (b m t) -> p b t m", b=i_passes, t=PACK))
-
-        nc.sync.dma_start(out=v2_tab[1][:], in_=words(tab2_words, 1))
         for b in range(i_passes):
             nc.sync.dma_start(
                 out=wo_raw[b][:], in_=wo[b * PASS : (b + 1) * PASS, :].rearrange("(p t) n -> p t n", t=PACK)
             )
-        wi_c = staged([P, i_passes, N // 2], I32, "wi_c", at_listed0 + LAP)
+        wi_c = staged([P, i_passes, N // 2], I32, "wi_c", at_wi)
         wi_s = staged([P, i_passes, N // 4], I32, "wi_s", at_vs)
         nc.sync.dma_start(out=wi_c[:], in_=wi_words.bitcast(I32).rearrange("b p w -> p b w"))
+        nc.vector.tensor_copy(v2_s[:], v2_tab_s[:].bitcast(U8).indirect(idx2[:]))
         nc.vector.memset(wi_s[:], 0)
         for q in range(QUADS):
             nc.sync.dma_start(
@@ -148,14 +173,12 @@ def tile_list_two_sided_match_kernel(
                 in_=wi_scales.bitcast(I32)[:, 4 * q : 4 * q + 4, :].rearrange("b r w -> r b w"),
             )
 
-        nc.vector.tensor_copy(v2_s[:], v2_tab_s[:].bitcast(U8).indirect(idx2[:]))
+        order_v_scales(1)
         gather_v2_words(0, 0)
-        for b in range(i_passes):
-            nc.vector.tensor_copy(
-                v_listed1[b][:], v_tab[1][:].bitcast(U32).indirect(idx[:, b * cols : (b + 1) * cols])
-            )
-        for b in range(i_passes):
-            order_v_words(v_c[1][:, b : b + 1], v_listed1[b][:], 1)
+        gather_v_words(1, 0)
+        gather_v_words(1, 1)
+        order_v_words(1, 0)
+        order_v_words(1, 1)
         gather_v2_words(1, 0)
         gather_v2_words(1, 1)
         gather_v2_words(0, 1)
@@ -171,11 +194,11 @@ def tile_list_two_sided_match_kernel(
 
         def fit_pass(h, b, t, a):
             if a == 0:
-                fit[h, b, t] = psum.tile([P, BANK], F32, name="bank")
+                fit[h, b, t] = psum.tile([P, BANK], F32, name=f"bank{PACK * b + t}")
             nc.tensor.matmul_mx(
                 out=fit[h, b, t][:],
-                lhsT=v_c[a][:, b, t, :].bitcast(FP8X4),
-                lhsT_scale=v_s[v_row + 4 * a : P, b, t, :],
+                lhsT=v_c[a][b][:, t, :].bitcast(FP8X4),
+                lhsT_scale=v_s[b][v_row + 4 * a : P, t, :],
                 rhs=v2_c[a, h][:].bitcast(FP8X4),
                 rhs_scale=v2_s[v2_row + 4 * a : P, BANK * h : BANK * (h + 1)],
                 start=(a == 0),
@@ -200,7 +223,7 @@ def tile_list_two_sided_match_kernel(
         def paired_surplus(h, b):
             above[h, b] = keep.tile([P, 2, BANK, 2], BF16, name=f"above{h}_{b}", align_bytes=64)
             for t in range(PACK):
-                for a in range(k_passes):
+                for a in range(1 - h, k_passes):
                     fit_pass(h, b, t, a)
                 nc.scalar.activation(
                     above[h, b][:, t // 2, :, t % 2],
@@ -238,7 +261,7 @@ def tile_list_two_sided_match_kernel(
 
         def interest_pass(h, n, b):
             if b == 0:
-                score["interest", h, n] = psum.tile([P, BANK], F32, name="bank")
+                score["interest", h, n] = psum.tile([P, BANK], F32, name=f"bank{INTEREST_BANK[h][n]}")
             nc.tensor.matmul_mx(
                 out=score["interest", h, n][:],
                 lhsT=wi_c[:, b, :].bitcast(U8)[:, 2 * P * n : 2 * P * (n + 1)].bitcast(FP4X4),
@@ -253,18 +276,18 @@ def tile_list_two_sided_match_kernel(
             chance[h, n] = keep.tile([P, BANK], F32, name=f"chance{h}_{n}")
             nc.scalar.activation(chance[h, n][:], score["interest", h, n][:], ACT.Sigmoid)
 
-        def offer_passes(h, n):
-            score["offer", h, n] = psum.tile([P, BANK], F32, name="bank")
-            for b in range(i_passes):
-                nc.tensor.matmul_mx(
-                    out=score["offer", h, n][:],
-                    lhsT=wo_c[b][:, P * n : P * (n + 1)].bitcast(FP8X4),
-                    lhsT_scale=wo_s[b][:, P * n : P * (n + 1)],
-                    rhs=z_c[h, b][:].bitcast(FP8X4),
-                    rhs_scale=z_s[h, b][:],
-                    start=(b == 0),
-                    stop=(b == i_passes - 1),
-                )
+        def offer_pass(h, n, b, first):
+            if b == first:
+                score["offer", h, n] = psum.tile([P, BANK], F32, name=f"bank{OFFER_BANK[h][n]}")
+            nc.tensor.matmul_mx(
+                out=score["offer", h, n][:],
+                lhsT=wo_c[b][:, P * n : P * (n + 1)].bitcast(FP8X4),
+                lhsT_scale=wo_s[b][:, P * n : P * (n + 1)],
+                rhs=z_c[h, b][:].bitcast(FP8X4),
+                rhs_scale=z_s[h, b][:],
+                start=(b == first),
+                stop=(b != first),
+            )
 
         def finish(h, n):
             result = keep.tile([P, BANK], F32, name=f"result{h}_{n}")
@@ -274,34 +297,46 @@ def tile_list_two_sided_match_kernel(
         for b in range(i_passes):
             for t in range(PACK):
                 fit_pass(0, b, t, 0)
-        surplus(0, 0)
+        paired_surplus(0, 0)
         surplus(0, 1)
-        weigh(0, 0)
         round_wo(0)
-        quantise_z(0, 0)
+        give_sign(0, 0)
         quantise_wo(0)
+        quantise_z(0, 0)
         weigh(0, 1)
-        quantise_z(0, 1)
         paired_surplus(1, 0)
+        round_wo(1)
+        quantise_z(0, 1)
         paired_surplus(1, 1)
         for b in range(i_passes):
             for n in range(n_tiles):
                 interest_pass(0, n, b)
-        round_wo(1)
         give_sign(1, 0)
         quantise_wo(1)
         quantise_z(1, 0)
+        for n in range(n_tiles):
+            for b in reversed(range(i_passes)):
+                offer_pass(0, n, b, 1)
         give_sign(1, 1)
-        quantise_z(1, 1)
         for n in range(n_tiles):
             sigmoid(0, n)
-            offer_passes(0, n)
-        for b in range(i_passes):
-            for n in range(n_tiles):
-                interest_pass(1, n, b)
-        for n in range(n_tiles):
+        finish(0, 0)
+        quantise_z(1, 1)
+        for n in range(2):
+            interest_pass(1, n, 0)
+            offer_pass(1, n, 0, 0)
+        interest_pass(1, 2, 0)
+        for n in range(1, n_tiles):
             finish(0, n)
-            sigmoid(1, n)
-            offer_passes(1, n)
+        for n in range(2):
+            interest_pass(1, n, 1)
+            offer_pass(1, n, 1, 0)
+        interest_pass(1, 2, 1)
+        for b in range(i_passes):
+            interest_pass(1, 3, b)
+        for n in range(2, n_tiles):
+            for b in range(i_passes):
+                offer_pass(1, n, b, 0)
         for n in range(n_tiles):
+            sigmoid(1, n)
             finish(1, n)

@@ -25,7 +25,7 @@ RUN = 4
 LIST_ROWS = 16
 INTEREST_BANK = [[0, 1, 2, 3], [0, 2, 4, 5]]
 OFFER_BANK = [[4, 5, 6, 7], [1, 3, 6, 7]]
-GPSIMD_LOADS = 4
+GPSIMD_LOADS = 3
 
 
 def tile_list_two_sided_match_kernel(
@@ -41,7 +41,6 @@ def tile_list_two_sided_match_kernel(
     with ExitStack() as ctx:
         keep = ctx.enter_context(tc.tile_pool(name="keep", bufs=1))
         stage = ctx.enter_context(tc.tile_pool(name="stage", bufs=1))
-        ring = ctx.enter_context(tc.tile_pool(name="ring", bufs=3))
         psum = ctx.enter_context(tc.psum_pool(name="psum", bufs=1))
 
         def staged(shape, dtype, name, offset):
@@ -70,6 +69,11 @@ def tile_list_two_sided_match_kernel(
         at_v2s = at_v2_0 + 4 * T2
         at_vs = at_v2s + T2
         at_v2s_listed = at_vs + T // 2
+        at_result2 = at_vs + T
+        at_above = at_result2 + 4 * BANK - LAP
+        at_result0 = at_above + LAP
+        at_result1 = at_result0 + 4 * BANK
+        at_z = at_result1 + 4 * BANK
 
         v2_tab_s = staged([P, T2 // 4], I32, "v2_tab_s", at_v2s)
         v_tab_s = staged([P, T // 4], I32, "v_tab_s", at_vs)
@@ -111,8 +115,7 @@ def tile_list_two_sided_match_kernel(
         ]
         v_s_listed = [staged([P, PASS], U8, f"v_s_listed{b}", at_vs_listed + PASS * b) for b in range(i_passes)]
         v_s = [keep.tile([P, PACK, P], U8, name=f"v_s{b}", align_bytes=64) for b in range(i_passes)]
-        v2_c = {ah: keep.tile([P, BANK], U32, name=f"v2_c{ah[0]}_{ah[1]}", align_bytes=64) for ah in [(0, 0), (1, 0), (1, 1)]}
-        v2_c[0, 1] = staged([P, BANK], U32, "v2_c0_1", at_v2_1 + LAP)
+        v2_c = {ah: keep.tile([P, BANK], U32, name=f"v2_c{ah[0]}_{ah[1]}", align_bytes=64) for ah in [(0, 0), (0, 1), (1, 0), (1, 1)]}
         v2_s = staged([P, S2], U8, "v2_s", at_v2s_listed)
 
         def gather_v_words(a, b):
@@ -147,11 +150,7 @@ def tile_list_two_sided_match_kernel(
         neg_level = keep.tile([P, i_passes, PACK], F32, name="neg_level")
         nc.scalar.activation(wt_size[:], wt_t[:], ACT.Abs)
         nc.scalar.activation(wt_sign[:], wt_t[:], ACT.Sign)
-        for b in range(i_passes):
-            for t in range(PACK):
-                nc.scalar.activation(
-                    neg_level[:, b, t : t + 1], neg_res[:, b, t : t + 1], ACT.Copy, scale=wt_size[:, b, t : t + 1]
-                )
+        nc.gpsimd.tensor_tensor(neg_level[:], neg_res[:], wt_size[:], MULT)
         order_v_words(0, 0)
         gather_v_scales(0)
         order_v_words(0, 1)
@@ -174,6 +173,7 @@ def tile_list_two_sided_match_kernel(
             )
 
         order_v_scales(1)
+        gather_v2_words(0, 1)
         gather_v2_words(0, 0)
         gather_v_words(1, 0)
         gather_v_words(1, 1)
@@ -181,7 +181,6 @@ def tile_list_two_sided_match_kernel(
         order_v_words(1, 1)
         gather_v2_words(1, 0)
         gather_v2_words(1, 1)
-        gather_v2_words(0, 1)
 
         z_c = {}
         z_s = {}
@@ -212,7 +211,7 @@ def tile_list_two_sided_match_kernel(
                 nc.scalar.activation(above[h, b][:, t, :], fit[h, b, t][:], ACT.Relu, bias=neg_res[:, b, t : t + 1])
 
         def weigh(h, b):
-            z_bf[h, b] = ring.tile([P, BANK * PACK], BF16, name="z_bf", align_bytes=64)
+            z_bf[h, b] = keep.tile([P, BANK * PACK], BF16, name=f"z_bf{h}" if h else f"z_bf{h}_{b}", align_bytes=64)
             nc.vector.tensor_tensor(
                 z_bf[h, b][:].rearrange("p (c r t) -> p c t r", r=RUN, t=PACK),
                 above[h, b][:].rearrange("p t (c r) -> p c t r", r=RUN),
@@ -221,7 +220,10 @@ def tile_list_two_sided_match_kernel(
             )
 
         def paired_surplus(h, b):
-            above[h, b] = keep.tile([P, 2, BANK, 2], BF16, name=f"above{h}_{b}", align_bytes=64)
+            if (h, b) == (1, 1):
+                above[h, b] = staged([P, 2, BANK, 2], BF16, "above_last", at_above)
+            else:
+                above[h, b] = keep.tile([P, 2, BANK, 2], BF16, name=f"above{h}_{b}", align_bytes=64)
             for t in range(PACK):
                 for a in range(1 - h, k_passes):
                     fit_pass(h, b, t, a)
@@ -234,7 +236,10 @@ def tile_list_two_sided_match_kernel(
                 )
 
         def give_sign(h, b):
-            z_bf[h, b] = ring.tile([P, BANK * PACK], BF16, name="z_bf", align_bytes=64)
+            if h:
+                z_bf[h, b] = staged([P, BANK * PACK], BF16, f"z_bf{h}_{b}", at_z)
+            else:
+                z_bf[h, b] = keep.tile([P, BANK * PACK], BF16, name=f"z_bf{h}_{b}", align_bytes=64)
             nc.vector.tensor_tensor(
                 z_bf[h, b][:].rearrange("p (c u e) -> p c u e", u=2, e=2),
                 above[h, b][:].rearrange("p u c e -> p c u e"),
@@ -290,50 +295,51 @@ def tile_list_two_sided_match_kernel(
             )
 
         def finish(h, n):
-            result = keep.tile([P, BANK], F32, name=f"result{h}_{n}")
+            if h:
+                result = keep.tile([P, BANK], F32, name=f"result{h}_{n}")
+            else:
+                result = staged([P, BANK], F32, f"result{h}_{n}", [at_result0, at_result1, at_result2, at_z][n])
             nc.vector.tensor_tensor(result[:], score["offer", h, n][:], chance[h, n][:], MULT)
             nc.sync.dma_start(out=out[P * n : P * (n + 1), BANK * h : BANK * (h + 1)], in_=result[:])
 
         for b in range(i_passes):
             for t in range(PACK):
                 fit_pass(0, b, t, 0)
-        paired_surplus(0, 0)
-        surplus(0, 1)
+        surplus(0, 0)
+        paired_surplus(0, 1)
         round_wo(0)
-        give_sign(0, 0)
+        weigh(0, 0)
         quantise_wo(0)
         quantise_z(0, 0)
-        weigh(0, 1)
+        give_sign(0, 1)
         paired_surplus(1, 0)
         round_wo(1)
         quantise_z(0, 1)
+        quantise_wo(1)
         paired_surplus(1, 1)
         for b in range(i_passes):
             for n in range(n_tiles):
                 interest_pass(0, n, b)
-        give_sign(1, 0)
-        quantise_wo(1)
-        quantise_z(1, 0)
         for n in range(n_tiles):
             for b in reversed(range(i_passes)):
                 offer_pass(0, n, b, 1)
+        give_sign(1, 0)
+        quantise_z(1, 0)
         give_sign(1, 1)
         for n in range(n_tiles):
             sigmoid(0, n)
-        finish(0, 0)
         quantise_z(1, 1)
         for n in range(2):
             interest_pass(1, n, 0)
             offer_pass(1, n, 0, 0)
-        interest_pass(1, 2, 0)
-        for n in range(1, n_tiles):
+        for n in range(n_tiles):
             finish(0, n)
         for n in range(2):
             interest_pass(1, n, 1)
             offer_pass(1, n, 1, 0)
-        interest_pass(1, 2, 1)
-        for b in range(i_passes):
-            interest_pass(1, 3, b)
+        for n in range(2, n_tiles):
+            for b in range(i_passes):
+                interest_pass(1, n, b)
         for n in range(2, n_tiles):
             for b in range(i_passes):
                 offer_pass(1, n, b, 0)

@@ -85,8 +85,8 @@ def tile_list_two_sided_match_kernel(
         v_tab = [staged([P, T], I32, f"v_tab{a}", at) for a, at in enumerate([at_v0, at_v1])]
         v2_tab = [staged([P, T2], I32, f"v2_tab{a}", at) for a, at in enumerate([at_v2_0, at_v2_1])]
         wo_raw = [staged([P, PACK, N], F32, f"wo_raw{b}", at) for b, at in enumerate([at_wo0, at_wo1])]
-        res_t = staged([P, i_passes, PACK], F32, "res_t", at_res)
-        wt_t = staged([P, i_passes, PACK], F32, "wt_t", at_wt)
+        res_t = staged([P, i_passes, 2 * PACK], F32, "res_t", at_res)
+        wt_t = staged([P, i_passes, 2 * PACK], F32, "wt_t", at_wt)
 
         v_row, v2_row = 0, 8
         nc.sync.dma_start(out=v_tab[0][:], in_=words(tab_words, 0))
@@ -142,15 +142,14 @@ def tile_list_two_sided_match_kernel(
         gather_v_words(0, 1)
         nc.sync.dma_start(out=v_tab[1][:], in_=words(tab_words, 1))
         nc.sync.dma_start(out=v2_tab[1][:], in_=words(tab2_words, 1))
-        nc.sync.dma_start(out=res_t[:], in_=res.rearrange("(b p t) -> p b t", p=P, t=PACK))
-        nc.sync.dma_start(out=wt_t[:], in_=wt.rearrange("(b p t) -> p b t", p=P, t=PACK))
-        nc.scalar.mul(neg_res[:], res_t[:], -1.0)
+        nc.sync.dma_start(out=res_t[:, :, 0:PACK], in_=res.rearrange("(b p t) -> p b t", p=P, t=PACK))
+        nc.sync.dma_start(out=wt_t[:, :, 0:PACK], in_=wt.rearrange("(b p t) -> p b t", p=P, t=PACK))
+        nc.scalar.mul(neg_res[:], res_t[:, :, 0:PACK], -1.0)
         wt_size = keep.tile([P, i_passes, PACK], F32, name="wt_size")
         wt_sign = keep.tile([P, i_passes, PACK], BF16, name="wt_sign")
         neg_level = keep.tile([P, i_passes, PACK], F32, name="neg_level")
-        nc.scalar.activation(wt_size[:], wt_t[:], ACT.Abs)
-        nc.scalar.activation(wt_sign[:], wt_t[:], ACT.Sign)
-        nc.gpsimd.tensor_tensor(neg_level[:], neg_res[:], wt_size[:], MULT)
+        nc.scalar.activation(wt_size[:], wt_t[:, :, 0:PACK], ACT.Abs)
+        nc.scalar.activation(wt_sign[:], wt_t[:, :, 0:PACK], ACT.Sign)
         order_v_words(0, 0)
         gather_v_scales(0)
         order_v_words(0, 1)
@@ -181,6 +180,7 @@ def tile_list_two_sided_match_kernel(
         order_v_words(1, 1)
         gather_v2_words(1, 0)
         gather_v2_words(1, 1)
+        nc.vector.tensor_tensor(neg_level[:], neg_res[:], wt_size[:], MULT)
 
         z_c = {}
         z_s = {}
@@ -207,15 +207,19 @@ def tile_list_two_sided_match_kernel(
         def surplus(h, b):
             above[h, b] = keep.tile([P, PACK, BANK], F32, name=f"above{h}_{b}", align_bytes=64)
             for t in range(PACK):
-                fit_pass(h, b, t, 1)
+                for a in range(1 - h, k_passes):
+                    fit_pass(h, b, t, a)
                 nc.scalar.activation(above[h, b][:, t, :], fit[h, b, t][:], ACT.Relu, bias=neg_res[:, b, t : t + 1])
 
         def weigh(h, b):
-            z_bf[h, b] = keep.tile([P, BANK * PACK], BF16, name=f"z_bf{h}" if h else f"z_bf{h}_{b}", align_bytes=64)
+            if h:
+                z_bf[h, b] = staged([P, BANK * PACK], BF16, f"z_bf{h}_{b}", at_z)
+            else:
+                z_bf[h, b] = keep.tile([P, BANK * PACK], BF16, name=f"z_bf{h}_{b}", align_bytes=64)
             nc.vector.tensor_tensor(
                 z_bf[h, b][:].rearrange("p (c r t) -> p c t r", r=RUN, t=PACK),
                 above[h, b][:].rearrange("p t (c r) -> p c t r", r=RUN),
-                wt_t[:, b, :].unsqueeze(1).unsqueeze(3).to_broadcast([P, BANK // RUN, PACK, RUN]),
+                wt_t[:, b, 0:PACK].unsqueeze(1).unsqueeze(3).to_broadcast([P, BANK // RUN, PACK, RUN]),
                 MULT,
             )
 
@@ -312,7 +316,7 @@ def tile_list_two_sided_match_kernel(
         quantise_wo(0)
         quantise_z(0, 0)
         give_sign(0, 1)
-        paired_surplus(1, 0)
+        surplus(1, 0)
         round_wo(1)
         quantise_z(0, 1)
         quantise_wo(1)
@@ -323,7 +327,7 @@ def tile_list_two_sided_match_kernel(
         for n in range(n_tiles):
             for b in reversed(range(i_passes)):
                 offer_pass(0, n, b, 1)
-        give_sign(1, 0)
+        weigh(1, 0)
         quantise_z(1, 0)
         give_sign(1, 1)
         for n in range(n_tiles):

@@ -25,7 +25,6 @@ RUN = 4
 LIST_ROWS = 16
 INTEREST_BANK = [[0, 1, 2, 3], [0, 2, 4, 5]]
 OFFER_BANK = [[4, 5, 6, 7], [1, 3, 6, 7]]
-GPSIMD_LOADS = 3
 
 
 def tile_list_two_sided_match_kernel(
@@ -54,69 +53,65 @@ def tile_list_two_sided_match_kernel(
         neg_res = keep.tile([P, i_passes, PACK], F32, name="neg_res")
 
         LAP = 64
-        at_v2_1 = 0
-        at_v0 = at_v2_1 + 4 * T2 - LAP
-        at_vs_listed = at_v0 + LAP
-        at_res = at_vs_listed + S
-        at_wt = at_res + LAP
-        at_v1 = at_v0 + 4 * T - LAP
-        at_wo0 = at_v1 + 4 * T
-        at_listed0 = at_wo0 + 4 * PACK * N - LAP
-        at_wi = at_listed0 + LAP
-        at_wo1 = at_listed0 + 4 * S - LAP
-        at_warm = at_wo1 + 4 * PACK * N
-        at_v2_0 = at_warm
-        at_v2s = at_v2_0 + 4 * T2
-        at_vs = at_v2s + T2
-        at_v2s_listed = at_vs + T // 2
-        at_result2 = at_vs + T
+        at_vs = 0
+        at_v0 = at_vs + T
+        at_wt = at_v0 + LAP
+        at_wo0 = at_v0 + 4 * T - LAP
+        at_v2_1 = at_wo0 + 4 * PACK * N
+        at_v2s = at_v2_1 + 4 * T2 - LAP
+        at_res = at_v2s + LAP
+        at_listed0_1 = at_res + LAP
+        at_wi_s = at_listed0_1
+        at_wi = at_wi_s + i_passes * N
+        at_v2_0 = at_v2s + T2
+        at_vs_listed = at_v2_0 + 4 * T2
+        at_v1 = at_vs_listed + S - LAP
+        at_listed0_0 = at_v1 + 4 * T
+        at_wo1 = at_listed0_0 + 4 * PASS - LAP
+        at_result2 = at_wo1 + 4 * PACK * N
         at_above = at_result2 + 4 * BANK - LAP
         at_result0 = at_above + LAP
         at_result1 = at_result0 + 4 * BANK
         at_z = at_result1 + 4 * BANK
 
-        v2_tab_s = staged([P, T2 // 4], I32, "v2_tab_s", at_v2s)
         v_tab_s = staged([P, T // 4], I32, "v_tab_s", at_vs)
-        warm = staged([P, 16], F32, "warm", at_warm)
+        v2_tab_s = staged([P, T2 // 4], I32, "v2_tab_s", at_v2s)
+        warm = staged([P, 16], F32, "warm", at_v2_0)
         nc.vector.memset(v2_tab_s[:], 0)
-        nc.vector.memset(v_tab_s[:], 0)
         nc.vector.memset(warm[:], 0.0)
+        nc.vector.memset(v_tab_s[32:64, :], 0)
+        nc.vector.memset(v_tab_s[64:P, :], 0)
+        nc.scalar.activation(warm[:, 0:1], warm[:, 1:2], ACT.Sigmoid)
 
         v_tab = [staged([P, T], I32, f"v_tab{a}", at) for a, at in enumerate([at_v0, at_v1])]
         v2_tab = [staged([P, T2], I32, f"v2_tab{a}", at) for a, at in enumerate([at_v2_0, at_v2_1])]
-        wo_raw = [staged([P, PACK, N], F32, f"wo_raw{b}", at) for b, at in enumerate([at_wo0, at_wo1])]
         res_t = staged([P, i_passes, 2 * PACK], F32, "res_t", at_res)
         wt_t = staged([P, i_passes, 2 * PACK], F32, "wt_t", at_wt)
 
-        v_row, v2_row = 0, 8
-        nc.sync.dma_start(out=v_tab[0][:], in_=words(tab_words, 0))
+        nc.sync.dma_start(out=v_tab_s[0:32, :], in_=tab_scales.bitcast(I32).rearrange("a q w -> (a q) w"))
         nc.sync.dma_start(out=idx[:], in_=offs)
+        nc.sync.dma_start(out=v_tab[0][:], in_=words(tab_words, 0))
         nc.sync.dma_start(out=idx2[:], in_=offs2)
-        for q in range(QUADS):
-            nc.sync.dma_start(
-                out=v_tab_s[32 * q + v_row : 32 * q + v_row + 8, :],
-                in_=tab_scales.bitcast(I32)[:, 4 * q : 4 * q + 4, :],
-            )
-        for q in range(QUADS):
-            queue = nc.gpsimd if q < GPSIMD_LOADS else nc.sync
-            queue.dma_start(
-                out=v2_tab_s[32 * q + v2_row : 32 * q + v2_row + 8, :],
-                in_=tab2_scales.bitcast(I32)[:, 4 * q : 4 * q + 4, :],
-            )
-        nc.scalar.activation(warm[:, 0:1], warm[:, 1:2], ACT.Sigmoid)
+        nc.sync.dma_start(out=v2_tab_s[0:P:4, :], in_=tab2_scales.bitcast(I32).rearrange("a q w -> (a q) w"))
         nc.sync.dma_start(out=v2_tab[0][:], in_=words(tab2_words, 0))
 
-        v_listed0 = [staged([P, PASS], U32, f"v_listed0_{b}", at_listed0 + 4 * PASS * b) for b in range(i_passes)]
-        v_listed1 = [staged([P, PASS], U32, f"v_listed1_{b}", at) for b, at in enumerate([at_v2s, at_v2s + 4 * PASS])]
-        v_listed = [v_listed0, v_listed1]
+        v_listed = [
+            [staged([P, PASS], U32, f"v_listed0_{b}", at) for b, at in enumerate([at_listed0_0, at_listed0_1])],
+            [keep.tile([P, PASS], U32, name=f"v_listed1_{b}", align_bytes=64) for b in range(i_passes)],
+        ]
         v_c = [
             [keep.tile([P, PACK, P], U32, name=f"v_c{a}_{b}", align_bytes=64) for b in range(i_passes)]
             for a in range(k_passes)
         ]
         v_s_listed = [staged([P, PASS], U8, f"v_s_listed{b}", at_vs_listed + PASS * b) for b in range(i_passes)]
-        v_s = [keep.tile([P, PACK, P], U8, name=f"v_s{b}", align_bytes=64) for b in range(i_passes)]
-        v2_c = {ah: keep.tile([P, BANK], U32, name=f"v2_c{ah[0]}_{ah[1]}", align_bytes=64) for ah in [(0, 0), (0, 1), (1, 0), (1, 1)]}
-        v2_s = staged([P, S2], U8, "v2_s", at_v2s_listed)
+        v_s = [keep.tile([P, S], U8, name="v_s0", align_bytes=64), keep.tile([P, S], U8, name="v_s1", align_bytes=64)]
+        v2_c = {
+            (a, h): keep.tile([P, BANK], U32, name=f"v2_c{a}_{h}", align_bytes=64)
+            for a in range(k_passes)
+            for h in range(j_chunks)
+        }
+        v2_s_listed = keep.tile([P, S2], U8, name="v2_s_listed", align_bytes=64)
+        v2_s = [staged([P, S2], U8, f"v2_s{a}", at_vs + S2 * a) for a in range(k_passes)]
 
         def gather_v_words(a, b):
             nc.vector.tensor_copy(
@@ -133,45 +128,69 @@ def tile_list_two_sided_match_kernel(
             nc.vector.tensor_copy(v_s_listed[b][:], v_tab_s[:].bitcast(U8).indirect(idx[:, b * cols : (b + 1) * cols]))
 
         def order_v_scales(b):
-            nc.vector.tensor_copy(v_s[b][:], v_s_listed[b][:].rearrange("p (m t) -> p t m", t=PACK))
+            nc.vector.tensor_copy(
+                v_s[0][:, PASS * b : PASS * (b + 1)].rearrange("p (t m) -> p t m", t=PACK),
+                v_s_listed[b][:].rearrange("p (m t) -> p t m", t=PACK),
+            )
 
         def gather_v2_words(a, h):
             nc.vector.tensor_copy(v2_c[a, h][:], v2_tab[a][:].bitcast(U32).indirect(idx2[:, h * cols : (h + 1) * cols]))
 
-        gather_v_words(0, 0)
-        gather_v_words(0, 1)
+        def place_v2_scales(a):
+            for q in range(QUADS):
+                first = 4 * (16 * a + 4 * q)
+                nc.sync.dma_start(
+                    out=v2_s[a][:].bitcast(I32)[32 * q : 32 * q + 4, :],
+                    in_=v2_s_listed[:].bitcast(I32)[first : first + 16 : 4, :],
+                )
+
+        def place_v_scales(a, q):
+            first = 16 * a + 4 * q
+            nc.sync.dma_start(
+                out=v_s[a][:].bitcast(I32)[32 * q : 32 * q + 4, :], in_=v_s[0][:].bitcast(I32)[first : first + 4, :]
+            )
+
+        gather_v_scales(0)
+        gather_v_scales(1)
+        order_v_scales(0)
+        order_v_scales(1)
+        moves = [(a, q) for a in range(k_passes) for q in range(QUADS)][1:]
+        for a, q in moves[:-1]:
+            place_v_scales(a, q)
         nc.sync.dma_start(out=v_tab[1][:], in_=words(tab_words, 1))
+        place_v_scales(*moves[-1])
+        nc.vector.tensor_copy(v2_s_listed[:], v2_tab_s[:].bitcast(U8).indirect(idx2[:]))
+        place_v2_scales(0)
         nc.sync.dma_start(out=v2_tab[1][:], in_=words(tab2_words, 1))
         nc.sync.dma_start(out=res_t[:, :, 0:PACK], in_=res.rearrange("(b p t) -> p b t", p=P, t=PACK))
-        nc.sync.dma_start(out=wt_t[:, :, 0:PACK], in_=wt.rearrange("(b p t) -> p b t", p=P, t=PACK))
+        place_v2_scales(1)
         nc.scalar.mul(neg_res[:], res_t[:, :, 0:PACK], -1.0)
         wt_size = keep.tile([P, i_passes, PACK], F32, name="wt_size")
         wt_sign = keep.tile([P, i_passes, PACK], BF16, name="wt_sign")
         neg_level = keep.tile([P, i_passes, PACK], F32, name="neg_level")
-        nc.scalar.activation(wt_size[:], wt_t[:, :, 0:PACK], ACT.Abs)
-        nc.scalar.activation(wt_sign[:], wt_t[:, :, 0:PACK], ACT.Sign)
-        order_v_words(0, 0)
-        gather_v_scales(0)
-        order_v_words(0, 1)
-        gather_v_scales(1)
-        order_v_scales(0)
 
-        for b in range(i_passes):
+        gather_v_words(0, 0)
+        gather_v_words(0, 1)
+        order_v_words(0, 0)
+        order_v_words(0, 1)
+        wo_raw = [staged([P, PACK, N], F32, f"wo_raw{b}", at) for b, at in enumerate([at_wo0, at_wo1])]
+        wi_c = staged([P, i_passes, N // 2], I32, "wi_c", at_wi)
+        wi_s = staged([P, i_passes, N // 4], I32, "wi_s", at_wi_s)
+
+        def load_wo(b):
             nc.sync.dma_start(
                 out=wo_raw[b][:], in_=wo[b * PASS : (b + 1) * PASS, :].rearrange("(p t) n -> p t n", t=PACK)
             )
-        wi_c = staged([P, i_passes, N // 2], I32, "wi_c", at_wi)
-        wi_s = staged([P, i_passes, N // 4], I32, "wi_s", at_vs)
+
+        nc.sync.dma_start(out=wt_t[:, :, 0:PACK], in_=wt.rearrange("(b p t) -> p b t", p=P, t=PACK))
+        load_wo(0)
+        load_wo(1)
         nc.sync.dma_start(out=wi_c[:], in_=wi_words.bitcast(I32).rearrange("b p w -> p b w"))
-        nc.vector.tensor_copy(v2_s[:], v2_tab_s[:].bitcast(U8).indirect(idx2[:]))
-        nc.vector.memset(wi_s[:], 0)
         for q in range(QUADS):
             nc.sync.dma_start(
                 out=wi_s[32 * q : 32 * q + 4, :, :],
                 in_=wi_scales.bitcast(I32)[:, 4 * q : 4 * q + 4, :].rearrange("b r w -> r b w"),
             )
-
-        order_v_scales(1)
         gather_v2_words(0, 1)
         gather_v2_words(0, 0)
         gather_v_words(1, 0)
@@ -180,6 +199,8 @@ def tile_list_two_sided_match_kernel(
         order_v_words(1, 1)
         gather_v2_words(1, 0)
         gather_v2_words(1, 1)
+        nc.scalar.activation(wt_size[:], wt_t[:, :, 0:PACK], ACT.Abs)
+        nc.scalar.activation(wt_sign[:], wt_t[:, :, 0:PACK], ACT.Sign)
         nc.vector.tensor_tensor(neg_level[:], neg_res[:], wt_size[:], MULT)
 
         z_c = {}
@@ -197,9 +218,9 @@ def tile_list_two_sided_match_kernel(
             nc.tensor.matmul_mx(
                 out=fit[h, b, t][:],
                 lhsT=v_c[a][b][:, t, :].bitcast(FP8X4),
-                lhsT_scale=v_s[b][v_row + 4 * a : P, t, :],
+                lhsT_scale=v_s[a][:, PASS * b + P * t : PASS * b + P * (t + 1)],
                 rhs=v2_c[a, h][:].bitcast(FP8X4),
-                rhs_scale=v2_s[v2_row + 4 * a : P, BANK * h : BANK * (h + 1)],
+                rhs_scale=v2_s[a][:, BANK * h : BANK * (h + 1)],
                 start=(a == 0),
                 stop=(a == k_passes - 1),
             )
@@ -207,15 +228,11 @@ def tile_list_two_sided_match_kernel(
         def surplus(h, b):
             above[h, b] = keep.tile([P, PACK, BANK], F32, name=f"above{h}_{b}", align_bytes=64)
             for t in range(PACK):
-                for a in range(1 - h, k_passes):
-                    fit_pass(h, b, t, a)
+                fit_pass(h, b, t, 1)
                 nc.scalar.activation(above[h, b][:, t, :], fit[h, b, t][:], ACT.Relu, bias=neg_res[:, b, t : t + 1])
 
         def weigh(h, b):
-            if h:
-                z_bf[h, b] = staged([P, BANK * PACK], BF16, f"z_bf{h}_{b}", at_z)
-            else:
-                z_bf[h, b] = keep.tile([P, BANK * PACK], BF16, name=f"z_bf{h}_{b}", align_bytes=64)
+            z_bf[h, b] = keep.tile([P, BANK * PACK], BF16, name=f"z_bf{h}" if h else f"z_bf{h}_{b}", align_bytes=64)
             nc.vector.tensor_tensor(
                 z_bf[h, b][:].rearrange("p (c r t) -> p c t r", r=RUN, t=PACK),
                 above[h, b][:].rearrange("p t (c r) -> p c t r", r=RUN),
@@ -316,7 +333,7 @@ def tile_list_two_sided_match_kernel(
         quantise_wo(0)
         quantise_z(0, 0)
         give_sign(0, 1)
-        surplus(1, 0)
+        paired_surplus(1, 0)
         round_wo(1)
         quantise_z(0, 1)
         quantise_wo(1)
@@ -327,7 +344,7 @@ def tile_list_two_sided_match_kernel(
         for n in range(n_tiles):
             for b in reversed(range(i_passes)):
                 offer_pass(0, n, b, 1)
-        weigh(1, 0)
+        give_sign(1, 0)
         quantise_z(1, 0)
         give_sign(1, 1)
         for n in range(n_tiles):

@@ -15,6 +15,7 @@ FP8X4 = mybir.dt.float8_e4m3fn_x4
 FP4X4 = mybir.dt.float4_e2m1fn_x4
 ACT = mybir.ActivationFunctionType
 MULT = mybir.AluOpType.mult
+ADD = mybir.AluOpType.add
 
 P = 128
 PACK = 4
@@ -23,6 +24,8 @@ QUADS = 4
 BANK = 512
 RUN = 4
 LIST_ROWS = 16
+ROWS_AT = 96
+V_PLANE_AT = [12, 0]
 INTEREST_BANK = [[0, 1, 2, 3], [0, 2, 4, 5]]
 OFFER_BANK = [[4, 5, 6, 7], [1, 3, 6, 7]]
 
@@ -53,22 +56,16 @@ def tile_list_two_sided_match_kernel(
         neg_res = keep.tile([P, i_passes, PACK], F32, name="neg_res")
 
         LAP = 64
-        at_vs = 0
-        at_v0 = at_vs + T
-        at_wt = at_v0 + LAP
-        at_wo0 = at_v0 + 4 * T - LAP
-        at_v2_1 = at_wo0 + 4 * PACK * N
-        at_v2s = at_v2_1 + 4 * T2 - LAP
-        at_res = at_v2s + LAP
-        at_listed0_1 = at_res + LAP
-        at_wi_s = at_listed0_1
-        at_wi = at_wi_s + i_passes * N
-        at_v2_0 = at_v2s + T2
-        at_vs_listed = at_v2_0 + 4 * T2
-        at_v1 = at_vs_listed + S - LAP
-        at_listed0_0 = at_v1 + 4 * T
-        at_wo1 = at_listed0_0 + 4 * PASS - LAP
-        at_result2 = at_wo1 + 4 * PACK * N
+        at_v = 0
+        at_wo = [at_v, at_v + 4 * PACK * N]
+        at_v2_0 = at_v + 4 * k_passes * T
+        at_wi_s = at_v2_0
+        at_v2_1 = at_v2_0 + 4 * T2
+        at_vs = at_v2_1
+        at_vs_listed = [at_vs + T, at_v2_1 + 4 * T2]
+        at_wi = at_vs_listed[1]
+        at_v2s = at_wi + 2 * i_passes * N
+        at_result2 = at_v2s + T2
         at_above = at_result2 + 4 * BANK - LAP
         at_result0 = at_above + LAP
         at_result1 = at_result0 + 4 * BANK
@@ -76,34 +73,45 @@ def tile_list_two_sided_match_kernel(
 
         v_tab_s = staged([P, T // 4], I32, "v_tab_s", at_vs)
         v2_tab_s = staged([P, T2 // 4], I32, "v2_tab_s", at_v2s)
-        warm = staged([P, 16], F32, "warm", at_v2_0)
-        nc.vector.memset(v2_tab_s[:], 0)
-        nc.vector.memset(warm[:], 0.0)
-        nc.vector.memset(v_tab_s[32:64, :], 0)
-        nc.vector.memset(v_tab_s[64:P, :], 0)
-        nc.scalar.activation(warm[:, 0:1], warm[:, 1:2], ACT.Sigmoid)
+        for window in (v2_tab_s, v_tab_s):
+            nc.vector.memset(window[0:ROWS_AT, :], 0)
 
-        v_tab = [staged([P, T], I32, f"v_tab{a}", at) for a, at in enumerate([at_v0, at_v1])]
+        v_tab = staged([P, k_passes, T], I32, "v_tab", at_v)
         v2_tab = [staged([P, T2], I32, f"v2_tab{a}", at) for a, at in enumerate([at_v2_0, at_v2_1])]
-        res_t = staged([P, i_passes, 2 * PACK], F32, "res_t", at_res)
-        wt_t = staged([P, i_passes, 2 * PACK], F32, "wt_t", at_wt)
+        res_t = keep.tile([P, i_passes, 2 * PACK], F32, name="res_t")
+        wt_t = keep.tile([P, i_passes, 2 * PACK], F32, name="wt_t")
 
-        nc.sync.dma_start(out=v_tab_s[0:32, :], in_=tab_scales.bitcast(I32).rearrange("a q w -> (a q) w"))
-        nc.sync.dma_start(out=idx[:], in_=offs)
-        nc.sync.dma_start(out=v_tab[0][:], in_=words(tab_words, 0))
         nc.sync.dma_start(out=idx2[:], in_=offs2)
-        nc.sync.dma_start(out=v2_tab_s[0:P:4, :], in_=tab2_scales.bitcast(I32).rearrange("a q w -> (a q) w"))
+        nc.sync.dma_start(out=v2_tab_s[ROWS_AT:P, :], in_=tab2_scales.bitcast(I32).rearrange("a q w -> (a q) w"))
+        nc.sync.dma_start(out=idx[:], in_=offs)
+        nc.sync.dma_start(out=v_tab_s[ROWS_AT:P, :], in_=tab_scales.bitcast(I32).rearrange("a q w -> (a q) w"))
+        nc.sync.dma_start(out=v_tab[:], in_=tab_words.rearrange("a p t i -> p a (t i)").bitcast(I32))
         nc.sync.dma_start(out=v2_tab[0][:], in_=words(tab2_words, 0))
+        nc.scalar.dma_start(out=res_t[:, :, 0:PACK], in_=res.rearrange("(b p t) -> p b t", p=P, t=PACK))
+        nc.scalar.dma_start(out=wt_t[:, :, 0:PACK], in_=wt.rearrange("(b p t) -> p b t", p=P, t=PACK))
+        wt_half = keep.tile([P, i_passes, PACK], F32, name="wt_half")
+        wt_size = keep.tile([P, i_passes, PACK], F32, name="wt_size")
+        wt_sign = keep.tile([P, i_passes, PACK], BF16, name="wt_sign")
+        neg_level = keep.tile([P, i_passes, PACK], F32, name="neg_level")
+        nc.scalar.mul(neg_res[:], res_t[:, :, 0:PACK], -1.0)
+        nc.scalar.mul(wt_half[:], wt_t[:, :, 0:PACK], 0.5)
+        nc.scalar.activation(wt_size[:], wt_t[:, :, 0:PACK], ACT.Abs, scale=0.5)
+        nc.scalar.activation(wt_sign[:], wt_t[:, :, 0:PACK], ACT.Sign)
+        for b in range(i_passes):
+            for t in range(PACK):
+                nc.scalar.activation(
+                    neg_level[:, b, t : t + 1], neg_res[:, b, t : t + 1], ACT.Copy, scale=wt_size[:, b, t : t + 1]
+                )
 
         v_listed = [
-            [staged([P, PASS], U32, f"v_listed0_{b}", at) for b, at in enumerate([at_listed0_0, at_listed0_1])],
-            [keep.tile([P, PASS], U32, name=f"v_listed1_{b}", align_bytes=64) for b in range(i_passes)],
+            [keep.tile([P, PASS], U32, name=f"v_listed{a}_{b}", align_bytes=64) for b in range(i_passes)]
+            for a in range(k_passes)
         ]
         v_c = [
             [keep.tile([P, PACK, P], U32, name=f"v_c{a}_{b}", align_bytes=64) for b in range(i_passes)]
             for a in range(k_passes)
         ]
-        v_s_listed = [staged([P, PASS], U8, f"v_s_listed{b}", at_vs_listed + PASS * b) for b in range(i_passes)]
+        v_s_listed = [staged([P, PASS], U8, f"v_s_listed{b}", at_vs_listed[b]) for b in range(i_passes)]
         v_s = [keep.tile([P, S], U8, name="v_s0", align_bytes=64), keep.tile([P, S], U8, name="v_s1", align_bytes=64)]
         v2_c = {
             (a, h): keep.tile([P, BANK], U32, name=f"v2_c{a}_{h}", align_bytes=64)
@@ -111,11 +119,11 @@ def tile_list_two_sided_match_kernel(
             for h in range(j_chunks)
         }
         v2_s_listed = keep.tile([P, S2], U8, name="v2_s_listed", align_bytes=64)
-        v2_s = [staged([P, S2], U8, f"v2_s{a}", at_vs + S2 * a) for a in range(k_passes)]
+        v2_s = [keep.tile([P, S2], U8, name=f"v2_s{a}", align_bytes=64) for a in range(k_passes)]
 
         def gather_v_words(a, b):
             nc.vector.tensor_copy(
-                v_listed[a][b][:], v_tab[a][:].bitcast(U32).indirect(idx[:, b * cols : (b + 1) * cols])
+                v_listed[a][b][:], v_tab[:, a, :].bitcast(U32).indirect(idx[:, b * cols : (b + 1) * cols])
             )
 
         def order_v_words(a, b):
@@ -138,70 +146,54 @@ def tile_list_two_sided_match_kernel(
 
         def place_v2_scales(a):
             for q in range(QUADS):
-                first = 4 * (16 * a + 4 * q)
-                nc.sync.dma_start(
+                first = ROWS_AT + 16 * a + 4 * q
+                nc.scalar.dma_start(
                     out=v2_s[a][:].bitcast(I32)[32 * q : 32 * q + 4, :],
-                    in_=v2_s_listed[:].bitcast(I32)[first : first + 16 : 4, :],
+                    in_=v2_s_listed[:].bitcast(I32)[first : first + 4, :],
                 )
 
         def place_v_scales(a, q):
-            first = 16 * a + 4 * q
-            nc.sync.dma_start(
-                out=v_s[a][:].bitcast(I32)[32 * q : 32 * q + 4, :], in_=v_s[0][:].bitcast(I32)[first : first + 4, :]
+            first = ROWS_AT + 16 * a + 4 * q
+            row = 32 * q + V_PLANE_AT[a]
+            nc.scalar.dma_start(
+                out=v_s[a][:].bitcast(I32)[row : row + 4, :], in_=v_s[0][:].bitcast(I32)[first : first + 4, :]
             )
 
-        gather_v_scales(0)
-        gather_v_scales(1)
-        order_v_scales(0)
-        order_v_scales(1)
-        moves = [(a, q) for a in range(k_passes) for q in range(QUADS)][1:]
-        for a, q in moves[:-1]:
-            place_v_scales(a, q)
-        nc.sync.dma_start(out=v_tab[1][:], in_=words(tab_words, 1))
-        place_v_scales(*moves[-1])
-        nc.vector.tensor_copy(v2_s_listed[:], v2_tab_s[:].bitcast(U8).indirect(idx2[:]))
-        place_v2_scales(0)
-        nc.sync.dma_start(out=v2_tab[1][:], in_=words(tab2_words, 1))
-        nc.sync.dma_start(out=res_t[:, :, 0:PACK], in_=res.rearrange("(b p t) -> p b t", p=P, t=PACK))
-        place_v2_scales(1)
-        nc.scalar.mul(neg_res[:], res_t[:, :, 0:PACK], -1.0)
-        wt_size = keep.tile([P, i_passes, PACK], F32, name="wt_size")
-        wt_sign = keep.tile([P, i_passes, PACK], BF16, name="wt_sign")
-        neg_level = keep.tile([P, i_passes, PACK], F32, name="neg_level")
-
-        gather_v_words(0, 0)
-        gather_v_words(0, 1)
-        order_v_words(0, 0)
-        order_v_words(0, 1)
-        wo_raw = [staged([P, PACK, N], F32, f"wo_raw{b}", at) for b, at in enumerate([at_wo0, at_wo1])]
+        wo_raw = [staged([P, PACK, N], F32, f"wo_raw{b}", at_wo[b]) for b in range(i_passes)]
         wi_c = staged([P, i_passes, N // 2], I32, "wi_c", at_wi)
         wi_s = staged([P, i_passes, N // 4], I32, "wi_s", at_wi_s)
 
-        def load_wo(b):
+        nc.vector.tensor_copy(v2_s_listed[:], v2_tab_s[:].bitcast(U8).indirect(idx2[:]))
+        for a in range(k_passes):
+            place_v2_scales(a)
+        gather_v_scales(0)
+        gather_v_scales(1)
+        order_v_scales(0)
+        nc.sync.dma_start(out=v2_tab[1][:], in_=words(tab2_words, 1))
+        order_v_scales(1)
+        for a in range(k_passes):
+            for q in range(QUADS):
+                if (a, q) != (0, QUADS - 1):
+                    place_v_scales(a, q)
+        nc.scalar.dma_start(out=wi_c[:], in_=wi_words.bitcast(I32).rearrange("b p w -> p b w"))
+        for a in range(k_passes):
+            gather_v_words(a, 0)
+            gather_v_words(a, 1)
+            order_v_words(a, 0)
+            order_v_words(a, 1)
+        for b in range(i_passes):
             nc.sync.dma_start(
                 out=wo_raw[b][:], in_=wo[b * PASS : (b + 1) * PASS, :].rearrange("(p t) n -> p t n", t=PACK)
             )
-
-        nc.sync.dma_start(out=wt_t[:, :, 0:PACK], in_=wt.rearrange("(b p t) -> p b t", p=P, t=PACK))
-        load_wo(0)
-        load_wo(1)
-        nc.sync.dma_start(out=wi_c[:], in_=wi_words.bitcast(I32).rearrange("b p w -> p b w"))
+        gather_v2_words(0, 1)
+        gather_v2_words(0, 0)
         for q in range(QUADS):
             nc.sync.dma_start(
                 out=wi_s[32 * q : 32 * q + 4, :, :],
                 in_=wi_scales.bitcast(I32)[:, 4 * q : 4 * q + 4, :].rearrange("b r w -> r b w"),
             )
-        gather_v2_words(0, 1)
-        gather_v2_words(0, 0)
-        gather_v_words(1, 0)
-        gather_v_words(1, 1)
-        order_v_words(1, 0)
-        order_v_words(1, 1)
         gather_v2_words(1, 0)
         gather_v2_words(1, 1)
-        nc.scalar.activation(wt_size[:], wt_t[:, :, 0:PACK], ACT.Abs)
-        nc.scalar.activation(wt_sign[:], wt_t[:, :, 0:PACK], ACT.Sign)
-        nc.vector.tensor_tensor(neg_level[:], neg_res[:], wt_size[:], MULT)
 
         z_c = {}
         z_s = {}
@@ -218,7 +210,7 @@ def tile_list_two_sided_match_kernel(
             nc.tensor.matmul_mx(
                 out=fit[h, b, t][:],
                 lhsT=v_c[a][b][:, t, :].bitcast(FP8X4),
-                lhsT_scale=v_s[a][:, PASS * b + P * t : PASS * b + P * (t + 1)],
+                lhsT_scale=v_s[a][V_PLANE_AT[a] :, PASS * b + P * t : PASS * b + P * (t + 1)],
                 rhs=v2_c[a, h][:].bitcast(FP8X4),
                 rhs_scale=v2_s[a][:, BANK * h : BANK * (h + 1)],
                 start=(a == 0),
@@ -236,7 +228,7 @@ def tile_list_two_sided_match_kernel(
             nc.vector.tensor_tensor(
                 z_bf[h, b][:].rearrange("p (c r t) -> p c t r", r=RUN, t=PACK),
                 above[h, b][:].rearrange("p t (c r) -> p c t r", r=RUN),
-                wt_t[:, b, 0:PACK].unsqueeze(1).unsqueeze(3).to_broadcast([P, BANK // RUN, PACK, RUN]),
+                wt_half[:, b, :].unsqueeze(1).unsqueeze(3).to_broadcast([P, BANK // RUN, PACK, RUN]),
                 MULT,
             )
 
@@ -300,7 +292,7 @@ def tile_list_two_sided_match_kernel(
 
         def sigmoid(h, n):
             chance[h, n] = keep.tile([P, BANK], F32, name=f"chance{h}_{n}")
-            nc.scalar.activation(chance[h, n][:], score["interest", h, n][:], ACT.Sigmoid)
+            nc.scalar.activation(chance[h, n][:], score["interest", h, n][:], ACT.Tanh)
 
         def offer_pass(h, n, b, first):
             if b == first:
@@ -320,7 +312,7 @@ def tile_list_two_sided_match_kernel(
                 result = keep.tile([P, BANK], F32, name=f"result{h}_{n}")
             else:
                 result = staged([P, BANK], F32, f"result{h}_{n}", [at_result0, at_result1, at_result2, at_z][n])
-            nc.vector.tensor_tensor(result[:], score["offer", h, n][:], chance[h, n][:], MULT)
+            nc.vector.scalar_tensor_tensor(result[:], chance[h, n][:], 1.0, score["offer", h, n][:], ADD, MULT)
             nc.sync.dma_start(out=out[P * n : P * (n + 1), BANK * h : BANK * (h + 1)], in_=result[:])
 
         for b in range(i_passes):

@@ -56,16 +56,22 @@ def tile_list_two_sided_match_kernel(
         neg_res = keep.tile([P, i_passes, PACK], F32, name="neg_res")
 
         LAP = 64
-        at_v = 0
-        at_wo = [at_v, at_v + 4 * PACK * N]
-        at_v2_0 = at_v + 4 * k_passes * T
-        at_wi_s = at_v2_0
+        at_vs = 0
+        at_wt = at_vs + T
+        at_v0 = at_wt
+        at_wo0 = at_wt + LAP
+        at_v2_0 = at_wo0 + 4 * PACK * N
         at_v2_1 = at_v2_0 + 4 * T2
-        at_vs = at_v2_1
-        at_vs_listed = [at_vs + T, at_v2_1 + 4 * T2]
-        at_wi = at_vs_listed[1]
-        at_v2s = at_wi + 2 * i_passes * N
-        at_result2 = at_v2s + T2
+        at_late = at_v2_1
+        at_v2s = at_v2_1 + 4 * T2 - LAP
+        at_res = at_v2s + LAP
+        at_listed = [at_res + LAP, at_res + LAP + 4 * PASS]
+        at_wi_s = at_listed[0]
+        at_wi = at_wi_s + i_passes * N
+        at_wo1 = at_wi + 2 * i_passes * N
+        at_vs_listed = at_wo1 + 4 * PACK * N
+        at_v1 = at_vs_listed + S - LAP
+        at_result2 = at_v1 + 4 * T
         at_above = at_result2 + 4 * BANK - LAP
         at_result0 = at_above + LAP
         at_result1 = at_result0 + 4 * BANK
@@ -73,57 +79,44 @@ def tile_list_two_sided_match_kernel(
 
         v_tab_s = staged([P, T // 4], I32, "v_tab_s", at_vs)
         v2_tab_s = staged([P, T2 // 4], I32, "v2_tab_s", at_v2s)
-        for window in (v2_tab_s, v_tab_s):
+        for window in (v_tab_s, v2_tab_s):
             nc.vector.memset(window[0:ROWS_AT, :], 0)
 
-        v_tab = staged([P, k_passes, T], I32, "v_tab", at_v)
+        v_tab = [staged([P, T], I32, f"v_tab{a}", at) for a, at in enumerate([at_v0, at_v1])]
         v2_tab = [staged([P, T2], I32, f"v2_tab{a}", at) for a, at in enumerate([at_v2_0, at_v2_1])]
-        res_t = keep.tile([P, i_passes, 2 * PACK], F32, name="res_t")
-        wt_t = keep.tile([P, i_passes, 2 * PACK], F32, name="wt_t")
+        res_t = staged([P, i_passes, 2 * PACK], F32, "res_t", at_res)
+        wt_t = staged([P, i_passes, 2 * PACK], F32, "wt_t", at_wt)
 
+        nc.sync.dma_start(out=v_tab_s[ROWS_AT:P, :], in_=tab_scales.bitcast(I32).rearrange("a q w -> (a q) w"))
+        nc.sync.dma_start(out=idx[:], in_=offs)
+        nc.sync.dma_start(out=v_tab[0][:], in_=words(tab_words, 0))
         nc.sync.dma_start(out=idx2[:], in_=offs2)
         nc.sync.dma_start(out=v2_tab_s[ROWS_AT:P, :], in_=tab2_scales.bitcast(I32).rearrange("a q w -> (a q) w"))
-        nc.sync.dma_start(out=idx[:], in_=offs)
-        nc.sync.dma_start(out=v_tab_s[ROWS_AT:P, :], in_=tab_scales.bitcast(I32).rearrange("a q w -> (a q) w"))
-        nc.sync.dma_start(out=v_tab[:], in_=tab_words.rearrange("a p t i -> p a (t i)").bitcast(I32))
         nc.sync.dma_start(out=v2_tab[0][:], in_=words(tab2_words, 0))
-        nc.scalar.dma_start(out=res_t[:, :, 0:PACK], in_=res.rearrange("(b p t) -> p b t", p=P, t=PACK))
-        nc.scalar.dma_start(out=wt_t[:, :, 0:PACK], in_=wt.rearrange("(b p t) -> p b t", p=P, t=PACK))
-        wt_half = keep.tile([P, i_passes, PACK], F32, name="wt_half")
-        wt_size = keep.tile([P, i_passes, PACK], F32, name="wt_size")
-        wt_sign = keep.tile([P, i_passes, PACK], BF16, name="wt_sign")
-        neg_level = keep.tile([P, i_passes, PACK], F32, name="neg_level")
-        nc.scalar.mul(neg_res[:], res_t[:, :, 0:PACK], -1.0)
-        nc.scalar.mul(wt_half[:], wt_t[:, :, 0:PACK], 0.5)
-        nc.scalar.activation(wt_size[:], wt_t[:, :, 0:PACK], ACT.Abs, scale=0.5)
-        nc.scalar.activation(wt_sign[:], wt_t[:, :, 0:PACK], ACT.Sign)
-        for b in range(i_passes):
-            for t in range(PACK):
-                nc.scalar.activation(
-                    neg_level[:, b, t : t + 1], neg_res[:, b, t : t + 1], ACT.Copy, scale=wt_size[:, b, t : t + 1]
-                )
 
         v_listed = [
-            [keep.tile([P, PASS], U32, name=f"v_listed{a}_{b}", align_bytes=64) for b in range(i_passes)]
-            for a in range(k_passes)
+            [staged([P, PASS], U32, f"v_listed0_{b}", at_listed[b]) for b in range(i_passes)],
+            [keep.tile([P, PASS], U32, name=f"v_listed1_{b}", align_bytes=64) for b in range(i_passes)],
         ]
         v_c = [
             [keep.tile([P, PACK, P], U32, name=f"v_c{a}_{b}", align_bytes=64) for b in range(i_passes)]
             for a in range(k_passes)
         ]
-        v_s_listed = [staged([P, PASS], U8, f"v_s_listed{b}", at_vs_listed[b]) for b in range(i_passes)]
+        v_s_listed = [staged([P, PASS], U8, f"v_s_listed{b}", at_vs_listed + PASS * b) for b in range(i_passes)]
         v_s = [keep.tile([P, S], U8, name="v_s0", align_bytes=64), keep.tile([P, S], U8, name="v_s1", align_bytes=64)]
         v2_c = {
-            (a, h): keep.tile([P, BANK], U32, name=f"v2_c{a}_{h}", align_bytes=64)
+            (a, h): staged([P, BANK], U32, "v2_c0_1", at_late)
+            if (a, h) == (0, 1)
+            else keep.tile([P, BANK], U32, name=f"v2_c{a}_{h}", align_bytes=64)
             for a in range(k_passes)
             for h in range(j_chunks)
         }
         v2_s_listed = keep.tile([P, S2], U8, name="v2_s_listed", align_bytes=64)
-        v2_s = [keep.tile([P, S2], U8, name=f"v2_s{a}", align_bytes=64) for a in range(k_passes)]
+        v2_s = [staged([P, S2], U8, f"v2_s{a}", at_vs + S2 * a) for a in range(k_passes)]
 
         def gather_v_words(a, b):
             nc.vector.tensor_copy(
-                v_listed[a][b][:], v_tab[:, a, :].bitcast(U32).indirect(idx[:, b * cols : (b + 1) * cols])
+                v_listed[a][b][:], v_tab[a][:].bitcast(U32).indirect(idx[:, b * cols : (b + 1) * cols])
             )
 
         def order_v_words(a, b):
@@ -147,7 +140,7 @@ def tile_list_two_sided_match_kernel(
         def place_v2_scales(a):
             for q in range(QUADS):
                 first = ROWS_AT + 16 * a + 4 * q
-                nc.scalar.dma_start(
+                nc.sync.dma_start(
                     out=v2_s[a][:].bitcast(I32)[32 * q : 32 * q + 4, :],
                     in_=v2_s_listed[:].bitcast(I32)[first : first + 4, :],
                 )
@@ -155,45 +148,66 @@ def tile_list_two_sided_match_kernel(
         def place_v_scales(a, q):
             first = ROWS_AT + 16 * a + 4 * q
             row = 32 * q + V_PLANE_AT[a]
-            nc.scalar.dma_start(
+            nc.sync.dma_start(
                 out=v_s[a][:].bitcast(I32)[row : row + 4, :], in_=v_s[0][:].bitcast(I32)[first : first + 4, :]
             )
 
-        wo_raw = [staged([P, PACK, N], F32, f"wo_raw{b}", at_wo[b]) for b in range(i_passes)]
-        wi_c = staged([P, i_passes, N // 2], I32, "wi_c", at_wi)
-        wi_s = staged([P, i_passes, N // 4], I32, "wi_s", at_wi_s)
-
-        nc.vector.tensor_copy(v2_s_listed[:], v2_tab_s[:].bitcast(U8).indirect(idx2[:]))
-        for a in range(k_passes):
-            place_v2_scales(a)
         gather_v_scales(0)
         gather_v_scales(1)
         order_v_scales(0)
-        nc.sync.dma_start(out=v2_tab[1][:], in_=words(tab2_words, 1))
         order_v_scales(1)
-        for a in range(k_passes):
-            for q in range(QUADS):
-                if (a, q) != (0, QUADS - 1):
-                    place_v_scales(a, q)
-        nc.scalar.dma_start(out=wi_c[:], in_=wi_words.bitcast(I32).rearrange("b p w -> p b w"))
-        for a in range(k_passes):
-            gather_v_words(a, 0)
-            gather_v_words(a, 1)
-            order_v_words(a, 0)
-            order_v_words(a, 1)
-        for b in range(i_passes):
+        moves = [(a, q) for a in range(k_passes) for q in range(QUADS) if (a, q) != (0, QUADS - 1)]
+        for a, q in moves[:-1]:
+            place_v_scales(a, q)
+        nc.sync.dma_start(out=v_tab[1][:], in_=words(tab_words, 1))
+        place_v_scales(*moves[-1])
+        nc.vector.tensor_copy(v2_s_listed[:], v2_tab_s[:].bitcast(U8).indirect(idx2[:]))
+        place_v2_scales(0)
+        nc.sync.dma_start(out=v2_tab[1][:], in_=words(tab2_words, 1))
+        nc.sync.dma_start(out=res_t[:, :, 0:PACK], in_=res.rearrange("(b p t) -> p b t", p=P, t=PACK))
+        place_v2_scales(1)
+        nc.scalar.mul(neg_res[:], res_t[:, :, 0:PACK], -1.0)
+        wt_size = keep.tile([P, i_passes, PACK], F32, name="wt_size")
+        wt_sign = keep.tile([P, i_passes, PACK], BF16, name="wt_sign")
+        neg_level = keep.tile([P, i_passes, PACK], F32, name="neg_level")
+
+        gather_v_words(0, 0)
+        gather_v_words(0, 1)
+        order_v_words(0, 0)
+        order_v_words(0, 1)
+        wo_raw = [staged([P, PACK, N], F32, f"wo_raw{b}", at) for b, at in enumerate([at_wo0, at_wo1])]
+        wi_c = staged([P, i_passes, N // 2], I32, "wi_c", at_wi)
+        wi_s = staged([P, i_passes, N // 4], I32, "wi_s", at_wi_s)
+
+        def load_wo(b):
             nc.sync.dma_start(
                 out=wo_raw[b][:], in_=wo[b * PASS : (b + 1) * PASS, :].rearrange("(p t) n -> p t n", t=PACK)
             )
-        gather_v2_words(0, 1)
-        gather_v2_words(0, 0)
+
+        nc.sync.dma_start(out=wt_t[:, :, 0:PACK], in_=wt.rearrange("(b p t) -> p b t", p=P, t=PACK))
+        load_wo(0)
+        load_wo(1)
+        nc.sync.dma_start(out=wi_c[:], in_=wi_words.bitcast(I32).rearrange("b p w -> p b w"))
         for q in range(QUADS):
             nc.sync.dma_start(
                 out=wi_s[32 * q : 32 * q + 4, :, :],
                 in_=wi_scales.bitcast(I32)[:, 4 * q : 4 * q + 4, :].rearrange("b r w -> r b w"),
             )
+        gather_v2_words(0, 0)
+        gather_v_words(1, 0)
+        gather_v_words(1, 1)
+        order_v_words(1, 0)
+        order_v_words(1, 1)
         gather_v2_words(1, 0)
         gather_v2_words(1, 1)
+        gather_v2_words(0, 1)
+        nc.scalar.activation(wt_size[:], wt_t[:, :, 0:PACK], ACT.Abs, scale=0.5)
+        nc.scalar.activation(wt_sign[:], wt_t[:, :, 0:PACK], ACT.Sign)
+        for b in range(i_passes):
+            for t in range(PACK):
+                nc.scalar.activation(
+                    neg_level[:, b, t : t + 1], neg_res[:, b, t : t + 1], ACT.Copy, scale=wt_size[:, b, t : t + 1]
+                )
 
         z_c = {}
         z_s = {}
@@ -215,21 +229,6 @@ def tile_list_two_sided_match_kernel(
                 rhs_scale=v2_s[a][:, BANK * h : BANK * (h + 1)],
                 start=(a == 0),
                 stop=(a == k_passes - 1),
-            )
-
-        def surplus(h, b):
-            above[h, b] = keep.tile([P, PACK, BANK], F32, name=f"above{h}_{b}", align_bytes=64)
-            for t in range(PACK):
-                fit_pass(h, b, t, 1)
-                nc.scalar.activation(above[h, b][:, t, :], fit[h, b, t][:], ACT.Relu, bias=neg_res[:, b, t : t + 1])
-
-        def weigh(h, b):
-            z_bf[h, b] = keep.tile([P, BANK * PACK], BF16, name=f"z_bf{h}" if h else f"z_bf{h}_{b}", align_bytes=64)
-            nc.vector.tensor_tensor(
-                z_bf[h, b][:].rearrange("p (c r t) -> p c t r", r=RUN, t=PACK),
-                above[h, b][:].rearrange("p t (c r) -> p c t r", r=RUN),
-                wt_half[:, b, :].unsqueeze(1).unsqueeze(3).to_broadcast([P, BANK // RUN, PACK, RUN]),
-                MULT,
             )
 
         def paired_surplus(h, b):
@@ -318,10 +317,10 @@ def tile_list_two_sided_match_kernel(
         for b in range(i_passes):
             for t in range(PACK):
                 fit_pass(0, b, t, 0)
-        surplus(0, 0)
+        paired_surplus(0, 0)
         paired_surplus(0, 1)
         round_wo(0)
-        weigh(0, 0)
+        give_sign(0, 0)
         quantise_wo(0)
         quantise_z(0, 0)
         give_sign(0, 1)

@@ -26,8 +26,8 @@ RUN = 4
 LIST_ROWS = 16
 ROWS_AT = 96
 V_PLANE_AT = [12, 0]
-INTEREST_BANK = [[0, 1, 2, 3], [0, 2, 4, 5]]
-OFFER_BANK = [[4, 5, 6, 7], [1, 3, 6, 7]]
+INTEREST_BANK = [[4, 5, 6, 7], [4, 6, 0, 1]]
+OFFER_BANK = [[0, 1, 2, 3], [5, 7, 2, 3]]
 
 
 def tile_list_two_sided_match_kernel(
@@ -62,7 +62,6 @@ def tile_list_two_sided_match_kernel(
         at_wo0 = at_wt + LAP
         at_v2_0 = at_wo0 + 4 * PACK * N
         at_v2_1 = at_v2_0 + 4 * T2
-        at_late = at_v2_1
         at_v2s = at_v2_1 + 4 * T2 - LAP
         at_res = at_v2s + LAP
         at_listed = [at_res + LAP, at_res + LAP + 4 * PASS]
@@ -105,9 +104,7 @@ def tile_list_two_sided_match_kernel(
         v_s_listed = [staged([P, PASS], U8, f"v_s_listed{b}", at_vs_listed + PASS * b) for b in range(i_passes)]
         v_s = [keep.tile([P, S], U8, name="v_s0", align_bytes=64), keep.tile([P, S], U8, name="v_s1", align_bytes=64)]
         v2_c = {
-            (a, h): staged([P, BANK], U32, "v2_c0_1", at_late)
-            if (a, h) == (0, 1)
-            else keep.tile([P, BANK], U32, name=f"v2_c{a}_{h}", align_bytes=64)
+            (a, h): keep.tile([P, BANK], U32, name=f"v2_c{a}_{h}", align_bytes=64)
             for a in range(k_passes)
             for h in range(j_chunks)
         }
@@ -167,6 +164,7 @@ def tile_list_two_sided_match_kernel(
         nc.sync.dma_start(out=res_t[:, :, 0:PACK], in_=res.rearrange("(b p t) -> p b t", p=P, t=PACK))
         place_v2_scales(1)
         nc.scalar.mul(neg_res[:], res_t[:, :, 0:PACK], -1.0)
+        wt_half = keep.tile([P, i_passes, PACK], F32, name="wt_half")
         wt_size = keep.tile([P, i_passes, PACK], F32, name="wt_size")
         wt_sign = keep.tile([P, i_passes, PACK], BF16, name="wt_sign")
         neg_level = keep.tile([P, i_passes, PACK], F32, name="neg_level")
@@ -193,6 +191,7 @@ def tile_list_two_sided_match_kernel(
                 out=wi_s[32 * q : 32 * q + 4, :, :],
                 in_=wi_scales.bitcast(I32)[:, 4 * q : 4 * q + 4, :].rearrange("b r w -> r b w"),
             )
+        gather_v2_words(0, 1)
         gather_v2_words(0, 0)
         gather_v_words(1, 0)
         gather_v_words(1, 1)
@@ -200,14 +199,10 @@ def tile_list_two_sided_match_kernel(
         order_v_words(1, 1)
         gather_v2_words(1, 0)
         gather_v2_words(1, 1)
-        gather_v2_words(0, 1)
         nc.scalar.activation(wt_size[:], wt_t[:, :, 0:PACK], ACT.Abs, scale=0.5)
         nc.scalar.activation(wt_sign[:], wt_t[:, :, 0:PACK], ACT.Sign)
-        for b in range(i_passes):
-            for t in range(PACK):
-                nc.scalar.activation(
-                    neg_level[:, b, t : t + 1], neg_res[:, b, t : t + 1], ACT.Copy, scale=wt_size[:, b, t : t + 1]
-                )
+        nc.scalar.mul(wt_half[:], wt_t[:, :, 0:PACK], 0.5)
+        nc.vector.tensor_tensor(neg_level[:], neg_res[:], wt_size[:], MULT)
 
         z_c = {}
         z_s = {}
@@ -220,7 +215,7 @@ def tile_list_two_sided_match_kernel(
 
         def fit_pass(h, b, t, a):
             if a == 0:
-                fit[h, b, t] = psum.tile([P, BANK], F32, name=f"bank{PACK * b + t}")
+                fit[h, b, t] = psum.tile([P, BANK], F32, name=f"bank{PACK * b * (1 - h) + t}")
             nc.tensor.matmul_mx(
                 out=fit[h, b, t][:],
                 lhsT=v_c[a][b][:, t, :].bitcast(FP8X4),
@@ -229,6 +224,24 @@ def tile_list_two_sided_match_kernel(
                 rhs_scale=v2_s[a][:, BANK * h : BANK * (h + 1)],
                 start=(a == 0),
                 stop=(a == k_passes - 1),
+            )
+
+        def surplus(h, b):
+            above[h, b] = keep.tile([P, PACK, BANK], F32, name=f"above{h}_{b}", align_bytes=64)
+            for t in range(PACK):
+                fit_pass(h, b, t, 1)
+                nc.scalar.activation(above[h, b][:, t, :], fit[h, b, t][:], ACT.Relu, bias=neg_res[:, b, t : t + 1])
+
+        def weigh(h, b):
+            if b == 0:
+                z_bf[h, b] = staged([P, BANK * PACK], BF16, "z_bf_first", at_wo0)
+            else:
+                z_bf[h, b] = keep.tile([P, BANK * PACK], BF16, name=f"z_bf{h}_{b}", align_bytes=64)
+            nc.vector.tensor_tensor(
+                z_bf[h, b][:].rearrange("p (c r t) -> p c t r", r=RUN, t=PACK),
+                above[h, b][:].rearrange("p t (c r) -> p c t r", r=RUN),
+                wt_half[:, b, :].unsqueeze(1).unsqueeze(3).to_broadcast([P, BANK // RUN, PACK, RUN]),
+                MULT,
             )
 
         def paired_surplus(h, b):
@@ -317,13 +330,13 @@ def tile_list_two_sided_match_kernel(
         for b in range(i_passes):
             for t in range(PACK):
                 fit_pass(0, b, t, 0)
-        paired_surplus(0, 0)
-        paired_surplus(0, 1)
+        surplus(0, 0)
+        surplus(0, 1)
         round_wo(0)
-        give_sign(0, 0)
         quantise_wo(0)
+        weigh(0, 0)
+        weigh(0, 1)
         quantise_z(0, 0)
-        give_sign(0, 1)
         paired_surplus(1, 0)
         round_wo(1)
         quantise_z(0, 1)

@@ -21,13 +21,13 @@ P = 128
 PACK = 4
 PASS = P * PACK
 QUADS = 4
-BANK = 512
+CHUNK = 256
 RUN = 4
 LIST_ROWS = 16
 ROWS_AT = 96
-V_PLANE_AT = [12, 0]
-INTEREST_BANK = [[4, 5, 6, 7], [4, 6, 0, 1]]
-OFFER_BANK = [[0, 1, 2, 3], [5, 7, 2, 3]]
+PLANE_AT = [12, 0]
+PLAIN_CHUNKS = 2
+LAP = 64
 
 
 def tile_list_two_sided_match_kernel(
@@ -36,9 +36,7 @@ def tile_list_two_sided_match_kernel(
     nc = tc.nc
     k_passes = K // PASS
     i_passes = S // PASS
-    j_chunks = S2 // BANK
-    n_tiles = N // P
-    cols = BANK // LIST_ROWS
+    chunks = S2 // CHUNK
 
     with ExitStack() as ctx:
         keep = ctx.enter_context(tc.tile_pool(name="keep", bufs=1))
@@ -48,131 +46,115 @@ def tile_list_two_sided_match_kernel(
         def staged(shape, dtype, name, offset):
             return stage.tile(shape, dtype, name=name, align_bytes=64, offset=offset)
 
+        def kept(shape, dtype, name):
+            return keep.tile(shape, dtype, name=name, align_bytes=64)
+
         def words(table, a):
             return table[a].rearrange("p t i -> p (t i)").bitcast(I32)
 
+        def entries(listed, first, count):
+            return listed[:, first // LIST_ROWS : (first + count) // LIST_ROWS]
+
         idx = keep.tile([P, S // LIST_ROWS], U16, name="idx")
         idx2 = keep.tile([P, S2 // LIST_ROWS], U16, name="idx2")
-        neg_res = keep.tile([P, i_passes, PACK], F32, name="neg_res")
 
-        LAP = 64
-        at_vs = 0
-        at_wt = at_vs + T
-        at_v0 = at_wt
-        at_wo0 = at_wt + LAP
-        at_v2_0 = at_wo0 + 4 * PACK * N
-        at_v2_1 = at_v2_0 + 4 * T2
-        at_v2s = at_v2_1 + 4 * T2 - LAP
-        at_res = at_v2s + LAP
-        at_listed = [at_res + LAP, at_res + LAP + 4 * PASS]
-        at_wi_s = at_listed[0]
-        at_wi = at_wi_s + i_passes * N
-        at_wo1 = at_wi + 2 * i_passes * N
-        at_vs_listed = at_wo1 + 4 * PACK * N
-        at_v1 = at_vs_listed + S - LAP
-        at_result2 = at_v1 + 4 * T
-        at_above = at_result2 + 4 * BANK - LAP
-        at_result0 = at_above + LAP
-        at_result1 = at_result0 + 4 * BANK
-        at_z = at_result1 + 4 * BANK
+        at_v2_1 = 0
+        at_v2s_listed = at_v2_1 + 4 * T2 - LAP
+        at_v0 = at_v2s_listed + S2
+        at_wi = at_v0
+        at_wi_s = at_wi + 2 * i_passes * N
+        at_wo0 = at_v0 + 4 * T - LAP
+        at_v1 = at_wo0 + 4 * PACK * N
+        at_wo1 = at_v1 + 4 * T - LAP
+        at_first_picks = at_wo1 + 4 * PACK * N
+        at_late_picks = at_first_picks + 4 * CHUNK - LAP
 
-        v_tab_s = staged([P, T // 4], I32, "v_tab_s", at_vs)
-        v2_tab_s = staged([P, T2 // 4], I32, "v2_tab_s", at_v2s)
+        v_tab_s = kept([P, T // 4], I32, "v_tab_s")
+        v2_tab_s = kept([P, T2 // 4], I32, "v2_tab_s")
         for window in (v_tab_s, v2_tab_s):
             nc.vector.memset(window[0:ROWS_AT, :], 0)
-
         v_tab = [staged([P, T], I32, f"v_tab{a}", at) for a, at in enumerate([at_v0, at_v1])]
-        v2_tab = [staged([P, T2], I32, f"v2_tab{a}", at) for a, at in enumerate([at_v2_0, at_v2_1])]
-        res_t = staged([P, i_passes, 2 * PACK], F32, "res_t", at_res)
-        wt_t = staged([P, i_passes, 2 * PACK], F32, "wt_t", at_wt)
+        v2_tab = [kept([P, T2], I32, "v2_tab0"), staged([P, T2], I32, "v2_tab1", at_v2_1)]
+        res_t = kept([P, i_passes, 2 * PACK], F32, "res_t")
+        wt_t = kept([P, i_passes, 2 * PACK], F32, "wt_t")
 
         nc.sync.dma_start(out=v_tab_s[ROWS_AT:P, :], in_=tab_scales.bitcast(I32).rearrange("a q w -> (a q) w"))
         nc.sync.dma_start(out=idx[:], in_=offs)
-        nc.sync.dma_start(out=v_tab[0][:], in_=words(tab_words, 0))
-        nc.sync.dma_start(out=idx2[:], in_=offs2)
         nc.sync.dma_start(out=v2_tab_s[ROWS_AT:P, :], in_=tab2_scales.bitcast(I32).rearrange("a q w -> (a q) w"))
+        nc.sync.dma_start(out=idx2[:], in_=offs2)
+        nc.sync.dma_start(out=v_tab[0][:], in_=words(tab_words, 0))
         nc.sync.dma_start(out=v2_tab[0][:], in_=words(tab2_words, 0))
+        nc.sync.dma_start(out=v_tab[1][:], in_=words(tab_words, 1))
+        nc.scalar.dma_start(out=res_t[:, :, 0:PACK], in_=res.rearrange("(b p t) -> p b t", p=P, t=PACK))
+        nc.scalar.dma_start(out=wt_t[:, :, 0:PACK], in_=wt.rearrange("(b p t) -> p b t", p=P, t=PACK))
 
-        v_listed = [
-            [staged([P, PASS], U32, f"v_listed0_{b}", at_listed[b]) for b in range(i_passes)],
-            [keep.tile([P, PASS], U32, name=f"v_listed1_{b}", align_bytes=64) for b in range(i_passes)],
-        ]
-        v_c = [
-            [keep.tile([P, PACK, P], U32, name=f"v_c{a}_{b}", align_bytes=64) for b in range(i_passes)]
-            for a in range(k_passes)
-        ]
-        v_s_listed = [staged([P, PASS], U8, f"v_s_listed{b}", at_vs_listed + PASS * b) for b in range(i_passes)]
-        v_s = [keep.tile([P, S], U8, name="v_s0", align_bytes=64), keep.tile([P, S], U8, name="v_s1", align_bytes=64)]
-        v2_c = {
-            (a, h): keep.tile([P, BANK], U32, name=f"v2_c{a}_{h}", align_bytes=64)
-            for a in range(k_passes)
-            for h in range(j_chunks)
-        }
-        v2_s_listed = keep.tile([P, S2], U8, name="v2_s_listed", align_bytes=64)
-        v2_s = [staged([P, S2], U8, f"v2_s{a}", at_vs + S2 * a) for a in range(k_passes)]
+        neg_res = kept([P, i_passes, PACK], F32, "neg_res")
+        wt_half = kept([P, i_passes, PACK], F32, "wt_half")
+        wt_size = kept([P, i_passes, PACK], F32, "wt_size")
+        wt_sign = kept([P, i_passes, PACK], BF16, "wt_sign")
+        neg_level = kept([P, i_passes, PACK], F32, "neg_level")
+        nc.scalar.mul(neg_res[:], res_t[:, :, 0:PACK], -1.0)
+        nc.scalar.activation(wt_size[:], wt_t[:, :, 0:PACK], ACT.Abs, scale=0.5)
+        nc.scalar.activation(wt_sign[:], wt_t[:, :, 0:PACK], ACT.Sign)
+        nc.scalar.mul(wt_half[:], wt_t[:, :, 0:PACK], 0.5)
+        nc.gpsimd.tensor_tensor(neg_level[:], neg_res[:], wt_size[:], MULT)
 
-        def gather_v_words(a, b):
+        vs_listed = kept([P, S], U8, "vs_listed")
+        v2s_listed = staged([P, S2], U8, "v2s_listed", at_v2s_listed)
+        planes = [kept([P, S + S2], U8, f"planes{a}") for a in range(k_passes)]
+        for b in range(i_passes):
             nc.vector.tensor_copy(
-                v_listed[a][b][:], v_tab[a][:].bitcast(U32).indirect(idx[:, b * cols : (b + 1) * cols])
+                vs_listed[:, PASS * b : PASS * (b + 1)], v_tab_s[:].bitcast(U8).indirect(entries(idx, PASS * b, PASS))
+            )
+        for b in range(i_passes):
+            nc.vector.tensor_copy(
+                planes[0][:, PASS * b : PASS * (b + 1)].rearrange("p (t m) -> p t m", t=PACK),
+                vs_listed[:, PASS * b : PASS * (b + 1)].rearrange("p (m t) -> p t m", t=PACK),
+            )
+        for h in range(2):
+            nc.vector.tensor_copy(
+                v2s_listed[:, PASS * h : PASS * (h + 1)],
+                v2_tab_s[:].bitcast(U8).indirect(entries(idx2, PASS * h, PASS)),
+            )
+        for h in range(2):
+            nc.vector.tensor_copy(
+                planes[0][:, S + PASS * h : S + PASS * (h + 1)].bitcast(I32),
+                v2s_listed[:, PASS * h : PASS * (h + 1)].bitcast(I32),
             )
 
-        def order_v_words(a, b):
-            nc.vector.tensor_copy(
-                v_c[a][b][:].bitcast(I32).rearrange("p t (g r) -> p g t r", r=4),
-                v_listed[a][b][:].bitcast(I32).rearrange("p (g r t) -> p g t r", r=4, t=PACK),
-            )
-
-        def gather_v_scales(b):
-            nc.vector.tensor_copy(v_s_listed[b][:], v_tab_s[:].bitcast(U8).indirect(idx[:, b * cols : (b + 1) * cols]))
-
-        def order_v_scales(b):
-            nc.vector.tensor_copy(
-                v_s[0][:, PASS * b : PASS * (b + 1)].rearrange("p (t m) -> p t m", t=PACK),
-                v_s_listed[b][:].rearrange("p (m t) -> p t m", t=PACK),
-            )
-
-        def gather_v2_words(a, h):
-            nc.vector.tensor_copy(v2_c[a, h][:], v2_tab[a][:].bitcast(U32).indirect(idx2[:, h * cols : (h + 1) * cols]))
-
-        def place_v2_scales(a):
+        def place_planes(a):
             for q in range(QUADS):
                 first = ROWS_AT + 16 * a + 4 * q
-                nc.sync.dma_start(
-                    out=v2_s[a][:].bitcast(I32)[32 * q : 32 * q + 4, :],
-                    in_=v2_s_listed[:].bitcast(I32)[first : first + 4, :],
+                row = 32 * q + PLANE_AT[a]
+                if (a, row) != (0, first):
+                    nc.sync.dma_start(
+                        out=planes[a][:].bitcast(I32)[row : row + 4, :],
+                        in_=planes[0][:].bitcast(I32)[first : first + 4, :],
+                    )
+
+        place_planes(0)
+        nc.sync.dma_start(out=v2_tab[1][:], in_=words(tab2_words, 1))
+        place_planes(1)
+
+        v_listed = [kept([P, S], U32, f"v_listed{a}") for a in range(k_passes)]
+        v_c = [kept([P, i_passes, PACK, P], U32, f"v_c{a}") for a in range(k_passes)]
+        v2_c = {}
+
+        def gather_v(a):
+            for b in range(i_passes):
+                nc.vector.tensor_copy(
+                    v_listed[a][:, PASS * b : PASS * (b + 1)],
+                    v_tab[a][:].bitcast(U32).indirect(entries(idx, PASS * b, PASS)),
+                )
+            for b in range(i_passes):
+                nc.vector.tensor_copy(
+                    v_c[a][:, b].bitcast(I32).rearrange("p t (g r) -> p g t r", r=RUN),
+                    v_listed[a][:, PASS * b : PASS * (b + 1)]
+                    .bitcast(I32)
+                    .rearrange("p (g r t) -> p g t r", r=RUN, t=PACK),
                 )
 
-        def place_v_scales(a, q):
-            first = ROWS_AT + 16 * a + 4 * q
-            row = 32 * q + V_PLANE_AT[a]
-            nc.sync.dma_start(
-                out=v_s[a][:].bitcast(I32)[row : row + 4, :], in_=v_s[0][:].bitcast(I32)[first : first + 4, :]
-            )
-
-        gather_v_scales(0)
-        gather_v_scales(1)
-        order_v_scales(0)
-        order_v_scales(1)
-        moves = [(a, q) for a in range(k_passes) for q in range(QUADS) if (a, q) != (0, QUADS - 1)]
-        for a, q in moves[:-1]:
-            place_v_scales(a, q)
-        nc.sync.dma_start(out=v_tab[1][:], in_=words(tab_words, 1))
-        place_v_scales(*moves[-1])
-        nc.vector.tensor_copy(v2_s_listed[:], v2_tab_s[:].bitcast(U8).indirect(idx2[:]))
-        place_v2_scales(0)
-        nc.sync.dma_start(out=v2_tab[1][:], in_=words(tab2_words, 1))
-        nc.sync.dma_start(out=res_t[:, :, 0:PACK], in_=res.rearrange("(b p t) -> p b t", p=P, t=PACK))
-        place_v2_scales(1)
-        nc.scalar.mul(neg_res[:], res_t[:, :, 0:PACK], -1.0)
-        wt_half = keep.tile([P, i_passes, PACK], F32, name="wt_half")
-        wt_size = keep.tile([P, i_passes, PACK], F32, name="wt_size")
-        wt_sign = keep.tile([P, i_passes, PACK], BF16, name="wt_sign")
-        neg_level = keep.tile([P, i_passes, PACK], F32, name="neg_level")
-
-        gather_v_words(0, 0)
-        gather_v_words(0, 1)
-        order_v_words(0, 0)
-        order_v_words(0, 1)
+        gather_v(0)
         wo_raw = [staged([P, PACK, N], F32, f"wo_raw{b}", at) for b, at in enumerate([at_wo0, at_wo1])]
         wi_c = staged([P, i_passes, N // 2], I32, "wi_c", at_wi)
         wi_s = staged([P, i_passes, N // 4], I32, "wi_s", at_wi_s)
@@ -182,192 +164,216 @@ def tile_list_two_sided_match_kernel(
                 out=wo_raw[b][:], in_=wo[b * PASS : (b + 1) * PASS, :].rearrange("(p t) n -> p t n", t=PACK)
             )
 
-        nc.sync.dma_start(out=wt_t[:, :, 0:PACK], in_=wt.rearrange("(b p t) -> p b t", p=P, t=PACK))
         load_wo(0)
-        load_wo(1)
         nc.sync.dma_start(out=wi_c[:], in_=wi_words.bitcast(I32).rearrange("b p w -> p b w"))
         for q in range(QUADS):
             nc.sync.dma_start(
                 out=wi_s[32 * q : 32 * q + 4, :, :],
                 in_=wi_scales.bitcast(I32)[:, 4 * q : 4 * q + 4, :].rearrange("b r w -> r b w"),
             )
-        gather_v2_words(0, 1)
-        gather_v2_words(0, 0)
-        gather_v_words(1, 0)
-        gather_v_words(1, 1)
-        order_v_words(1, 0)
-        order_v_words(1, 1)
-        gather_v2_words(1, 0)
-        gather_v2_words(1, 1)
-        nc.scalar.activation(wt_size[:], wt_t[:, :, 0:PACK], ACT.Abs, scale=0.5)
-        nc.scalar.activation(wt_sign[:], wt_t[:, :, 0:PACK], ACT.Sign)
-        nc.scalar.mul(wt_half[:], wt_t[:, :, 0:PACK], 0.5)
-        nc.vector.tensor_tensor(neg_level[:], neg_res[:], wt_size[:], MULT)
 
-        z_c = {}
-        z_s = {}
-        z_bf = {}
-        above = {}
-        fit = {}
-        wo_bf = [keep.tile([P, N * PACK], BF16, name=f"wo_bf{b}", align_bytes=64) for b in range(i_passes)]
-        wo_c = [keep.tile([P, N], U32, name=f"wo_c{b}", align_bytes=64) for b in range(i_passes)]
-        wo_s = [keep.tile([P, N], U8, name=f"wo_s{b}", align_bytes=64) for b in range(i_passes)]
+        def gather_v2(a, first, count, offset=None):
+            shape, name = [P, CHUNK * count], f"v2_c{a}_{first}"
+            picked = kept(shape, U32, name) if offset is None else staged(shape, U32, name, offset)
+            nc.vector.tensor_copy(
+                picked[:], v2_tab[a][:].bitcast(U32).indirect(entries(idx2, CHUNK * first, CHUNK * count))
+            )
+            for c in range(count):
+                v2_c[a, first + c] = picked[:, CHUNK * c : CHUNK * (c + 1)]
 
-        def fit_pass(h, b, t, a):
+        fit, above, z_bf, z_c, z_s, score, chance = {}, {}, {}, {}, {}, {}, {}
+        wo_bf = [kept([P, N * PACK], BF16, f"wo_bf{b}") for b in range(i_passes)]
+        wo_c = [kept([P, N], U32, f"wo_c{b}") for b in range(i_passes)]
+        wo_s = [kept([P, N], U8, f"wo_s{b}") for b in range(i_passes)]
+
+        def bank(number):
+            return psum.tile([P, 2, CHUNK], F32, name=f"bank{number}")
+
+        def fit_passes(c, b, u, a):
             if a == 0:
-                fit[h, b, t] = psum.tile([P, BANK], F32, name=f"bank{PACK * b * (1 - h) + t}")
-            nc.tensor.matmul_mx(
-                out=fit[h, b, t][:],
-                lhsT=v_c[a][b][:, t, :].bitcast(FP8X4),
-                lhsT_scale=v_s[a][V_PLANE_AT[a] :, PASS * b + P * t : PASS * b + P * (t + 1)],
-                rhs=v2_c[a, h][:].bitcast(FP8X4),
-                rhs_scale=v2_s[a][:, BANK * h : BANK * (h + 1)],
-                start=(a == 0),
-                stop=(a == k_passes - 1),
-            )
-
-        def surplus(h, b):
-            above[h, b] = keep.tile([P, PACK, BANK], F32, name=f"above{h}_{b}", align_bytes=64)
-            for t in range(PACK):
-                fit_pass(h, b, t, 1)
-                nc.scalar.activation(above[h, b][:, t, :], fit[h, b, t][:], ACT.Relu, bias=neg_res[:, b, t : t + 1])
-
-        def weigh(h, b):
-            if b == 0:
-                z_bf[h, b] = staged([P, BANK * PACK], BF16, "z_bf_first", at_wo0)
-            else:
-                z_bf[h, b] = keep.tile([P, BANK * PACK], BF16, name=f"z_bf{h}_{b}", align_bytes=64)
-            nc.vector.tensor_tensor(
-                z_bf[h, b][:].rearrange("p (c r t) -> p c t r", r=RUN, t=PACK),
-                above[h, b][:].rearrange("p t (c r) -> p c t r", r=RUN),
-                wt_half[:, b, :].unsqueeze(1).unsqueeze(3).to_broadcast([P, BANK // RUN, PACK, RUN]),
-                MULT,
-            )
-
-        def paired_surplus(h, b):
-            if (h, b) == (1, 1):
-                above[h, b] = staged([P, 2, BANK, 2], BF16, "above_last", at_above)
-            else:
-                above[h, b] = keep.tile([P, 2, BANK, 2], BF16, name=f"above{h}_{b}", align_bytes=64)
-            for t in range(PACK):
-                for a in range(1 - h, k_passes):
-                    fit_pass(h, b, t, a)
-                nc.scalar.activation(
-                    above[h, b][:, t // 2, :, t % 2],
-                    fit[h, b, t][:],
-                    ACT.Relu,
-                    bias=neg_level[:, b, t : t + 1],
-                    scale=wt_size[:, b, t : t + 1],
+                fit[c, b, u] = bank(4 * (c == 1) + 2 * b + u)
+            for e in range(2):
+                t = 2 * u + e
+                nc.tensor.matmul_mx(
+                    out=fit[c, b, u][:, e, :],
+                    lhsT=v_c[a][:, b, t, :].bitcast(FP8X4),
+                    lhsT_scale=planes[a][PLANE_AT[a] :, PASS * b + P * t : PASS * b + P * (t + 1)],
+                    rhs=v2_c[a, c].bitcast(FP8X4),
+                    rhs_scale=planes[a][PLANE_AT[a] :, S + CHUNK * c : S + CHUNK * (c + 1)],
+                    start=(a, e) == (0, 0),
+                    stop=(a, e) == (k_passes - 1, 1),
                 )
 
-        def give_sign(h, b):
-            if h:
-                z_bf[h, b] = staged([P, BANK * PACK], BF16, f"z_bf{h}_{b}", at_z)
-            else:
-                z_bf[h, b] = keep.tile([P, BANK * PACK], BF16, name=f"z_bf{h}_{b}", align_bytes=64)
-            nc.vector.tensor_tensor(
-                z_bf[h, b][:].rearrange("p (c u e) -> p c u e", u=2, e=2),
-                above[h, b][:].rearrange("p u c e -> p c u e"),
-                wt_sign[:, b, :].rearrange("p (u e) -> p u e", e=2).unsqueeze(1).to_broadcast([P, BANK, 2, 2]),
-                MULT,
-            )
+        def fit_bank(c, b, u):
+            for a in range(k_passes):
+                fit_passes(c, b, u, a)
 
-        def quantise_z(h, b):
-            z_c[h, b] = keep.tile([P, BANK], U32, name=f"z_c{h}_{b}", align_bytes=64)
-            z_s[h, b] = keep.tile([P, BANK], U8, name=f"z_s{h}_{b}", align_bytes=64)
-            nc.vector.quantize_mx(out=z_c[h, b][:].bitcast(FP8X4), scales=z_s[h, b][:], in_=z_bf[h, b][:])
+        def surplus(c, b, u):
+            if c < PLAIN_CHUNKS:
+                if u == 0:
+                    above[c, b] = kept([P, PACK, CHUNK], F32, f"above{c}_{b}")
+                for e in range(2):
+                    t = 2 * u + e
+                    nc.scalar.activation(
+                        above[c, b][:, t, :], fit[c, b, u][:, e, :], ACT.Relu, bias=neg_res[:, b, t : t + 1]
+                    )
+            else:
+                if u == 0:
+                    above[c, b] = kept([P, 2, CHUNK, 2], BF16, f"above{c}_{b}")
+                for e in range(2):
+                    t = 2 * u + e
+                    nc.scalar.activation(
+                        above[c, b][:, u, :, e],
+                        fit[c, b, u][:, e, :],
+                        ACT.Relu,
+                        bias=neg_level[:, b, t : t + 1],
+                        scale=wt_size[:, b, t : t + 1],
+                    )
+
+        def weigh(c, b):
+            z_bf[c, b] = kept([P, CHUNK * PACK], BF16, f"z_bf{c}_{b}")
+            if c < PLAIN_CHUNKS:
+                nc.vector.tensor_tensor(
+                    z_bf[c, b][:].rearrange("p (j r t) -> p j t r", r=RUN, t=PACK),
+                    above[c, b][:].rearrange("p t (j r) -> p j t r", r=RUN),
+                    wt_half[:, b, :].unsqueeze(1).unsqueeze(3).to_broadcast([P, CHUNK // RUN, PACK, RUN]),
+                    MULT,
+                )
+            else:
+                nc.vector.tensor_tensor(
+                    z_bf[c, b][:].rearrange("p (j u e) -> p j u e", u=2, e=2),
+                    above[c, b][:].rearrange("p u j e -> p j u e"),
+                    wt_sign[:, b, :].rearrange("p (u e) -> p u e", e=2).unsqueeze(1).to_broadcast([P, CHUNK, 2, 2]),
+                    MULT,
+                )
+
+        def quantise_z(c, b):
+            z_c[c, b] = kept([P, CHUNK], U32, f"z_c{c}_{b}")
+            z_s[c, b] = kept([P, CHUNK], U8, f"z_s{c}_{b}")
+            nc.vector.quantize_mx(out=z_c[c, b][:].bitcast(FP8X4), scales=z_s[c, b][:], in_=z_bf[c, b][:])
 
         def round_wo(b):
             nc.vector.tensor_copy(
-                wo_bf[b][:].rearrange("p (c r t) -> p c t r", r=4, t=PACK),
-                wo_raw[b][:].rearrange("p t (c r) -> p c t r", r=4),
+                wo_bf[b][:].rearrange("p (n r t) -> p n t r", r=RUN, t=PACK),
+                wo_raw[b][:].rearrange("p t (n r) -> p n t r", r=RUN),
             )
 
         def quantise_wo(b):
             nc.vector.quantize_mx(out=wo_c[b][:].bitcast(FP8X4), scales=wo_s[b][:], in_=wo_bf[b][:])
 
-        chance = {}
-        score = {}
-
-        def interest_pass(h, n, b):
+        def score_passes(kind, c, v, b, number=None):
             if b == 0:
-                score["interest", h, n] = psum.tile([P, BANK], F32, name=f"bank{INTEREST_BANK[h][n]}")
-            nc.tensor.matmul_mx(
-                out=score["interest", h, n][:],
-                lhsT=wi_c[:, b, :].bitcast(U8)[:, 2 * P * n : 2 * P * (n + 1)].bitcast(FP4X4),
-                lhsT_scale=wi_s[:, b, :].bitcast(U8)[:, P * n : P * (n + 1)],
-                rhs=z_c[h, b][:].bitcast(FP8X4),
-                rhs_scale=z_s[h, b][:],
-                start=(b == 0),
-                stop=(b == i_passes - 1),
+                score[kind, c, v] = bank(number)
+            for e in range(2):
+                n = 2 * v + e
+                if kind == "interest":
+                    codes = wi_c[:, b, :].bitcast(U8)[:, 2 * P * n : 2 * P * (n + 1)].bitcast(FP4X4)
+                    scales = wi_s[:, b, :].bitcast(U8)[:, P * n : P * (n + 1)]
+                else:
+                    codes = wo_c[b][:, P * n : P * (n + 1)].bitcast(FP8X4)
+                    scales = wo_s[b][:, P * n : P * (n + 1)]
+                nc.tensor.matmul_mx(
+                    out=score[kind, c, v][:, e, :],
+                    lhsT=codes,
+                    lhsT_scale=scales,
+                    rhs=z_c[c, b][:].bitcast(FP8X4),
+                    rhs_scale=z_s[c, b][:],
+                    start=(b, e) == (0, 0),
+                    stop=(b, e) == (i_passes - 1, 1),
+                )
+
+        def scores(kind, c, b, first_bank=0):
+            for v in range(2):
+                score_passes(kind, c, v, b, first_bank + v)
+
+        def sigmoid(c, v):
+            chance[c, v] = kept([P, 2, CHUNK], F32, f"chance{c}_{v}")
+            nc.scalar.activation(chance[c, v][:], score["interest", c, v][:], ACT.Tanh)
+
+        def finish(c, v):
+            result = kept([P, 2, CHUNK], F32, f"result{c}_{v}")
+            nc.vector.scalar_tensor_tensor(result[:], chance[c, v][:], 1.0, score["offer", c, v][:], ADD, MULT)
+            nc.sync.dma_start(
+                out=out[2 * P * v : 2 * P * (v + 1), CHUNK * c : CHUNK * (c + 1)].rearrange("(e p) j -> p e j", p=P),
+                in_=result[:],
             )
 
-        def sigmoid(h, n):
-            chance[h, n] = keep.tile([P, BANK], F32, name=f"chance{h}_{n}")
-            nc.scalar.activation(chance[h, n][:], score["interest", h, n][:], ACT.Tanh)
-
-        def offer_pass(h, n, b, first):
-            if b == first:
-                score["offer", h, n] = psum.tile([P, BANK], F32, name=f"bank{OFFER_BANK[h][n]}")
-            nc.tensor.matmul_mx(
-                out=score["offer", h, n][:],
-                lhsT=wo_c[b][:, P * n : P * (n + 1)].bitcast(FP8X4),
-                lhsT_scale=wo_s[b][:, P * n : P * (n + 1)],
-                rhs=z_c[h, b][:].bitcast(FP8X4),
-                rhs_scale=z_s[h, b][:],
-                start=(b == first),
-                stop=(b != first),
-            )
-
-        def finish(h, n):
-            if h:
-                result = keep.tile([P, BANK], F32, name=f"result{h}_{n}")
-            else:
-                result = staged([P, BANK], F32, f"result{h}_{n}", [at_result0, at_result1, at_result2, at_z][n])
-            nc.vector.scalar_tensor_tensor(result[:], chance[h, n][:], 1.0, score["offer", h, n][:], ADD, MULT)
-            nc.sync.dma_start(out=out[P * n : P * (n + 1), BANK * h : BANK * (h + 1)], in_=result[:])
-
-        for b in range(i_passes):
-            for t in range(PACK):
-                fit_pass(0, b, t, 0)
-        surplus(0, 0)
-        surplus(0, 1)
-        round_wo(0)
-        quantise_wo(0)
+        halves = [(b, u) for b in range(i_passes) for u in range(2)]
+        gather_v2(0, 2, 1)
+        gather_v2(0, 0, 2)
+        gather_v(1)
+        load_wo(1)
+        for c in range(2):
+            for b, u in halves:
+                fit_passes(c, b, u, 0)
+        gather_v2(1, 0, 1, at_first_picks)
+        for c in range(1, chunks):
+            gather_v2(1, c, 1)
+        for c in range(2):
+            for b, u in halves:
+                fit_passes(c, b, u, 1)
+        gather_v2(0, 3, 1, at_late_picks)
+        for c in range(2):
+            for b, u in halves:
+                surplus(c, b, u)
+        for b, u in halves:
+            fit_bank(2, b, u)
         weigh(0, 0)
+        round_wo(0)
         weigh(0, 1)
         quantise_z(0, 0)
-        paired_surplus(1, 0)
-        round_wo(1)
+        quantise_wo(0)
         quantise_z(0, 1)
+        scores("interest", 0, 0, 4)
+        scores("offer", 0, 0, 6)
+        scores("interest", 0, 1)
+        for b, u in halves:
+            surplus(2, b, u)
+            fit_bank(3, b, u)
+        round_wo(1)
+        weigh(1, 0)
         quantise_wo(1)
-        paired_surplus(1, 1)
-        for b in range(i_passes):
-            for n in range(n_tiles):
-                interest_pass(0, n, b)
-        for n in range(n_tiles):
-            for b in reversed(range(i_passes)):
-                offer_pass(0, n, b, 1)
-        give_sign(1, 0)
+        scores("offer", 0, 1)
+        sigmoid(0, 0)
+        sigmoid(0, 1)
+        weigh(1, 1)
         quantise_z(1, 0)
-        give_sign(1, 1)
-        for n in range(n_tiles):
-            sigmoid(0, n)
+        finish(0, 0)
         quantise_z(1, 1)
-        for n in range(2):
-            interest_pass(1, n, 0)
-            offer_pass(1, n, 0, 0)
-        for n in range(n_tiles):
-            finish(0, n)
-        for n in range(2):
-            interest_pass(1, n, 1)
-            offer_pass(1, n, 1, 0)
-        for n in range(2, n_tiles):
-            for b in range(i_passes):
-                interest_pass(1, n, b)
-        for n in range(2, n_tiles):
-            for b in range(i_passes):
-                offer_pass(1, n, b, 0)
-        for n in range(n_tiles):
-            sigmoid(1, n)
-            finish(1, n)
+        finish(0, 1)
+        surplus(3, 0, 0)
+        surplus(3, 0, 1)
+        for b in range(i_passes):
+            scores("interest", 1, b, 4)
+        for b in range(i_passes):
+            scores("offer", 1, b, 6)
+        sigmoid(1, 0)
+        sigmoid(1, 1)
+        surplus(3, 1, 0)
+        surplus(3, 1, 1)
+        weigh(2, 0)
+        weigh(2, 1)
+        quantise_z(2, 0)
+        weigh(3, 0)
+        quantise_z(2, 1)
+        for b in range(i_passes):
+            scores("interest", 2, b, 0)
+        for b in range(i_passes):
+            scores("offer", 2, b, 4)
+        finish(1, 0)
+        quantise_z(3, 0)
+        finish(1, 1)
+        weigh(3, 1)
+        sigmoid(2, 0)
+        sigmoid(2, 1)
+        finish(2, 0)
+        quantise_z(3, 1)
+        finish(2, 1)
+        scores("interest", 3, 0, 6)
+        scores("offer", 3, 0, 2)
+        for v in range(2):
+            score_passes("interest", 3, v, 1)
+            score_passes("offer", 3, v, 1)
+        for v in range(2):
+            sigmoid(3, v)
+            finish(3, v)

@@ -60,6 +60,8 @@ def tile_list_two_sided_match_kernel(
 
         at_v2_1 = 0
         at_v2s_listed = at_v2_1 + 4 * T2 - LAP
+        at_res = at_v2s_listed + LAP
+        at_wt = at_res + LAP
         at_v0 = at_v2s_listed + S2
         at_wi = at_v0
         at_wi_s = at_wi + 2 * i_passes * N
@@ -75,30 +77,14 @@ def tile_list_two_sided_match_kernel(
             nc.vector.memset(window[0:ROWS_AT, :], 0)
         v_tab = [staged([P, T], I32, f"v_tab{a}", at) for a, at in enumerate([at_v0, at_v1])]
         v2_tab = [kept([P, T2], I32, "v2_tab0"), staged([P, T2], I32, "v2_tab1", at_v2_1)]
-        res_t = kept([P, i_passes, 2 * PACK], F32, "res_t")
-        wt_t = kept([P, i_passes, 2 * PACK], F32, "wt_t")
 
-        nc.sync.dma_start(out=v_tab_s[ROWS_AT:P, :], in_=tab_scales.bitcast(I32).rearrange("a q w -> (a q) w"))
+        nc.scalar.dma_start(out=v_tab_s[ROWS_AT:P, :], in_=tab_scales.bitcast(I32).rearrange("a q w -> (a q) w"))
         nc.sync.dma_start(out=idx[:], in_=offs)
         nc.sync.dma_start(out=v2_tab_s[ROWS_AT:P, :], in_=tab2_scales.bitcast(I32).rearrange("a q w -> (a q) w"))
         nc.sync.dma_start(out=idx2[:], in_=offs2)
         nc.sync.dma_start(out=v_tab[0][:], in_=words(tab_words, 0))
         nc.sync.dma_start(out=v2_tab[0][:], in_=words(tab2_words, 0))
         nc.sync.dma_start(out=v_tab[1][:], in_=words(tab_words, 1))
-        nc.scalar.dma_start(out=res_t[:, :, 0:PACK], in_=res.rearrange("(b p t) -> p b t", p=P, t=PACK))
-        nc.scalar.dma_start(out=wt_t[:, :, 0:PACK], in_=wt.rearrange("(b p t) -> p b t", p=P, t=PACK))
-
-        neg_res = kept([P, i_passes, PACK], F32, "neg_res")
-        wt_half = kept([P, i_passes, PACK], F32, "wt_half")
-        wt_size = kept([P, i_passes, PACK], F32, "wt_size")
-        wt_sign = kept([P, i_passes, PACK], BF16, "wt_sign")
-        neg_level = kept([P, i_passes, PACK], F32, "neg_level")
-        nc.scalar.mul(neg_res[:], res_t[:, :, 0:PACK], -1.0)
-        nc.scalar.activation(wt_size[:], wt_t[:, :, 0:PACK], ACT.Abs, scale=0.5)
-        nc.scalar.activation(wt_sign[:], wt_t[:, :, 0:PACK], ACT.Sign)
-        nc.scalar.mul(wt_half[:], wt_t[:, :, 0:PACK], 0.5)
-        nc.gpsimd.tensor_tensor(neg_level[:], neg_res[:], wt_size[:], MULT)
-
         vs_listed = kept([P, S], U8, "vs_listed")
         v2s_listed = staged([P, S2], U8, "v2s_listed", at_v2s_listed)
         planes = [kept([P, S + S2], U8, f"planes{a}") for a in range(k_passes)]
@@ -134,7 +120,22 @@ def tile_list_two_sided_match_kernel(
 
         place_planes(0)
         nc.sync.dma_start(out=v2_tab[1][:], in_=words(tab2_words, 1))
+        res_t = staged([P, i_passes, 2 * PACK], F32, "res_t", at_res)
+        wt_t = staged([P, i_passes, 2 * PACK], F32, "wt_t", at_wt)
+        nc.sync.dma_start(out=res_t[:, :, 0:PACK], in_=res.rearrange("(b p t) -> p b t", p=P, t=PACK))
         place_planes(1)
+        nc.sync.dma_start(out=wt_t[:, :, 0:PACK], in_=wt.rearrange("(b p t) -> p b t", p=P, t=PACK))
+        neg_res = kept([P, i_passes, PACK], F32, "neg_res")
+        wt_half = kept([P, i_passes, PACK], F32, "wt_half")
+        wt_size = kept([P, i_passes, PACK], F32, "wt_size")
+        wt_sign = kept([P, i_passes, PACK], BF16, "wt_sign")
+        neg_level = kept([P, i_passes, PACK], F32, "neg_level")
+        nc.scalar.mul(neg_res[:], res_t[:, :, 0:PACK], -1.0)
+        nc.scalar.activation(wt_size[:], wt_t[:, :, 0:PACK], ACT.Abs, scale=0.5)
+        nc.scalar.activation(wt_sign[:], wt_t[:, :, 0:PACK], ACT.Sign)
+        nc.scalar.mul(wt_half[:], wt_t[:, :, 0:PACK], 0.5)
+        nc.gpsimd.tensor_tensor(neg_level[:], neg_res[:], wt_size[:], MULT)
+
 
         v_listed = [kept([P, S], U32, f"v_listed{a}") for a in range(k_passes)]
         v_c = [kept([P, i_passes, PACK, P], U32, f"v_c{a}") for a in range(k_passes)]
@@ -341,39 +342,37 @@ def tile_list_two_sided_match_kernel(
         finish(0, 0)
         quantise_z(1, 1)
         finish(0, 1)
-        surplus(3, 0, 0)
-        surplus(3, 0, 1)
+        for b, u in halves:
+            surplus(3, b, u)
         for b in range(i_passes):
             scores("interest", 1, b, 4)
         for b in range(i_passes):
             scores("offer", 1, b, 6)
-        sigmoid(1, 0)
-        sigmoid(1, 1)
-        surplus(3, 1, 0)
-        surplus(3, 1, 1)
         weigh(2, 0)
         weigh(2, 1)
         quantise_z(2, 0)
         weigh(3, 0)
         quantise_z(2, 1)
+        quantise_z(3, 0)
         for b in range(i_passes):
             scores("interest", 2, b, 0)
         for b in range(i_passes):
-            scores("offer", 2, b, 4)
-        finish(1, 0)
-        quantise_z(3, 0)
-        finish(1, 1)
+            scores("offer", 2, b, 2)
         weigh(3, 1)
+        sigmoid(1, 0)
+        sigmoid(1, 1)
+        finish(1, 0)
+        quantise_z(3, 1)
+        finish(1, 1)
+        for b in range(i_passes):
+            scores("interest", 3, b, 4)
         sigmoid(2, 0)
         sigmoid(2, 1)
         finish(2, 0)
-        quantise_z(3, 1)
         finish(2, 1)
-        scores("interest", 3, 0, 6)
-        scores("offer", 3, 0, 2)
         for v in range(2):
-            score_passes("interest", 3, v, 1)
-            score_passes("offer", 3, v, 1)
+            for b in range(i_passes):
+                score_passes("offer", 3, v, b, 6 + v)
         for v in range(2):
             sigmoid(3, v)
             finish(3, v)

@@ -26,7 +26,11 @@ RUN = 4
 LIST_ROWS = 16
 ROWS_AT = 96
 PLANE_AT = [12, 0]
-PLAIN_CHUNKS = 2
+BANK = 512
+GROUPS = [(0, 256), (256, 512), (768, 256)]
+GROUP_OF = [0, 1, 1, 2]
+FIT_BANK = [[0, 2], [4, 0], [0, 4]]
+PLAIN = [(0, 0), (0, 1), (1, 0)]
 LAP = 64
 
 
@@ -36,7 +40,6 @@ def tile_list_two_sided_match_kernel(
     nc = tc.nc
     k_passes = K // PASS
     i_passes = S // PASS
-    chunks = S2 // CHUNK
 
     with ExitStack() as ctx:
         keep = ctx.enter_context(tc.tile_pool(name="keep", bufs=1))
@@ -63,12 +66,13 @@ def tile_list_two_sided_match_kernel(
         at_res = at_v2s_listed + LAP
         at_wt = at_res + LAP
         at_v0 = at_v2s_listed + S2
-        at_wi = at_v0
+        at_wo0 = at_v0
+        at_wi = at_v0 + 4 * T
         at_wi_s = at_wi + 2 * i_passes * N
-        at_wo0 = at_v0 + 4 * T - LAP
-        at_v1 = at_wo0 + 4 * PACK * N
-        at_wo1 = at_v1 + 4 * T - LAP
-        at_first_picks = at_wo1 + 4 * PACK * N
+        at_z_late = at_wi + 4 * S
+        at_v1 = at_z_late + 12 * CHUNK * PACK - LAP
+        at_wo1 = at_v1
+        at_first_picks = at_v1 + 4 * T
         at_late_picks = at_first_picks + 4 * CHUNK - LAP
 
         v_tab_s = kept([P, T // 4], I32, "v_tab_s")
@@ -134,10 +138,10 @@ def tile_list_two_sided_match_kernel(
         nc.scalar.activation(wt_size[:], wt_t[:, :, 0:PACK], ACT.Abs, scale=0.5)
         nc.scalar.activation(wt_sign[:], wt_t[:, :, 0:PACK], ACT.Sign)
         nc.scalar.mul(wt_half[:], wt_t[:, :, 0:PACK], 0.5)
-        nc.gpsimd.tensor_tensor(neg_level[:], neg_res[:], wt_size[:], MULT)
+        nc.vector.tensor_tensor(neg_level[:], neg_res[:], wt_size[:], MULT)
 
 
-        v_listed = [kept([P, S], U32, f"v_listed{a}") for a in range(k_passes)]
+        v_listed = [staged([P, S], U32, "v_listed0", at_wi), kept([P, S], U32, "v_listed1")]
         v_c = [kept([P, i_passes, PACK, P], U32, f"v_c{a}") for a in range(k_passes)]
         v2_c = {}
 
@@ -173,94 +177,112 @@ def tile_list_two_sided_match_kernel(
                 in_=wi_scales.bitcast(I32)[:, 4 * q : 4 * q + 4, :].rearrange("b r w -> r b w"),
             )
 
-        def gather_v2(a, first, count, offset=None):
-            shape, name = [P, CHUNK * count], f"v2_c{a}_{first}"
-            picked = kept(shape, U32, name) if offset is None else staged(shape, U32, name, offset)
-            nc.vector.tensor_copy(
-                picked[:], v2_tab[a][:].bitcast(U32).indirect(entries(idx2, CHUNK * first, CHUNK * count))
-            )
-            for c in range(count):
-                v2_c[a, first + c] = picked[:, CHUNK * c : CHUNK * (c + 1)]
+        def gather_v2(a, g, offset=None):
+            first, width = GROUPS[g]
+            shape, name = [P, width], f"v2_c{a}_{g}"
+            v2_c[a, g] = kept(shape, U32, name) if offset is None else staged(shape, U32, name, offset)
+            nc.vector.tensor_copy(v2_c[a, g][:], v2_tab[a][:].bitcast(U32).indirect(entries(idx2, first, width)))
 
+        z_late, result = [], {}
         fit, above, z_bf, z_c, z_s, score, chance = {}, {}, {}, {}, {}, {}, {}
         wo_bf = [kept([P, N * PACK], BF16, f"wo_bf{b}") for b in range(i_passes)]
         wo_c = [kept([P, N], U32, f"wo_c{b}") for b in range(i_passes)]
         wo_s = [kept([P, N], U8, f"wo_s{b}") for b in range(i_passes)]
 
-        def bank(number):
-            return psum.tile([P, 2, CHUNK], F32, name=f"bank{number}")
+        def bank(number, width=CHUNK):
+            return psum.tile([P, BANK // width, width], F32, name=f"bank{number}")
 
-        def fit_passes(c, b, u, a):
+        def fit_passes(g, b, s, a):
+            width = GROUPS[g][1]
+            share = BANK // width
             if a == 0:
-                fit[c, b, u] = bank(4 * (c == 1) + 2 * b + u)
-            for e in range(2):
-                t = 2 * u + e
+                fit[g, b, s] = bank(FIT_BANK[g][b] + s, width)
+            for e in range(share):
+                t = share * s + e
                 nc.tensor.matmul_mx(
-                    out=fit[c, b, u][:, e, :],
+                    out=fit[g, b, s][:, e, :],
                     lhsT=v_c[a][:, b, t, :].bitcast(FP8X4),
                     lhsT_scale=planes[a][PLANE_AT[a] :, PASS * b + P * t : PASS * b + P * (t + 1)],
-                    rhs=v2_c[a, c].bitcast(FP8X4),
-                    rhs_scale=planes[a][PLANE_AT[a] :, S + CHUNK * c : S + CHUNK * (c + 1)],
+                    rhs=v2_c[a, g][:].bitcast(FP8X4),
+                    rhs_scale=planes[a][PLANE_AT[a] :, S + GROUPS[g][0] : S + GROUPS[g][0] + width],
                     start=(a, e) == (0, 0),
-                    stop=(a, e) == (k_passes - 1, 1),
+                    stop=(a, e) == (k_passes - 1, share - 1),
                 )
 
-        def fit_bank(c, b, u):
-            for a in range(k_passes):
-                fit_passes(c, b, u, a)
+        def banks_of(g):
+            return range(PACK * GROUPS[g][1] // BANK)
 
-        def surplus(c, b, u):
-            if c < PLAIN_CHUNKS:
-                if u == 0:
-                    above[c, b] = kept([P, PACK, CHUNK], F32, f"above{c}_{b}")
-                for e in range(2):
-                    t = 2 * u + e
+        def fit_bank(g, b, s):
+            for a in range(k_passes):
+                fit_passes(g, b, s, a)
+
+        def surplus(g, b, s):
+            width = GROUPS[g][1]
+            share = BANK // width
+            plain = (g, b) in PLAIN
+            if s == 0:
+                shape, dtype = ([P, PACK, width], F32) if plain else ([P, 2, width, 2], BF16)
+                above[g, b] = kept(shape, dtype, f"above{g}_{b}")
+            for e in range(share):
+                t = share * s + e
+                if plain:
                     nc.scalar.activation(
-                        above[c, b][:, t, :], fit[c, b, u][:, e, :], ACT.Relu, bias=neg_res[:, b, t : t + 1]
+                        above[g, b][:, t, :], fit[g, b, s][:, e, :], ACT.Relu, bias=neg_res[:, b, t : t + 1]
                     )
-            else:
-                if u == 0:
-                    above[c, b] = kept([P, 2, CHUNK, 2], BF16, f"above{c}_{b}")
-                for e in range(2):
-                    t = 2 * u + e
+                else:
                     nc.scalar.activation(
-                        above[c, b][:, u, :, e],
-                        fit[c, b, u][:, e, :],
+                        above[g, b][:, t // 2, :, t % 2],
+                        fit[g, b, s][:, e, :],
                         ACT.Relu,
                         bias=neg_level[:, b, t : t + 1],
                         scale=wt_size[:, b, t : t + 1],
                     )
 
         def weigh(c, b):
-            z_bf[c, b] = kept([P, CHUNK * PACK], BF16, f"z_bf{c}_{b}")
-            if c < PLAIN_CHUNKS:
+            if c:
+                at = CHUNK * PACK * (i_passes * (c - 1) + b)
+                z_bf[c, b] = z_late[0][:, at : at + CHUNK * PACK]
+            else:
+                z_bf[c, b] = kept([P, CHUNK * PACK], BF16, f"z_bf{c}_{b}")[:]
+            g = GROUP_OF[c]
+            cols = slice(CHUNK * c - GROUPS[g][0], CHUNK * (c + 1) - GROUPS[g][0])
+            if (g, b) in PLAIN:
                 nc.vector.tensor_tensor(
-                    z_bf[c, b][:].rearrange("p (j r t) -> p j t r", r=RUN, t=PACK),
-                    above[c, b][:].rearrange("p t (j r) -> p j t r", r=RUN),
+                    z_bf[c, b].rearrange("p (j r t) -> p j t r", r=RUN, t=PACK),
+                    above[g, b][:, :, cols].rearrange("p t (j r) -> p j t r", r=RUN),
                     wt_half[:, b, :].unsqueeze(1).unsqueeze(3).to_broadcast([P, CHUNK // RUN, PACK, RUN]),
                     MULT,
                 )
             else:
                 nc.vector.tensor_tensor(
-                    z_bf[c, b][:].rearrange("p (j u e) -> p j u e", u=2, e=2),
-                    above[c, b][:].rearrange("p u j e -> p j u e"),
+                    z_bf[c, b].rearrange("p (j u e) -> p j u e", u=2, e=2),
+                    above[g, b][:, :, cols, :].rearrange("p u j e -> p j u e"),
                     wt_sign[:, b, :].rearrange("p (u e) -> p u e", e=2).unsqueeze(1).to_broadcast([P, CHUNK, 2, 2]),
                     MULT,
                 )
 
         def quantise_z(c, b):
-            z_c[c, b] = kept([P, CHUNK], U32, f"z_c{c}_{b}")
+            if c == 0:
+                z_c[c, b] = staged([P, CHUNK], U32, f"z_c{c}_{b}", at_wo0 + 4 * CHUNK * b)
+            else:
+                z_c[c, b] = kept([P, CHUNK], U32, f"z_c{c}_{b}")
             z_s[c, b] = kept([P, CHUNK], U8, f"z_s{c}_{b}")
-            nc.vector.quantize_mx(out=z_c[c, b][:].bitcast(FP8X4), scales=z_s[c, b][:], in_=z_bf[c, b][:])
+            nc.vector.quantize_mx(out=z_c[c, b][:].bitcast(FP8X4), scales=z_s[c, b][:], in_=z_bf[c, b])
 
         def round_wo(b):
-            nc.vector.tensor_copy(
-                wo_bf[b][:].rearrange("p (n r t) -> p n t r", r=RUN, t=PACK),
-                wo_raw[b][:].rearrange("p t (n r) -> p n t r", r=RUN),
-            )
+            for v in range(2):
+                nc.vector.tensor_copy(
+                    wo_bf[b][:, 2 * N * v : 2 * N * (v + 1)].rearrange("p (n r t) -> p n t r", r=RUN, t=PACK),
+                    wo_raw[b][:, :, 2 * P * v : 2 * P * (v + 1)].rearrange("p t (n r) -> p n t r", r=RUN),
+                )
 
-        def quantise_wo(b):
-            nc.vector.quantize_mx(out=wo_c[b][:].bitcast(FP8X4), scales=wo_s[b][:], in_=wo_bf[b][:])
+        def quantise_wo(b, v):
+            cols = slice(2 * P * v, 2 * P * (v + 1))
+            nc.vector.quantize_mx(
+                out=wo_c[b][:, cols].bitcast(FP8X4),
+                scales=wo_s[b][:, cols],
+                in_=wo_bf[b][:, 2 * N * v : 2 * N * (v + 1)],
+            )
 
         def score_passes(kind, c, v, b, number=None):
             if b == 0:
@@ -291,88 +313,106 @@ def tile_list_two_sided_match_kernel(
             chance[c, v] = kept([P, 2, CHUNK], F32, f"chance{c}_{v}")
             nc.scalar.activation(chance[c, v][:], score["interest", c, v][:], ACT.Tanh)
 
-        def finish(c, v):
-            result = kept([P, 2, CHUNK], F32, f"result{c}_{v}")
-            nc.vector.scalar_tensor_tensor(result[:], chance[c, v][:], 1.0, score["offer", c, v][:], ADD, MULT)
-            nc.sync.dma_start(
-                out=out[2 * P * v : 2 * P * (v + 1), CHUNK * c : CHUNK * (c + 1)].rearrange("(e p) j -> p e j", p=P),
-                in_=result[:],
-            )
+        def store(c, first, tile):
+            rows = out[P * first : P * (first + tile.shape[1]), CHUNK * c : CHUNK * (c + 1)]
+            nc.sync.dma_start(out=rows.rearrange("(e p) j -> p e j", p=P), in_=tile)
 
-        halves = [(b, u) for b in range(i_passes) for u in range(2)]
-        gather_v2(0, 2, 1)
-        gather_v2(0, 0, 2)
+        def finish(c, v):
+            if c == 0:
+                if v == 0:
+                    result[c] = kept([P, 4, CHUNK], F32, "result0")
+                part = result[c][:, 2 * v : 2 * (v + 1), :]
+            else:
+                part = kept([P, 2, CHUNK], F32, f"result{c}_{v}")[:]
+            pieces = [slice(0, 1), slice(1, 2)] if (c, v) == (3, 1) else [slice(0, 2)]
+            for e in pieces:
+                nc.vector.scalar_tensor_tensor(
+                    part[:, e, :], chance[c, v][:, e, :], 1.0, score["offer", c, v][:, e, :], ADD, MULT
+                )
+                if c:
+                    store(c, 2 * v + e.start, part[:, e, :])
+            if (c, v) == (0, 1):
+                store(c, 0, result[c][:])
+
+        opened = [(0, 0), (0, 1), (1, 0)]
+        gather_v2(0, 1)
+        gather_v2(0, 0)
         gather_v(1)
         load_wo(1)
-        for c in range(2):
-            for b, u in halves:
-                fit_passes(c, b, u, 0)
-        gather_v2(1, 0, 1, at_first_picks)
-        for c in range(1, chunks):
-            gather_v2(1, c, 1)
-        for c in range(2):
-            for b, u in halves:
-                fit_passes(c, b, u, 1)
-        gather_v2(0, 3, 1, at_late_picks)
-        for c in range(2):
-            for b, u in halves:
-                surplus(c, b, u)
-        for b, u in halves:
-            fit_bank(2, b, u)
+        for g, b in opened:
+            for s in banks_of(g):
+                fit_passes(g, b, s, 0)
+        gather_v2(1, 0, at_first_picks)
+        gather_v2(1, 1)
+        gather_v2(1, 2)
+        for g, b in opened:
+            for s in banks_of(g):
+                fit_passes(g, b, s, 1)
+        gather_v2(0, 2, at_late_picks)
+        for g, b in opened:
+            for s in banks_of(g):
+                surplus(g, b, s)
+        for s in banks_of(1):
+            fit_bank(1, 1, s)
         weigh(0, 0)
-        round_wo(0)
         weigh(0, 1)
-        quantise_z(0, 0)
-        quantise_wo(0)
-        quantise_z(0, 1)
+        round_wo(0)
+        for b in range(i_passes):
+            quantise_wo(0, b)
+            quantise_z(0, b)
         scores("interest", 0, 0, 4)
         scores("offer", 0, 0, 6)
         scores("interest", 0, 1)
-        for b, u in halves:
-            surplus(2, b, u)
-            fit_bank(3, b, u)
+        for s in banks_of(1):
+            surplus(1, 1, s)
+        for s in banks_of(2):
+            fit_bank(2, 0, s)
         round_wo(1)
+        z_late.append(staged([P, 6 * CHUNK * PACK], BF16, "z_late", at_z_late))
+        quantise_wo(1, 0)
+        quantise_wo(1, 1)
         weigh(1, 0)
-        quantise_wo(1)
         scores("offer", 0, 1)
-        sigmoid(0, 0)
-        sigmoid(0, 1)
+        for v in range(2):
+            sigmoid(0, v)
+            fit_bank(2, 1, v)
         weigh(1, 1)
         quantise_z(1, 0)
-        finish(0, 0)
-        quantise_z(1, 1)
-        finish(0, 1)
-        for b, u in halves:
-            surplus(3, b, u)
-        for b in range(i_passes):
-            scores("interest", 1, b, 4)
-        for b in range(i_passes):
-            scores("offer", 1, b, 6)
         weigh(2, 0)
+        quantise_z(1, 1)
+        finish(0, 0)
         weigh(2, 1)
+        finish(0, 1)
+        for b in range(i_passes):
+            for s in banks_of(2):
+                surplus(2, b, s)
+        for b in range(i_passes):
+            scores("interest", 1, b, 2)
+        for b in range(i_passes):
+            scores("offer", 1, b, 0)
         quantise_z(2, 0)
         weigh(3, 0)
         quantise_z(2, 1)
-        quantise_z(3, 0)
-        for b in range(i_passes):
-            scores("interest", 2, b, 0)
-        for b in range(i_passes):
-            scores("offer", 2, b, 2)
+        scores("interest", 2, 0, 6)
+        scores("offer", 2, 0, 4)
+        scores("interest", 2, 1)
+        scores("offer", 2, 1)
         weigh(3, 1)
+        quantise_z(3, 0)
         sigmoid(1, 0)
         sigmoid(1, 1)
         finish(1, 0)
         quantise_z(3, 1)
         finish(1, 1)
-        for b in range(i_passes):
-            scores("interest", 3, b, 4)
+        scores("interest", 3, 0, 2)
         sigmoid(2, 0)
         sigmoid(2, 1)
         finish(2, 0)
         finish(2, 1)
         for v in range(2):
+            score_passes("interest", 3, v, 1)
             for b in range(i_passes):
-                score_passes("offer", 3, v, b, 6 + v)
+                score_passes("offer", 3, v, b, v)
         for v in range(2):
             sigmoid(3, v)
             finish(3, v)

@@ -29,8 +29,8 @@ PLANE_AT = [12, 0]
 BANK = 512
 GROUPS = [(0, 256), (256, 512), (768, 256)]
 GROUP_OF = [0, 1, 1, 2]
-FIT_BANK = [[0, 2], [4, 0], [0, 4]]
-PLAIN = [(0, 0), (0, 1), (1, 0)]
+FIT_BANK = [[0, 2], [4, 0], [0, 2]]
+PLAIN = [(0, 0), (1, 0)]
 LAP = 64
 
 
@@ -70,10 +70,11 @@ def tile_list_two_sided_match_kernel(
         at_wi = at_v0 + 4 * T
         at_wi_s = at_wi + 2 * i_passes * N
         at_z_late = at_wi + 4 * S
-        at_v1 = at_z_late + 12 * CHUNK * PACK - LAP
+        at_v1 = at_z_late + 10 * CHUNK * PACK - LAP
         at_wo1 = at_v1
         at_first_picks = at_v1 + 4 * T
         at_late_picks = at_first_picks + 4 * CHUNK - LAP
+        at_wo_bf = at_late_picks + 4 * CHUNK
 
         v_tab_s = kept([P, T // 4], I32, "v_tab_s")
         v2_tab_s = kept([P, T2 // 4], I32, "v2_tab_s")
@@ -185,7 +186,7 @@ def tile_list_two_sided_match_kernel(
 
         z_late, result = [], {}
         fit, above, z_bf, z_c, z_s, score, chance = {}, {}, {}, {}, {}, {}, {}
-        wo_bf = [kept([P, N * PACK], BF16, f"wo_bf{b}") for b in range(i_passes)]
+        wo_bf = [staged([P, N * PACK], BF16, "wo_bf0", at_wo_bf), kept([P, N * PACK], BF16, "wo_bf1")]
         wo_c = [kept([P, N], U32, f"wo_c{b}") for b in range(i_passes)]
         wo_s = [kept([P, N], U8, f"wo_s{b}") for b in range(i_passes)]
 
@@ -222,7 +223,10 @@ def tile_list_two_sided_match_kernel(
             plain = (g, b) in PLAIN
             if s == 0:
                 shape, dtype = ([P, PACK, width], F32) if plain else ([P, 2, width, 2], BF16)
-                above[g, b] = kept(shape, dtype, f"above{g}_{b}")
+                if (g, b) == (1, 1):
+                    above[g, b] = staged(shape, dtype, "above1_1", at_wo_bf)
+                else:
+                    above[g, b] = kept(shape, dtype, f"above{g}_{b}")
             for e in range(share):
                 t = share * s + e
                 if plain:
@@ -239,11 +243,13 @@ def tile_list_two_sided_match_kernel(
                     )
 
         def weigh(c, b):
-            if c:
-                at = CHUNK * PACK * (i_passes * (c - 1) + b)
-                z_bf[c, b] = z_late[0][:, at : at + CHUNK * PACK]
+            number = i_passes * c + b
+            if number > 2:
+                z_bf[c, b] = z_late[0][:, CHUNK * PACK * (number - 3) : CHUNK * PACK * (number - 2)]
+            elif number:
+                z_bf[c, b] = staged([P, CHUNK * PACK], BF16, f"z_bf{c}_{b}", at_wo0 + 8 * CHUNK * number)[:]
             else:
-                z_bf[c, b] = kept([P, CHUNK * PACK], BF16, f"z_bf{c}_{b}")[:]
+                z_bf[c, b] = kept([P, CHUNK * PACK], BF16, "z_bf0_0")[:]
             g = GROUP_OF[c]
             cols = slice(CHUNK * c - GROUPS[g][0], CHUNK * (c + 1) - GROUPS[g][0])
             if (g, b) in PLAIN:
@@ -264,6 +270,8 @@ def tile_list_two_sided_match_kernel(
         def quantise_z(c, b):
             if c == 0:
                 z_c[c, b] = staged([P, CHUNK], U32, f"z_c{c}_{b}", at_wo0 + 4 * CHUNK * b)
+            elif (c, b) == (1, 0):
+                z_c[c, b] = staged([P, CHUNK], U32, "z_c1_0", at_wo1 + 4 * CHUNK)
             else:
                 z_c[c, b] = kept([P, CHUNK], U32, f"z_c{c}_{b}")
             z_s[c, b] = kept([P, CHUNK], U8, f"z_s{c}_{b}")
@@ -285,7 +293,7 @@ def tile_list_two_sided_match_kernel(
             )
 
         def score_passes(kind, c, v, b, number=None):
-            if b == 0:
+            if number is not None:
                 score[kind, c, v] = bank(number)
             for e in range(2):
                 n = 2 * v + e
@@ -301,13 +309,17 @@ def tile_list_two_sided_match_kernel(
                     lhsT_scale=scales,
                     rhs=z_c[c, b][:].bitcast(FP8X4),
                     rhs_scale=z_s[c, b][:],
-                    start=(b, e) == (0, 0),
-                    stop=(b, e) == (i_passes - 1, 1),
+                    start=number is not None and e == 0,
+                    stop=number is None and e == 1,
                 )
 
-        def scores(kind, c, b, first_bank=0):
+        def scores(kind, c, b, first_bank=None):
             for v in range(2):
-                score_passes(kind, c, v, b, first_bank + v)
+                score_passes(kind, c, v, b, None if first_bank is None else first_bank + v)
+
+        def score_bank(kind, c, v, number, first):
+            score_passes(kind, c, v, first, number)
+            score_passes(kind, c, v, 1 - first)
 
         def sigmoid(c, v):
             chance[c, v] = kept([P, 2, CHUNK], F32, f"chance{c}_{v}")
@@ -355,48 +367,46 @@ def tile_list_two_sided_match_kernel(
         for s in banks_of(1):
             fit_bank(1, 1, s)
         weigh(0, 0)
-        weigh(0, 1)
         round_wo(0)
-        for b in range(i_passes):
-            quantise_wo(0, b)
-            quantise_z(0, b)
+        quantise_wo(0, 0)
+        weigh(0, 1)
+        quantise_wo(0, 1)
+        quantise_z(0, 0)
+        quantise_z(0, 1)
+        weigh(1, 0)
         scores("interest", 0, 0, 4)
         scores("offer", 0, 0, 6)
         scores("interest", 0, 1)
         for s in banks_of(1):
             surplus(1, 1, s)
-        for s in banks_of(2):
-            fit_bank(2, 0, s)
+            fit_bank(2, s // 2, s % 2)
         round_wo(1)
-        z_late.append(staged([P, 6 * CHUNK * PACK], BF16, "z_late", at_z_late))
+        z_late.append(staged([P, 5 * CHUNK * PACK], BF16, "z_late", at_z_late))
         quantise_wo(1, 0)
         quantise_wo(1, 1)
-        weigh(1, 0)
         scores("offer", 0, 1)
-        for v in range(2):
-            sigmoid(0, v)
-            fit_bank(2, 1, v)
-        weigh(1, 1)
-        quantise_z(1, 0)
-        weigh(2, 0)
-        quantise_z(1, 1)
-        finish(0, 0)
-        weigh(2, 1)
-        finish(0, 1)
+        sigmoid(0, 0)
+        sigmoid(0, 1)
         for b in range(i_passes):
             for s in banks_of(2):
                 surplus(2, b, s)
-        for b in range(i_passes):
-            scores("interest", 1, b, 2)
-        for b in range(i_passes):
-            scores("offer", 1, b, 0)
-        quantise_z(2, 0)
-        weigh(3, 0)
+        quantise_z(1, 0)
+        scores("interest", 1, 0, 4)
+        weigh(1, 1)
+        weigh(2, 1)
+        quantise_z(1, 1)
+        scores("interest", 1, 1)
+        for v in range(2):
+            score_bank("offer", 1, v, v, 1)
+        weigh(2, 0)
         quantise_z(2, 1)
-        scores("interest", 2, 0, 6)
-        scores("offer", 2, 0, 4)
-        scores("interest", 2, 1)
-        scores("offer", 2, 1)
+        finish(0, 0)
+        quantise_z(2, 0)
+        finish(0, 1)
+        for v in range(2):
+            score_bank("interest", 2, v, 6 + v, 1)
+            score_bank("offer", 2, v, 2 + v, 0)
+        weigh(3, 0)
         weigh(3, 1)
         quantise_z(3, 0)
         sigmoid(1, 0)
@@ -404,15 +414,14 @@ def tile_list_two_sided_match_kernel(
         finish(1, 0)
         quantise_z(3, 1)
         finish(1, 1)
-        scores("interest", 3, 0, 2)
+        scores("interest", 3, 0, 4)
         sigmoid(2, 0)
         sigmoid(2, 1)
         finish(2, 0)
         finish(2, 1)
         for v in range(2):
             score_passes("interest", 3, v, 1)
-            for b in range(i_passes):
-                score_passes("offer", 3, v, b, v)
+            score_bank("offer", 3, v, v, 1)
         for v in range(2):
             sigmoid(3, v)
             finish(3, v)

@@ -131,15 +131,13 @@ def tile_list_two_sided_match_kernel(
         place_planes(1)
         nc.sync.dma_start(out=wt_t[:, :, 0:PACK], in_=wt.rearrange("(b p t) -> p b t", p=P, t=PACK))
         neg_res = kept([P, i_passes, PACK], F32, "neg_res")
-        wt_half = kept([P, i_passes, PACK], F32, "wt_half")
         wt_size = kept([P, i_passes, PACK], F32, "wt_size")
         wt_sign = kept([P, i_passes, PACK], BF16, "wt_sign")
         neg_level = kept([P, i_passes, PACK], F32, "neg_level")
-        nc.scalar.mul(neg_res[:], res_t[:, :, 0:PACK], -1.0)
+        nc.scalar.mul(neg_res[:], res_t[:, :, 0:PACK], -0.5)
         nc.scalar.activation(wt_size[:], wt_t[:, :, 0:PACK], ACT.Abs, scale=0.5)
         nc.scalar.activation(wt_sign[:], wt_t[:, :, 0:PACK], ACT.Sign)
-        nc.scalar.mul(wt_half[:], wt_t[:, :, 0:PACK], 0.5)
-        nc.vector.tensor_tensor(neg_level[:], neg_res[:], wt_size[:], MULT)
+        nc.vector.scalar_tensor_tensor(neg_level[:], res_t[:, :, 0:PACK], -1.0, wt_size[:], MULT, MULT)
 
 
         v_listed = [staged([P, S], U32, "v_listed0", at_wi), kept([P, S], U32, "v_listed1")]
@@ -231,7 +229,7 @@ def tile_list_two_sided_match_kernel(
                 t = share * s + e
                 if plain:
                     nc.scalar.activation(
-                        above[g, b][:, t, :], fit[g, b, s][:, e, :], ACT.Relu, bias=neg_res[:, b, t : t + 1]
+                        above[g, b][:, t, :], fit[g, b, s][:, e, :], ACT.Relu, bias=neg_res[:, b, t : t + 1], scale=0.5
                     )
                 else:
                     nc.scalar.activation(
@@ -256,7 +254,7 @@ def tile_list_two_sided_match_kernel(
                 nc.vector.tensor_tensor(
                     z_bf[c, b].rearrange("p (j r t) -> p j t r", r=RUN, t=PACK),
                     above[g, b][:, :, cols].rearrange("p t (j r) -> p j t r", r=RUN),
-                    wt_half[:, b, :].unsqueeze(1).unsqueeze(3).to_broadcast([P, CHUNK // RUN, PACK, RUN]),
+                    wt_t[:, b, 0:PACK].unsqueeze(1).unsqueeze(3).to_broadcast([P, CHUNK // RUN, PACK, RUN]),
                     MULT,
                 )
             else:
@@ -402,13 +400,13 @@ def tile_list_two_sided_match_kernel(
         quantise_z(2, 1)
         finish(0, 0)
         quantise_z(2, 0)
+        weigh(3, 0)
         finish(0, 1)
         for v in range(2):
             score_bank("interest", 2, v, 6 + v, 1)
             score_bank("offer", 2, v, 2 + v, 0)
-        weigh(3, 0)
-        weigh(3, 1)
         quantise_z(3, 0)
+        weigh(3, 1)
         sigmoid(1, 0)
         sigmoid(1, 1)
         finish(1, 0)

@@ -390,21 +390,21 @@ def tile_list_two_sided_match_kernel(
                 surplus(2, b, s)
         quantise_z(1, 0)
         scores("interest", 1, 0, 4)
+        weigh(2, 0)
         weigh(1, 1)
-        weigh(2, 1)
+        quantise_z(2, 0)
         quantise_z(1, 1)
         scores("interest", 1, 1)
         for v in range(2):
             score_bank("offer", 1, v, v, 1)
-        weigh(2, 0)
-        quantise_z(2, 1)
+        weigh(2, 1)
         finish(0, 0)
-        quantise_z(2, 0)
+        quantise_z(2, 1)
         weigh(3, 0)
         finish(0, 1)
         for v in range(2):
-            score_bank("interest", 2, v, 6 + v, 1)
-            score_bank("offer", 2, v, 2 + v, 0)
+            score_bank("interest", 2, v, 6 + v, 0)
+            score_bank("offer", 2, v, 2 + v, 1)
         quantise_z(3, 0)
         weigh(3, 1)
         sigmoid(1, 0)

@@ -29,7 +29,7 @@ PLANE_AT = [12, 0]
 BANK = 512
 GROUPS = [(0, 256), (256, 512), (768, 256)]
 GROUP_OF = [0, 1, 1, 2]
-FIT_BANK = [[0, 2], [4, 0], [0, 2]]
+FIT_BANK = [[0, 2], [4, 0], [4, 0]]
 PLAIN = [(0, 0), (1, 0)]
 LAP = 64
 
@@ -223,6 +223,8 @@ def tile_list_two_sided_match_kernel(
                 shape, dtype = ([P, PACK, width], F32) if plain else ([P, 2, width, 2], BF16)
                 if (g, b) == (1, 1):
                     above[g, b] = staged(shape, dtype, "above1_1", at_wo_bf)
+                elif (g, b) == (2, 0):
+                    above[g, b] = staged(shape, dtype, "above2_0", at_wo0 + 8 * CHUNK)
                 else:
                     above[g, b] = kept(shape, dtype, f"above{g}_{b}")
             for e in range(share):
@@ -364,6 +366,8 @@ def tile_list_two_sided_match_kernel(
                 surplus(g, b, s)
         for s in banks_of(1):
             fit_bank(1, 1, s)
+        for s in banks_of(2):
+            fit_bank(2, 0, s)
         weigh(0, 0)
         round_wo(0)
         quantise_wo(0, 0)
@@ -372,39 +376,40 @@ def tile_list_two_sided_match_kernel(
         quantise_z(0, 0)
         quantise_z(0, 1)
         weigh(1, 0)
-        scores("interest", 0, 0, 4)
-        scores("offer", 0, 0, 6)
+        scores("interest", 0, 0, 6)
         scores("interest", 0, 1)
         for s in banks_of(1):
             surplus(1, 1, s)
-            fit_bank(2, s // 2, s % 2)
+        for s in banks_of(2):
+            fit_bank(2, 1, s)
         round_wo(1)
         z_late.append(staged([P, 5 * CHUNK * PACK], BF16, "z_late", at_z_late))
         quantise_wo(1, 0)
         quantise_wo(1, 1)
-        scores("offer", 0, 1)
+        for v in range(2):
+            score_bank("offer", 0, v, 2 + v, 1)
         sigmoid(0, 0)
         sigmoid(0, 1)
         for b in range(i_passes):
             for s in banks_of(2):
                 surplus(2, b, s)
         quantise_z(1, 0)
-        scores("interest", 1, 0, 4)
+        scores("interest", 1, 0, 6)
         weigh(2, 0)
         weigh(1, 1)
         quantise_z(2, 0)
         quantise_z(1, 1)
         scores("interest", 1, 1)
         for v in range(2):
-            score_bank("offer", 1, v, v, 1)
+            score_bank("offer", 1, v, 4 + v, 1)
         weigh(2, 1)
         finish(0, 0)
         quantise_z(2, 1)
         weigh(3, 0)
         finish(0, 1)
         for v in range(2):
-            score_bank("interest", 2, v, 6 + v, 0)
-            score_bank("offer", 2, v, 2 + v, 1)
+            score_bank("interest", 2, v, 2 + v, 0)
+            score_bank("offer", 2, v, v, 1)
         quantise_z(3, 0)
         weigh(3, 1)
         sigmoid(1, 0)
@@ -412,14 +417,14 @@ def tile_list_two_sided_match_kernel(
         finish(1, 0)
         quantise_z(3, 1)
         finish(1, 1)
-        scores("interest", 3, 0, 4)
+        scores("interest", 3, 0, 6)
         sigmoid(2, 0)
         sigmoid(2, 1)
         finish(2, 0)
         finish(2, 1)
         for v in range(2):
             score_passes("interest", 3, v, 1)
-            score_bank("offer", 3, v, v, 1)
+            score_bank("offer", 3, v, 4 + v, 1)
         for v in range(2):
             sigmoid(3, v)
             finish(3, v)

@@ -32,6 +32,7 @@ GROUP_OF = [0, 1, 1, 2]
 FIT_BANK = [[0, 2], [4, 0], [4, 0]]
 PLAIN = [(0, 0), (1, 0)]
 LAP = 64
+ROW_ALIGN = 256
 
 
 def tile_list_two_sided_match_kernel(
@@ -47,10 +48,10 @@ def tile_list_two_sided_match_kernel(
         psum = ctx.enter_context(tc.psum_pool(name="psum", bufs=1))
 
         def staged(shape, dtype, name, offset):
-            return stage.tile(shape, dtype, name=name, align_bytes=64, offset=offset)
+            return stage.tile(shape, dtype, name=name, align_bytes=64 if offset % ROW_ALIGN else ROW_ALIGN, offset=offset)
 
         def kept(shape, dtype, name):
-            return keep.tile(shape, dtype, name=name, align_bytes=64)
+            return keep.tile(shape, dtype, name=name, align_bytes=ROW_ALIGN)
 
         def words(table, a):
             return table[a].rearrange("p t i -> p (t i)").bitcast(I32)
@@ -65,11 +66,11 @@ def tile_list_two_sided_match_kernel(
         at_v2s_listed = at_v2_1 + 4 * T2 - LAP
         at_res = at_v2s_listed + LAP
         at_wt = at_res + LAP
-        at_v0 = at_v2s_listed + S2
+        at_v0 = at_v2s_listed + LAP + S2
         at_wo0 = at_v0
         at_wi = at_v0 + 4 * T
         at_wi_s = at_wi + 2 * i_passes * N
-        at_z_late = at_wi + 4 * S
+        at_z_late = at_wi + 4 * S + LAP
         at_v1 = at_z_late + 10 * CHUNK * PACK - LAP
         at_wo1 = at_v1
         at_first_picks = at_v1 + 4 * T

@@ -23,6 +23,7 @@ PASS = P * PACK
 QUADS = 4
 CHUNK = 256
 RUN = 4
+WORD_RUN = 2
 LIST_ROWS = 16
 ROWS_AT = 96
 PLANE_AT = [12, 0]
@@ -153,10 +154,10 @@ def tile_list_two_sided_match_kernel(
                 )
             for b in range(i_passes):
                 nc.vector.tensor_copy(
-                    v_c[a][:, b].bitcast(I32).rearrange("p t (g r) -> p g t r", r=RUN),
+                    v_c[a][:, b].bitcast(I32).rearrange("p t (g r) -> p g t r", r=WORD_RUN),
                     v_listed[a][:, PASS * b : PASS * (b + 1)]
                     .bitcast(I32)
-                    .rearrange("p (g r t) -> p g t r", r=RUN, t=PACK),
+                    .rearrange("p (g r t) -> p g t r", r=WORD_RUN, t=PACK),
                 )
 
         gather_v(0)

@@ -23,7 +23,6 @@ PASS = P * PACK
 QUADS = 4
 CHUNK = 256
 RUN = 4
-WORD_RUN = 2
 LIST_ROWS = 16
 ROWS_AT = 96
 PLANE_AT = [12, 0]
@@ -68,15 +67,13 @@ def tile_list_two_sided_match_kernel(
         at_res = at_v2s_listed + LAP
         at_wt = at_res + LAP
         at_v0 = at_v2s_listed + LAP + S2
-        at_wo0 = at_v0
-        at_wi = at_v0 + 4 * T
+        at_wo0 = at_v0 - ROW_ALIGN
+        at_wi = at_wo0 + 4 * T
         at_wi_s = at_wi + 2 * i_passes * N
         at_z_late = at_wi + 4 * S + LAP
         at_v1 = at_z_late + 10 * CHUNK * PACK - LAP
         at_wo1 = at_v1
-        at_first_picks = at_v1 + 4 * T
-        at_late_picks = at_first_picks + 4 * CHUNK - LAP
-        at_wo_bf = at_late_picks + 4 * CHUNK
+        at_wo_bf = at_v1 + 4 * T
 
         v_tab_s = kept([P, T // 4], I32, "v_tab_s")
         v2_tab_s = kept([P, T2 // 4], I32, "v2_tab_s")
@@ -142,22 +139,14 @@ def tile_list_two_sided_match_kernel(
         nc.vector.scalar_tensor_tensor(neg_level[:], res_t[:, :, 0:PACK], -1.0, wt_size[:], MULT, MULT)
 
 
-        v_listed = [staged([P, S], U32, "v_listed0", at_wi), kept([P, S], U32, "v_listed1")]
         v_c = [kept([P, i_passes, PACK, P], U32, f"v_c{a}") for a in range(k_passes)]
         v2_c = {}
 
         def gather_v(a):
             for b in range(i_passes):
                 nc.vector.tensor_copy(
-                    v_listed[a][:, PASS * b : PASS * (b + 1)],
+                    v_c[a][:, b].rearrange("p t m -> p m t"),
                     v_tab[a][:].bitcast(U32).indirect(entries(idx, PASS * b, PASS)),
-                )
-            for b in range(i_passes):
-                nc.vector.tensor_copy(
-                    v_c[a][:, b].bitcast(I32).rearrange("p t (g r) -> p g t r", r=WORD_RUN),
-                    v_listed[a][:, PASS * b : PASS * (b + 1)]
-                    .bitcast(I32)
-                    .rearrange("p (g r t) -> p g t r", r=WORD_RUN, t=PACK),
                 )
 
         gather_v(0)
@@ -178,10 +167,9 @@ def tile_list_two_sided_match_kernel(
                 in_=wi_scales.bitcast(I32)[:, 4 * q : 4 * q + 4, :].rearrange("b r w -> r b w"),
             )
 
-        def gather_v2(a, g, offset=None):
+        def gather_v2(a, g):
             first, width = GROUPS[g]
-            shape, name = [P, width], f"v2_c{a}_{g}"
-            v2_c[a, g] = kept(shape, U32, name) if offset is None else staged(shape, U32, name, offset)
+            v2_c[a, g] = kept([P, width], U32, f"v2_c{a}_{g}")
             nc.vector.tensor_copy(v2_c[a, g][:], v2_tab[a][:].bitcast(U32).indirect(entries(idx2, first, width)))
 
         z_late, result = [], {}
@@ -349,6 +337,7 @@ def tile_list_two_sided_match_kernel(
                 store(c, 0, result[c][:])
 
         opened = [(0, 0), (0, 1), (1, 0)]
+        gather_v2(0, 2)
         gather_v2(0, 1)
         gather_v2(0, 0)
         gather_v(1)
@@ -356,13 +345,12 @@ def tile_list_two_sided_match_kernel(
         for g, b in opened:
             for s in banks_of(g):
                 fit_passes(g, b, s, 0)
-        gather_v2(1, 0, at_first_picks)
+        gather_v2(1, 0)
         gather_v2(1, 1)
         gather_v2(1, 2)
         for g, b in opened:
             for s in banks_of(g):
                 fit_passes(g, b, s, 1)
-        gather_v2(0, 2, at_late_picks)
         for g, b in opened:
             for s in banks_of(g):
                 surplus(g, b, s)

from contextlib import ExitStack

import concourse.mybir as mybir

K, T, S, T2, S2, N = 1024, 2048, 1024, 4096, 1024, 512
FLOPS = 2 * K * S * S2 + 2 * 2 * S * N * S2

F32 = mybir.dt.float32
BF16 = mybir.dt.bfloat16
I32 = mybir.dt.int32
U32 = mybir.dt.uint32
U16 = mybir.dt.uint16
U8 = mybir.dt.uint8
FP8X4 = mybir.dt.float8_e4m3fn_x4
FP4X4 = mybir.dt.float4_e2m1fn_x4
ACT = mybir.ActivationFunctionType
MULT = mybir.AluOpType.mult
ADD = mybir.AluOpType.add

P = 128
PACK = 4
PASS = P * PACK
QUADS = 4
CHUNK = 256
RUN = 4
LIST_ROWS = 16
ROWS_AT = 96
PLANE_AT = [12, 0]
BANK = 512
GROUPS = [(0, 256), (256, 512), (768, 256)]
GROUP_OF = [0, 1, 1, 2]
FIT_BANK = [[0, 2], [4, 0], [4, 0]]
PLAIN = [(0, 0), (1, 0)]
LAP = 64
ROW_ALIGN = 256


def tile_list_two_sided_match_kernel(
    tc, tab_words, tab_scales, offs, tab2_words, tab2_scales, offs2, res, wt, wi_words, wi_scales, wo, out
):
    nc = tc.nc
    k_passes = K // PASS
    i_passes = S // PASS

    with ExitStack() as ctx:
        keep = ctx.enter_context(tc.tile_pool(name="keep", bufs=1))
        stage = ctx.enter_context(tc.tile_pool(name="stage", bufs=1))
        psum = ctx.enter_context(tc.psum_pool(name="psum", bufs=1))

        def staged(shape, dtype, name, offset):
            return stage.tile(shape, dtype, name=name, align_bytes=64 if offset % ROW_ALIGN else ROW_ALIGN, offset=offset)

        def kept(shape, dtype, name):
            return keep.tile(shape, dtype, name=name, align_bytes=ROW_ALIGN)

        def words(table, a):
            return table[a].rearrange("p t i -> p (t i)").bitcast(I32)

        def entries(listed, first, count):
            return listed[:, first // LIST_ROWS : (first + count) // LIST_ROWS]

        idx = keep.tile([P, S // LIST_ROWS], U16, name="idx")
        idx2 = keep.tile([P, S2 // LIST_ROWS], U16, name="idx2")

        at_v2_1 = 0
        at_v2s_listed = at_v2_1 + 4 * T2 - LAP
        at_res = at_v2s_listed + LAP
        at_wt = at_res + LAP
        at_v0 = at_v2s_listed + LAP + S2
        at_wo0 = at_v0 - ROW_ALIGN
        at_wi = at_wo0 + 4 * T
        at_wi_s = at_wi + 2 * i_passes * N
        at_z_late = at_wi + 4 * S + LAP
        at_v1 = at_z_late + 10 * CHUNK * PACK - LAP
        at_wo1 = at_v1
        at_wo_bf = at_v1 + 4 * T

        v_tab_s = kept([P, T // 4], I32, "v_tab_s")
        v2_tab_s = kept([P, T2 // 4], I32, "v2_tab_s")
        for window in (v_tab_s, v2_tab_s):
            nc.vector.memset(window[0:ROWS_AT, :], 0)
        v_tab = [staged([P, T], I32, f"v_tab{a}", at) for a, at in enumerate([at_v0, at_v1])]
        v2_tab = [kept([P, T2], I32, "v2_tab0"), staged([P, T2], I32, "v2_tab1", at_v2_1)]

        nc.scalar.dma_start(out=v_tab_s[ROWS_AT:P, :], in_=tab_scales.bitcast(I32).rearrange("a q w -> (a q) w"))
        nc.sync.dma_start(out=idx[:], in_=offs)
        nc.sync.dma_start(out=v2_tab_s[ROWS_AT:P, :], in_=tab2_scales.bitcast(I32).rearrange("a q w -> (a q) w"))
        nc.sync.dma_start(out=idx2[:], in_=offs2)
        nc.sync.dma_start(out=v_tab[0][:], in_=words(tab_words, 0))
        nc.sync.dma_start(out=v2_tab[0][:], in_=words(tab2_words, 0))
        nc.sync.dma_start(out=v_tab[1][:], in_=words(tab_words, 1))
        vs_listed = kept([P, S], U8, "vs_listed")
        v2s_listed = staged([P, S2], U8, "v2s_listed", at_v2s_listed)
        planes = [kept([P, S + S2], U8, f"planes{a}") for a in range(k_passes)]
        for b in range(i_passes):
            nc.vector.tensor_copy(
                vs_listed[:, PASS * b : PASS * (b + 1)], v_tab_s[:].bitcast(U8).indirect(entries(idx, PASS * b, PASS))
            )
        for b in range(i_passes):
            nc.vector.tensor_copy(
                planes[0][:, PASS * b : PASS * (b + 1)].rearrange("p (t m) -> p t m", t=PACK),
                vs_listed[:, PASS * b : PASS * (b + 1)].rearrange("p (m t) -> p t m", t=PACK),
            )
        for h in range(2):
            nc.vector.tensor_copy(
                v2s_listed[:, PASS * h : PASS * (h + 1)],
                v2_tab_s[:].bitcast(U8).indirect(entries(idx2, PASS * h, PASS)),
            )
        for h in range(2):
            nc.vector.tensor_copy(
                planes[0][:, S + PASS * h : S + PASS * (h + 1)].bitcast(I32),
                v2s_listed[:, PASS * h : PASS * (h + 1)].bitcast(I32),
            )

        def place_planes(a):
            for q in range(QUADS):
                first = ROWS_AT + 16 * a + 4 * q
                row = 32 * q + PLANE_AT[a]
                if (a, row) != (0, first):
                    nc.sync.dma_start(
                        out=planes[a][:].bitcast(I32)[row : row + 4, :],
                        in_=planes[0][:].bitcast(I32)[first : first + 4, :],
                    )

        place_planes(0)
        nc.sync.dma_start(out=v2_tab[1][:], in_=words(tab2_words, 1))
        res_t = staged([P, i_passes, 2 * PACK], F32, "res_t", at_res)
        wt_t = staged([P, i_passes, 2 * PACK], F32, "wt_t", at_wt)
        nc.sync.dma_start(out=res_t[:, :, 0:PACK], in_=res.rearrange("(b p t) -> p b t", p=P, t=PACK))
        place_planes(1)
        nc.sync.dma_start(out=wt_t[:, :, 0:PACK], in_=wt.rearrange("(b p t) -> p b t", p=P, t=PACK))
        neg_res = kept([P, i_passes, PACK], F32, "neg_res")
        wt_size = kept([P, i_passes, PACK], F32, "wt_size")
        wt_sign = kept([P, i_passes, PACK], BF16, "wt_sign")
        neg_level = kept([P, i_passes, PACK], F32, "neg_level")
        nc.scalar.mul(neg_res[:], res_t[:, :, 0:PACK], -0.5)
        nc.scalar.activation(wt_size[:], wt_t[:, :, 0:PACK], ACT.Abs, scale=0.5)
        nc.scalar.activation(wt_sign[:], wt_t[:, :, 0:PACK], ACT.Sign)
        nc.vector.scalar_tensor_tensor(neg_level[:], res_t[:, :, 0:PACK], -1.0, wt_size[:], MULT, MULT)


        v_c = [kept([P, i_passes, PACK, P], U32, f"v_c{a}") for a in range(k_passes)]
        v2_c = {}

        def gather_v(a):
            for b in range(i_passes):
                nc.vector.tensor_copy(
                    v_c[a][:, b].rearrange("p t m -> p m t"),
                    v_tab[a][:].bitcast(U32).indirect(entries(idx, PASS * b, PASS)),
                )

        gather_v(0)
        wo_raw = [staged([P, PACK, N], F32, f"wo_raw{b}", at) for b, at in enumerate([at_wo0, at_wo1])]
        wi_c = staged([P, i_passes, N // 2], I32, "wi_c", at_wi)
        wi_s = staged([P, i_passes, N // 4], I32, "wi_s", at_wi_s)

        def load_wo(b):
            nc.sync.dma_start(
                out=wo_raw[b][:], in_=wo[b * PASS : (b + 1) * PASS, :].rearrange("(p t) n -> p t n", t=PACK)
            )

        load_wo(0)
        nc.sync.dma_start(out=wi_c[:], in_=wi_words.bitcast(I32).rearrange("b p w -> p b w"))
        for q in range(QUADS):
            nc.sync.dma_start(
                out=wi_s[32 * q : 32 * q + 4, :, :],
                in_=wi_scales.bitcast(I32)[:, 4 * q : 4 * q + 4, :].rearrange("b r w -> r b w"),
            )

        def gather_v2(a, g):
            first, width = GROUPS[g]
            v2_c[a, g] = kept([P, width], U32, f"v2_c{a}_{g}")
            nc.vector.tensor_copy(v2_c[a, g][:], v2_tab[a][:].bitcast(U32).indirect(entries(idx2, first, width)))

        z_late, result = [], {}
        fit, above, z_bf, z_c, z_s, score, chance = {}, {}, {}, {}, {}, {}, {}
        wo_bf = [staged([P, N * PACK], BF16, "wo_bf0", at_wo_bf), kept([P, N * PACK], BF16, "wo_bf1")]
        wo_c = [kept([P, N], U32, f"wo_c{b}") for b in range(i_passes)]
        wo_s = [kept([P, N], U8, f"wo_s{b}") for b in range(i_passes)]

        def bank(number, width=CHUNK):
            return psum.tile([P, BANK // width, width], F32, name=f"bank{number}")

        def fit_passes(g, b, s, a):
            width = GROUPS[g][1]
            share = BANK // width
            if a == 0:
                fit[g, b, s] = bank(FIT_BANK[g][b] + s, width)
            for e in range(share):
                t = share * s + e
                nc.tensor.matmul_mx(
                    out=fit[g, b, s][:, e, :],
                    lhsT=v_c[a][:, b, t, :].bitcast(FP8X4),
                    lhsT_scale=planes[a][PLANE_AT[a] :, PASS * b + P * t : PASS * b + P * (t + 1)],
                    rhs=v2_c[a, g][:].bitcast(FP8X4),
                    rhs_scale=planes[a][PLANE_AT[a] :, S + GROUPS[g][0] : S + GROUPS[g][0] + width],
                    start=(a, e) == (0, 0),
                    stop=(a, e) == (k_passes - 1, share - 1),
                )

        def banks_of(g):
            return range(PACK * GROUPS[g][1] // BANK)

        def fit_bank(g, b, s):
            for a in range(k_passes):
                fit_passes(g, b, s, a)

        def surplus(g, b, s):
            width = GROUPS[g][1]
            share = BANK // width
            plain = (g, b) in PLAIN
            if s == 0:
                shape, dtype = ([P, PACK, width], F32) if plain else ([P, 2, width, 2], BF16)
                if (g, b) == (1, 1):
                    above[g, b] = staged(shape, dtype, "above1_1", at_wo_bf)
                elif (g, b) == (2, 0):
                    above[g, b] = staged(shape, dtype, "above2_0", at_wo0 + 8 * CHUNK)
                else:
                    above[g, b] = kept(shape, dtype, f"above{g}_{b}")
            for e in range(share):
                t = share * s + e
                if plain:
                    nc.scalar.activation(
                        above[g, b][:, t, :], fit[g, b, s][:, e, :], ACT.Relu, bias=neg_res[:, b, t : t + 1], scale=0.5
                    )
                else:
                    nc.scalar.activation(
                        above[g, b][:, t // 2, :, t % 2],
                        fit[g, b, s][:, e, :],
                        ACT.Relu,
                        bias=neg_level[:, b, t : t + 1],
                        scale=wt_size[:, b, t : t + 1],
                    )

        def weigh(c, b):
            number = i_passes * c + b
            if number > 2:
                z_bf[c, b] = z_late[0][:, CHUNK * PACK * (number - 3) : CHUNK * PACK * (number - 2)]
            elif number:
                z_bf[c, b] = staged([P, CHUNK * PACK], BF16, f"z_bf{c}_{b}", at_wo0 + 8 * CHUNK * number)[:]
            else:
                z_bf[c, b] = kept([P, CHUNK * PACK], BF16, "z_bf0_0")[:]
            g = GROUP_OF[c]
            cols = slice(CHUNK * c - GROUPS[g][0], CHUNK * (c + 1) - GROUPS[g][0])
            if (g, b) in PLAIN:
                nc.vector.tensor_tensor(
                    z_bf[c, b].rearrange("p (j r t) -> p j t r", r=RUN, t=PACK),
                    above[g, b][:, :, cols].rearrange("p t (j r) -> p j t r", r=RUN),
                    wt_t[:, b, 0:PACK].unsqueeze(1).unsqueeze(3).to_broadcast([P, CHUNK // RUN, PACK, RUN]),
                    MULT,
                )
            else:
                nc.vector.tensor_tensor(
                    z_bf[c, b].rearrange("p (j u e) -> p j u e", u=2, e=2),
                    above[g, b][:, :, cols, :].rearrange("p u j e -> p j u e"),
                    wt_sign[:, b, :].rearrange("p (u e) -> p u e", e=2).unsqueeze(1).to_broadcast([P, CHUNK, 2, 2]),
                    MULT,
                )

        def quantise_z(c, b):
            if c == 0:
                z_c[c, b] = staged([P, CHUNK], U32, f"z_c{c}_{b}", at_wo0 + 4 * CHUNK * b)
            elif (c, b) == (1, 0):
                z_c[c, b] = staged([P, CHUNK], U32, "z_c1_0", at_wo1 + 4 * CHUNK)
            else:
                z_c[c, b] = kept([P, CHUNK], U32, f"z_c{c}_{b}")
            z_s[c, b] = kept([P, CHUNK], U8, f"z_s{c}_{b}")
            nc.vector.quantize_mx(out=z_c[c, b][:].bitcast(FP8X4), scales=z_s[c, b][:], in_=z_bf[c, b])

        def round_wo(b):
            for v in range(2):
                nc.vector.tensor_copy(
                    wo_bf[b][:, 2 * N * v : 2 * N * (v + 1)].rearrange("p (n r t) -> p n t r", r=RUN, t=PACK),
                    wo_raw[b][:, :, 2 * P * v : 2 * P * (v + 1)].rearrange("p t (n r) -> p n t r", r=RUN),
                )

        def quantise_wo(b, v):
            cols = slice(2 * P * v, 2 * P * (v + 1))
            nc.vector.quantize_mx(
                out=wo_c[b][:, cols].bitcast(FP8X4),
                scales=wo_s[b][:, cols],
                in_=wo_bf[b][:, 2 * N * v : 2 * N * (v + 1)],
            )

        def score_passes(kind, c, v, b, number=None):
            if number is not None:
                score[kind, c, v] = bank(number)
            for e in range(2):
                n = 2 * v + e
                if kind == "interest":
                    codes = wi_c[:, b, :].bitcast(U8)[:, 2 * P * n : 2 * P * (n + 1)].bitcast(FP4X4)
                    scales = wi_s[:, b, :].bitcast(U8)[:, P * n : P * (n + 1)]
                else:
                    codes = wo_c[b][:, P * n : P * (n + 1)].bitcast(FP8X4)
                    scales = wo_s[b][:, P * n : P * (n + 1)]
                nc.tensor.matmul_mx(
                    out=score[kind, c, v][:, e, :],
                    lhsT=codes,
                    lhsT_scale=scales,
                    rhs=z_c[c, b][:].bitcast(FP8X4),
                    rhs_scale=z_s[c, b][:],
                    start=number is not None and e == 0,
                    stop=number is None and e == 1,
                )

        def scores(kind, c, b, first_bank=None):
            for v in range(2):
                score_passes(kind, c, v, b, None if first_bank is None else first_bank + v)

        def score_bank(kind, c, v, number, first):
            score_passes(kind, c, v, first, number)
            score_passes(kind, c, v, 1 - first)

        def sigmoid(c, v):
            chance[c, v] = kept([P, 2, CHUNK], F32, f"chance{c}_{v}")
            nc.scalar.activation(chance[c, v][:], score["interest", c, v][:], ACT.Tanh)

        def store(c, first, tile):
            rows = out[P * first : P * (first + tile.shape[1]), CHUNK * c : CHUNK * (c + 1)]
            nc.sync.dma_start(out=rows.rearrange("(e p) j -> p e j", p=P), in_=tile)

        def finish(c, v):
            if c == 0:
                if v == 0:
                    result[c] = kept([P, 4, CHUNK], F32, "result0")
                part = result[c][:, 2 * v : 2 * (v + 1), :]
            else:
                part = kept([P, 2, CHUNK], F32, f"result{c}_{v}")[:]
            pieces = [slice(0, 1), slice(1, 2)] if (c, v) == (3, 1) else [slice(0, 2)]
            for e in pieces:
                nc.vector.scalar_tensor_tensor(
                    part[:, e, :], chance[c, v][:, e, :], 1.0, score["offer", c, v][:, e, :], ADD, MULT
                )
                if c:
                    store(c, 2 * v + e.start, part[:, e, :])
            if (c, v) == (0, 1):
                store(c, 0, result[c][:])

        opened = [(0, 0), (0, 1), (1, 0)]
        gather_v2(0, 2)
        gather_v2(0, 1)
        gather_v2(0, 0)
        gather_v(1)
        load_wo(1)
        for g, b in opened:
            for s in banks_of(g):
                fit_passes(g, b, s, 0)
        gather_v2(1, 0)
        gather_v2(1, 1)
        gather_v2(1, 2)
        for g, b in opened:
            for s in banks_of(g):
                fit_passes(g, b, s, 1)
        for g, b in opened:
            for s in banks_of(g):
                surplus(g, b, s)
        for s in banks_of(1):
            fit_bank(1, 1, s)
        for s in banks_of(2):
            fit_bank(2, 0, s)
        weigh(0, 0)
        round_wo(0)
        quantise_wo(0, 0)
        weigh(0, 1)
        quantise_wo(0, 1)
        quantise_z(0, 0)
        quantise_z(0, 1)
        weigh(1, 0)
        scores("interest", 0, 0, 6)
        scores("interest", 0, 1)
        for s in banks_of(1):
            surplus(1, 1, s)
        for s in banks_of(2):
            fit_bank(2, 1, s)
        round_wo(1)
        z_late.append(staged([P, 5 * CHUNK * PACK], BF16, "z_late", at_z_late))
        quantise_wo(1, 0)
        quantise_wo(1, 1)
        for v in range(2):
            score_bank("offer", 0, v, 2 + v, 1)
        sigmoid(0, 0)
        sigmoid(0, 1)
        for b in range(i_passes):
            for s in banks_of(2):
                surplus(2, b, s)
        quantise_z(1, 0)
        scores("interest", 1, 0, 6)
        weigh(2, 0)
        weigh(1, 1)
        quantise_z(2, 0)
        quantise_z(1, 1)
        scores("interest", 1, 1)
        for v in range(2):
            score_bank("offer", 1, v, 4 + v, 1)
        weigh(2, 1)
        finish(0, 0)
        quantise_z(2, 1)
        weigh(3, 0)
        finish(0, 1)
        for v in range(2):
            score_bank("interest", 2, v, 2 + v, 0)
            score_bank("offer", 2, v, v, 1)
        quantise_z(3, 0)
        weigh(3, 1)
        sigmoid(1, 0)
        sigmoid(1, 1)
        finish(1, 0)
        quantise_z(3, 1)
        finish(1, 1)
        scores("interest", 3, 0, 6)
        sigmoid(2, 0)
        sigmoid(2, 1)
        finish(2, 0)
        finish(2, 1)
        for v in range(2):
            score_passes("interest", 3, v, 1)
            score_bank("offer", 3, v, 4 + v, 1)
        for v in range(2):
            sigmoid(3, v)
            finish(3, v)
